import numpy as np, ml_dtypes
CORES = [48,51,52,55]
N = 4
BF = ml_dtypes.bfloat16
def gentries(a):
    return np.ascontiguousarray(a.reshape(8, 16, -1).transpose(0, 2, 1)).reshape(8, -1)
def gtable(e):
    e = np.asarray(e); return np.ascontiguousarray(e.reshape(8, -1, 16).transpose(0, 2, 1)).reshape(128, -1).astype(np.int32)
V, G, BL, K, CAP, HO, RO = 1920, 1024, 480, 2048, 512, 2, 2
W = V + G; CL = RO + 1; OWN = np.arange(V); LO = BL * (OWN // BL + 1)
def glists(a):
    return np.stack([gentries(x) for x in a]).astype(np.int64)
def pick(x, i):
    return np.take_along_axis(x, i[:, :, None, :], 3)
def reals(rng, top):
    return (0.5 + (top - 0.5) * rng.random((N, 8, 16, V))) * np.exp2(rng.integers(-1, 2, (N, 8, 1, V)))
def later(rng):
    r = rng.random((N, 8, V)); r = np.where(rng.random((N, 8, V)) < 0.5, r, r * r * r)
    return np.minimum(LO + ((W - LO) * r).astype(np.int64), W - 1)
def parts(rng):
    d = dict(a=rng.integers(-127, 128, (N, 8, 16, V)), b=rng.integers(-127, 128, (N, 8, 16, V)), h=reals(rng, 1.0), u=rng.integers(0, 256, (N, 8, 16, K)), v=rng.integers(0, 256, (N, 8, 16, K)))
    d["n0"] = later(rng); d["n1"] = later(rng); d["s"] = rng.integers(0, K, (N, 8, V))
    share = rng.permutation(np.array([0.1, 0.1, 0.2, 0.2, 0.35, 0.35, 0.5, 0.5])).reshape(1, 8, 1)
    d["f"] = np.where(rng.random((N, 8, K)) < share, rng.integers(V, W, (N, 8, K)), rng.integers(0, V, (N, 8, K)))
    d["th"] = rng.integers(60, 111, (N, 8, 1, RO)) + rng.integers(-15, 16, (N, 8, 16, RO))
    return d
def pack(d):
    o = {}
    for k, x, n in (("ta", "a", V), ("tb", "b", V), ("h0", "h", V), ("u0", "u", K), ("v0", "v", K)):
        o[k] = np.ascontiguousarray(d[x].reshape(N, 128, n)).astype(np.float32).astype(BF)
    for k, x in (("na", "n0"), ("nb", "n1"), ("sd", "s"), ("pf", "f")): o[k] = np.stack([gtable(e) for e in d[x]])
    o["th"] = np.ascontiguousarray(d["th"].reshape(N, 128, RO)).astype(np.int32)
    return o
def setup_inputs(rng):
    return pack(parts(rng))
def setup_inputs_spread(rng):
    d = parts(rng); d["h"] = reals(rng, 2.0)
    d["u"] = (256 * rng.random((N, 8, 16, K)) ** rng.integers(1, 5, (N, 8, 1, K))).astype(np.int64)
    d["u"] = np.minimum(d["u"], 255)
    d["th"] = np.clip(rng.choice(np.array([5, 40, 80, 120, 250]), (N, 8, 1, RO)) + rng.integers(-40, 41, (N, 8, 16, RO)), 0, 255)
    return pack(d)
def setup_inputs_ends(rng):
    d = parts(rng)
    def two(lo, hi, n):
        e = rng.integers(0, 2, (N, 8, 16, n)); r = rng.integers(0, 2, (N, 8, 1, n))
        return np.where(np.where(rng.random((N, 8, 1, n)) < 0.5, r, e) == 1, hi, lo)
    d["a"] = two(-127, 127, V); d["b"] = two(-127, 127, V); d["h"] = two(0.25, 4.0, V); d["u"] = two(0, 255, K); d["v"] = two(0, 255, K); d["th"] = two(0, 255, RO)
    for k in ("n0", "n1"): d[k] = np.where(rng.random((N, 8, V)) < 0.75, W - 1, LO)
    d["s"] = np.where(rng.random((N, 8, V)) < 0.5, 0, K - 1)
    d["f"] = np.where(rng.random((N, 8, K)) < 0.7, np.where(rng.random((N, 8, K)) < 0.5, 0, W - 1), rng.integers(0, W, (N, 8, K)))
    d["th"][:, 0] = 255; d["th"][:, 6:, :, 0] = 255
    for g, s, w in ((7, 127, 255), (6, -127, 0)):
        d["a"][:, g, :, 0] = s; d["a"][:, g, :, V - 1] = s; d["b"][:, g, :, 0] = s
        for p in (1, K - 1): d["u"][:, g, :, p] = w; d["v"][:, g, :, p] = 255; d["f"][:, g, p] = 0
    d["n1"][:, 6:, 0] = BL
    L = V - 1 - (V - RO) % CL; d["th"][:, 6:, :, RO - 1] = 255
    for g, s, w in ((7, 127, 255), (6, -127, 0)):
        d["a"][:, g, :, L] = 0; d["b"][:, g, :, L] = s
        d["u"][:, g, :, K - 2] = 255; d["v"][:, g, :, K - 2] = w; d["f"][:, g, K - 2] = L
    return pack(d)
def setup_inputs_corners(rng):
    d = parts(rng); rest = OWN[OWN % CL == RO]; far = V + np.arange(RO, G, CL)
    n = np.array([0, 1, CAP - 1, CAP, CAP + 1, K, RO * CAP - 1, CAP])
    for g in range(8):
        q = int(rng.integers(N))
        for r in range(N):
            k = int(n[g])
            if r != q: k = K if g == 6 else int(rng.choice(np.array([k, min(k + 1, K), K])))
            if g == 6: gh = rng.choice(far, k)
            else: gh = np.where(rng.random(k) < 0.5, rng.integers(V, W, k), rng.choice(np.array([V, W - 1]), k))
            d["f"][r, g] = rng.permutation(np.concatenate([gh, rng.choice(rest, K - k)]))
    d["s"][:, 2] = K - 1; d["s"][:, 4] = K - 1; d["s"][:, 4, 0] = 0; d["s"][:, 3] = rng.choice(np.array([0, 1, K - 2, K - 1]), (N, V))
    t = rng.integers(20, 101, (N, 8, 16, 1)); d["th"] = np.repeat(t, RO, axis=3)
    c = rng.choice(np.array([0, 1, 8, 9, 15, 16]), (N, 8, 1, V)); at = (np.argsort(rng.random((N, 8, 16, V)), axis=2) < c).astype(np.int64)
    e = t + 1 - at; x = pick(d["u"], d["s"]) - 128
    d["a"] = np.where(x - e >= -127, x - e, x + e)
    return pack(d)
def setup_inputs_calm(rng):
    d = parts(rng); rest = OWN[OWN % CL == RO]; far = V + np.arange(RO, G, CL)
    c = ((0, 1, 2, 3, 0, 0, 1, 2), (0, 0, 0, 0, 1, 2, 1, 1), (0, 1, 0, 0, 0, 1, 1, 0))
    d["f"][..., :16] = rng.choice(far, (N, 8, 16))
    for g in range(8):
        q = int(rng.integers(N)); w = rng.choice(rest, K); at = rng.permutation(K); j = c[0][g]
        w[at[:j]] = rng.choice(far, j)
        for t in range(1, RO):
            k = c[t][g]; e = rng.choice(OWN[OWN % CL == t], k); w[at[j:j + k]] = e; j += k
            d["n0"][q, g, e] = rng.choice(far, k); d["n1"][q, g, e] = rng.choice(far, k); d["th"][q, g, :, t] = 255
        d["f"][q, g] = w
    return pack(d)
def setup_inputs_chains(rng):
    d = parts(rng); nxt = LO + (OWN - LO) % CL
    d["n0"][:, :4] = nxt; d["n1"][:, 2:6] = nxt; d["th"][:, ::2] = 255; d["th"][:, 5] = 0
    d["f"] = np.where(rng.random((N, 8, K)) < 0.6, rng.integers(0, BL, (N, 8, K)), d["f"])
    z = rng.random((N, 8, 1, V)) < 0.33; d["a"] = np.where(z, 0, d["a"]); d["b"] = np.where(z, 0, d["b"])
    c = rng.choice(np.array([0, 8, 9, 16]), (N, 8, 1, K)); tie = (np.argsort(rng.random((N, 8, 16, K)), axis=2) < c).astype(np.int64)
    d["u"] = np.minimum(d["u"], 254); d["v"] = np.where(rng.random((N, 8, 1, K)) < 0.5, d["u"] + 1 - tie, d["v"])
    d["f"][:, 4] = 0; d["f"][:, 4, K - 1] = V - 1
    d["s"][:, 1] = 0; d["s"][:, 3] = K - 1; d["s"][:, 3, V - 1] = 0
    return pack(d)
def check_ranges(d):
    bad = []
    for k, lo, hi in (("ta", -127, 127), ("tb", -127, 127), ("u0", 0, 255), ("v0", 0, 255), ("na", BL, W - 1), ("nb", BL, W - 1), ("sd", 0, K - 1), ("pf", 0, W - 1), ("th", 0, 255)):
        x = np.asarray(d[k]).astype(np.float64)
        if not np.all((x >= lo) & (x <= hi) & (x == np.floor(x))): bad.append("range of " + k)
    y = np.asarray(d["h0"]).astype(np.float64)
    if not np.all((y >= 0.25) & (y <= 4)): bad.append("range of h0")
    for k in ("na", "nb"):
        if not np.all(glists(d[k]) >= LO): bad.append("blocks of " + k)
    return bad
def reference(ta, tb, h0, u0, v0, na, nb, sd, pf, th):
    a = ta.astype(np.float32).astype(np.int64).reshape(N, 8, 16, V); b = tb.astype(np.float32).astype(np.int64).reshape(N, 8, 16, V)
    u = u0.astype(np.float32).astype(np.int64).reshape(N, 8, 16, K); v = v0.astype(np.float32).astype(np.int64).reshape(N, 8, 16, K)
    h = h0.astype(np.float64).reshape(N, 8, 16, V); limit = th.astype(np.int64).reshape(N, 8, 16, RO)
    n0, n1, s, face = glists(na), glists(nb), glists(sd), glists(pf)
    dead = np.zeros((N, 8, W), bool); shift = np.zeros(8, np.int64)
    for t in range(RO):
        w = np.concatenate([h, np.roll(h, -1, axis=0)[..., :G]], axis=3)
        x = pick(u, (s + shift[None, :, None]) & (K - 1))
        count = np.add.reduce((np.abs(x - 128 - a) <= limit[..., t:t + 1]).astype(np.int64), axis=2)
        dead[..., :V] |= (OWN % CL == t) & (count >= 9)
        for hop in range(HO):
            go = np.take_along_axis(dead, face, 2); fi = np.minimum(face, V - 1)
            un = (u + pick(a, fi) * v) & 255; vn = (v + pick(b, fi) * un) & 255
            u = np.where(go[:, :, None, :], un, u); v = np.where(go[:, :, None, :], vn, v)
            count = np.add.reduce((u >= v).astype(np.int64), axis=2)
            to = np.where(count >= 9, np.take_along_axis(n0, fi, 2), np.take_along_axis(n1, fi, 2))
            face = np.where(go, to, face)
        on = face >= V
        m = np.minimum(np.min(np.add.reduce(on.astype(np.int64), axis=2), axis=0), CAP)
        nu, nv, nf = u.copy(), v.copy(), face.copy()
        for g in range(8):
            at = [np.flatnonzero(on[r, g])[:int(m[g])] for r in range(N)]
            for r in range(N):
                e = (r + 1) % N
                nu[e, g][:, at[e]] = u[r, g][:, at[r]]; nv[e, g][:, at[e]] = v[r, g][:, at[r]]; nf[e, g, at[e]] = face[r, g, at[r]] - V
        u, v, face = nu, nv, nf; shift = shift + m
        x = pick(u, (s + shift[None, :, None]) & (K - 1))
        w[..., :V] = 0.5 * (h + x * 0.015625 - 2.0)
        for k in range(V // BL - 1, -1, -1):
            c = slice(k * BL, (k + 1) * BL)
            y = (a[..., c] * pick(w, n0[..., c]) + b[..., c] * pick(w, n1[..., c])) * 0.00390625
            w[..., c] = np.where(dead[:, :, None, c], y, w[..., c])
        h = w[..., :V]
    z = ((u - 128) * (v - 128)) * 2.0 ** -13
    p = pick(w, face) * (0.5 * (1.0 + np.tanh(0.5 * z)))
    yh = np.add.reduce(h.reshape(N, 8, 16, V // BL, BL), axis=3)
    return {"yh": yh.reshape(N, 128, BL).astype(np.float32), "yw": (p[..., :K // 2] + p[..., K // 2:]).reshape(N, 128, K // 2).astype(np.float32)}

def check_inputs(d):
    bad = list(check_ranges(d))
    if not bad:
        for name, y in reference(**d).items():
            for q in range(N):
                v = np.abs(np.asarray(y[q], np.float64)); s = np.sqrt(np.mean(v * v))
                if v.max() > 8 * s or s < 2.0 ** -3: bad.append('%s of rank %d is uneven or too small' % (name, q))
    return bad

@@ -1,0 +1,556 @@
+from concourse.bass import DstId, RemoteDMATransfer
+from concourse.mybir import AluOpType as OP, AxisListType as AX, ActivationFunctionType as AF
+
+V, GH, BL, NP, CAP, W = 1920, 1024, 480, 2048, 512, 2944
+KK = float(2 ** 19)
+RND = 1.5 * 2.0 ** 31
+RND64 = 1.5 * 2.0 ** 29
+CMP_ON = "aaaa"
+
+F, B, I, U = "float32", "bfloat16", "int32", "uint16"
+COLS = {
+    "ta": 0, "a": (V, B), "b": (V, B), "h": (V, B), "ui": (NP, B), "vi": (NP, B), "lst": (360, I), "pfi": (128, I), "thi": (2, I),
+    "lstf": (360, F), "thf": (2, F), "pi": (1, I), "pj": (2, I), "pc": (8, F), "c128": (128, F), "i16": (128, F), "a16": (128, F), "v64": (128, F),
+    "blkf": (128, F), "blk": (128, B), "blkn": (128, B), "idn": (128, B), "idm": (128, B), "id256": (128, B), "idf": (128, F), "idmf": (128, F),
+    "trik": (128, B), "tri": (128, B), "id4k": (128, B), "z1": (144, B), "z2": (144, B), "zall": (2304, B), "half": (144, B), "id64": (128, B),
+    "pm": (768, F), "diag": (128, F), "reset": (128, F), "pidx": (128, F), "pid2": (128, F), "rampv": (128, B), "rampb": (128, B), "one": (128, F),
+    "negk": (CAP, F), "dd": (240, F), "dhi": (240, B), "dlo": (240, B), "tst": (V, B), "xa": (1936, B), "xb": (1936, B), "xn": (1936, B),
+    "cl": (240, F), "fk": (80, F), "b480": (40, F), "cli": (40, I), "clj": (40, I), "clu": (40, U), "cx": (640, F), "cy": (640, B), "ok": (640, B), "dead": (640, B),
+    "dl": (40, F), "de": (40, F), "n0u": (80, U), "n1u": (80, U), "c0": (1280, B), "c1": (1280, B),
+    "face": (128, F), "off": (128, U), "ga": (NP, B), "gb": (NP, B), "q": (NP, I), "gn": (2 * NP, B), "um": (NP, B), "vm": (NP, B),
+    "ua": (2 * NP, B), "va": (2 * NP, B), "ub": (2 * NP, B), "zz": (2 * NP, F), "u1": (NP, B), "v1": (NP, B),
+    "sg": (128, F), "on": (128, B), "s": (2 * 132, F), "land": (32, F), "o1": (128, F), "o2": (128, F), "o3": (128, F), "o4": (128, F),
+    "offc": (8, U), "endc": (8, U), "val": (128, F), "v2": (128, B), "gj": (128, F), "sc": (4096, F), "dk": (CAP, F), "rs": (2 * CAP, F), "rl": (2 * CAP, F),
+    "ab": (CAP, F), "e": (CAP, B), "ne": (CAP, B), "es": (CAP, B), "y": (128, I), "y1": (128, I), "y2": (128, I), "y3": (128, I),
+    "posx": (128, F), "hb": (128, F), "nlv": (128, F), "m": (8, F), "idx": (128, U), "xi": (120, I), "xj": (120, I), "xu": (120, U),
+    "hl": (GH, B), "k0": (V, F), "w0": (W, F), "w1": (W, F), "hsend": (GH, F), "p0": (320, F), "p1": (320, F),
+    "oh": (BL, F), "fu": (128, U),
+}
+SAME = {"pw": "w0", "sig": "sc", "u2": "um", "vc": "v1", "ow": "k0", "vv": "ab", "hs": "dk", "xg": "tst", "uc": "ga"}
+del COLS["ta"]
+SCRATCH = {k: ("sbuf", [128, n], d) for k, (n, d) in COLS.items()}
+SCRATCH["ps"] = ("psum", [128, 4096], F)
+LOADS = ["sd", "na", "nb", "pf", "th", "u0", "ta", "v0", "tb", "h0"]
+REMOTE = ["h", "c0", "uv0", "r0", "g1", "c1", "u1", "r1", "z1"]
+SEMAPHORES = ["ev", "ea", "ep", "eg", "sent"] + ["l" + k for k in LOADS] + ["r" + k for k in REMOTE] + ["o0", "o1", "o2"]
+PAR = {"span": 1500.0, "wide": 512, "lead": 7000.0, "lat": 120.0, "seed": 1, "turns": 12000, "shake": 800.0}
+KEPT = {}
+CY, PE, GA, SC = 1.0, 0.5, 1.56, 3.8
+
+
+def build(g, T, topo, core):
+    rank = T.rank_of(core)
+    n = len(T.cores)
+    nxt, prv = T.cores[(rank + 1) % n], T.cores[(rank - 1) % n]
+    ops, lead = [], [0.0]
+
+    def A(name, lo=0, hi=None, st=1):
+        name = SAME.get(name, name)
+        if hi is None:
+            hi = SCRATCH[name][1][1]
+        ap = T[name][:, lo:hi] if st == 1 else T[name][:, lo:hi:st]
+        return (ap, [(name, lo, hi)], len(range(lo, hi, st)), name)
+
+    def P(lo, k, st=1):
+        return A("ps", lo, lo + k, st)
+
+    def IX(win, offs):
+        return (win[0].indirect(offs[0]), win[1] + offs[1], 16 * offs[2], "*")
+
+    def wide(*xs):
+        return 0.5 if all(x[3] != "*" and SCRATCH[x[3]][2] in (B, U) for x in xs) else 1.0
+
+    def add(q, fn, rd, wr, ns, kind=None):
+        ops.append(dict(q=q, fn=fn, rd=[r for x in rd for r in x[1]], wr=[r for x in wr for r in x[1]], ns=ns, kind=kind, lead=lead[0]))
+
+    def cost(o, i, f=1.0):
+        if i[3] == "*":
+            return 50 + GA * CY * i[2]
+        return 50 + CY * max(64, f * o[2])
+
+    def ts(o, i, s1, o1, s2=None, o2=None):
+        cols = [s for s in (s1, s2) if isinstance(s, tuple)]
+        a1 = s1[0] if isinstance(s1, tuple) else s1
+        a2 = s2[0] if isinstance(s2, tuple) else s2
+        if o2 is None:
+            fn = lambda: g.vector.tensor_scalar(o[0], i[0], a1, None, o1)
+        else:
+            fn = lambda: g.vector.tensor_scalar(o[0], i[0], a1, a2, o1, o2)
+        add("v", fn, [i] + cols, [o], cost(o, i, wide(o, i)))
+
+    def tt(o, x, y, op):
+        f = 1.0 if "ps" in (x[3], y[3]) else 2.0 * wide(o, x, y)
+        add("v", lambda: g.vector.tensor_tensor(o[0], x[0], y[0], op), [x, y], [o], cost(o, x, f))
+
+    def cp(o, i):
+        add("v", lambda: g.vector.tensor_copy(o[0], i[0]), [i], [o], cost(o, i, wide(o, i)))
+
+    def scan(o, d0, d1, o0, o1):
+        add("v", lambda: g.vector.tensor_tensor_scan(o[0], d0[0], d1[0], 0.0, o0, o1), [d0, d1], [o], cost(o, d0))
+
+    def fill(o, c):
+        add("v", lambda: g.vector.memset(o[0], c), [], [o], 50 + CY * max(64, o[2] * wide(o)))
+
+    def act(o, i, f=AF.Identity, bias=0.0, scale=1.0):
+        cols = [s for s in (bias, scale) if isinstance(s, tuple)]
+        bb = bias[0] if isinstance(bias, tuple) else bias
+        ss = scale[0] if isinstance(scale, tuple) else scale
+        add("a", lambda: g.scalar.activation(o[0], i[0], f, bias=bb, scale=ss), [i] + cols, [o], 15 + cost(o, i))
+
+    def mm(o, pairs, start=True, stop=True):
+        def fn():
+            last = None
+            for k, (l, r) in enumerate(pairs):
+                last = g.tensor.matmul(o[0], l[0], r[0], start and k == 0, stop and k == len(pairs) - 1)
+            return last
+        ns = 60 + sum(PE * max(64, r[2]) * (4 if SCRATCH[r[3]][2] == F else 1) for l, r in pairs)
+        add("p", fn, [x for pr in pairs for x in pr], [o], ns)
+
+    def iota(o, pat, base=0, cm=0):
+        if SCRATCH[o[3]][2] == I:
+            fn = lambda: g.iota(o[0], pat, base, cm)
+        else:
+            fn = lambda: g.iota(o[0], pat, base, cm, allow_small_or_imprecise_dtypes=True)
+        add("g", fn, [], [o], 130 + 2 * CY * o[2])
+
+    def load(q, name, o):
+        e = g.sync if q == "s" else g.scalar
+        bts = o[2] * (2 if SCRATCH[o[3]][2] == B else 4)
+        add(q, lambda: e.dma_start(o[0], T[name][:]), [], [o], 60, ("dma", "l" + name, 2000 + 0.25 * bts))
+
+    def store(sem, dst, i):
+        add("s", lambda: g.sync.dma_start(dst, i[0]), [i], [], 60, ("dma", sem, 2000 + i[2]))
+
+    def send(sem, items):
+        engs = [e for e in topo.engines(core, items[0][1][0][0]) if all(e in topo.engines(core, c) for s, ds in items for c, d in ds)]
+        per = len(engs) // len(items)
+        def fn():
+            trs = []
+            for k, (s, ds) in enumerate(items):
+                mask = sum(1 << e for e in engs[k * per:(k + 1) * per])
+                ids = [DstId(rid=topo.addr(c)[0], pnc=topo.addr(c)[1]) for c, d in ds]
+                trs.append(RemoteDMATransfer(dst_ids=ids, dma_engine_mask=mask, remote_sem=T.sem["r" + sem], srcs=[s[0]], dsts=[d[0] for c, d in ds]))
+            return g.remote_dma_fused(trs, local_sem=T.sem.sent)
+        bts = sum(s[2] * (2 if SCRATCH[s[3]][2] == B else 4) for s, ds in items)
+        add("g", fn, [s for s, ds in items], [d for s, ds in items for c, d in ds], 500,
+            ("rem", "r" + sem, 2000 + 0.4 * bts, per * sum(len(ds) for s, ds in items), per * len(items)))
+
+    def tolist(o, z, src, lo, hi, more=()):
+        mm(o, [(A(z, 15 - i, 143 - i), A(src, lo + i, hi, 16)) for i in range(16)] + list(more))
+
+    load("s", "sd", A("lst", 0, 120)); load("a", "na", A("lst", 120, 240)); load("s", "nb", A("lst", 240, 360))
+    load("a", "u0", A("ui")); load("s", "ta", A("a")); load("a", "th", A("thi")); load("s", "pf", A("pfi"))
+    load("a", "v0", A("vi")); load("s", "tb", A("b")); load("s", "h0", A("h"))
+    for k in range(10):
+        ops[k]["lead"] = 1e6 - 1e4 * k
+    iota(A("pi"), [[0, 1]], 0, 1); iota(A("v64"), [[64, 8], [3, 16]]); iota(A("a16"), [[1, 8], [0, 16]])
+    iota(A("c128"), [[1, 128]]); iota(A("i16"), [[0, 8], [1, 16]])
+    pp, pmod, pgr, p64, pwt, ptm = (A("pc", k, k + 1) for k in range(6))
+    cp(pp, A("pi")); ts(A("pj", 0, 1), A("pi"), 15, OP.bitwise_and); ts(A("pj", 1, 2), A("pi"), 4, OP.arith_shift_right)
+    cp(A("pc", 1, 3), A("pj")); ts(p64, pgr, 64.0, OP.mult, pmod, OP.add)
+    for t in range(2):
+        for r in range(3):
+            ts(A("pm", 128 * (3 * t + r), 128 * (3 * t + r + 1)), A("v64"), float(t - 16 * r), OP.add, p64, OP.is_equal)
+    ts(A("blk"), A("a16"), pgr, OP.is_equal); ts(A("idn"), A("c128"), pp, OP.is_equal)
+    for name, src, f in (("blkf", "blk", 1.0), ("blkn", "blk", -4096.0), ("idm", "idn", -1.0), ("id256", "idn", 1.0 / 256), ("idf", "idn", 1.0),
+                         ("idmf", "idn", -1.0), ("id4k", "idn", -4096.0), ("id64", "idn", 64.0)):
+        act(A(name), A(src), scale=f)
+    add("g", lambda: g.affine_select(T.tri[:], T.blk[:], [[1, 128]], OP.is_gt, 0.0, 0, -1), [A("blk")], [A("tri")], 170 + 256)
+    act(A("trik"), A("tri"), scale=KK)
+    fill(A("z1"), 0.0); act(A("z1", 15, 128, 16), A("blk", 0, 128, 16))
+    ts(pwt, pmod, 2.0, OP.is_lt, 2.0, OP.mult); ts(ptm, pmod, 4.0, OP.is_lt, -1.0, OP.mult); ts(pwt, pwt, ptm, OP.add)
+    act(A("z2"), A("z1"), scale=pwt)
+    fill(A("zall"), 0.0); fill(A("half"), 0.5)
+    add("g", lambda: g.affine_select(T.zall[:, 15:2304:16], T.half[:, 0:144], [[-1, 16], [-16, 9]], OP.is_equal, 0.0, 0, 1),
+        [A("half")], [A("zall")], 170 + 288)
+    act(A("pidx"), A("c128"), bias=pmod, scale=16.0); act(A("pid2"), A("pidx"), bias=float(NP))
+    ts(A("diag"), A("i16"), pmod, OP.is_equal); act(A("reset"), A("i16"), AF.Sign)
+    act(A("rampv"), A("c128"), bias=1024.0 * 256, scale=-1024.0); act(A("rampb"), A("c128"), bias=128.0)
+    iota(A("one"), [[0, 128]], 1); iota(A("b480"), [[BL, 4], [0, 10]])
+    act(A("xa"), A("ui", 0, 1936), scale=0.0)
+    for x in ("xb", "xn"):
+        iota(A(x, 1, 1936, 3), [[0, 645]]); iota(A(x, 2, 1936, 3), [[0, 645]]); iota(A(x, V, V + 1), [[0, 1]])
+    iota(A("negk"), [[0, CAP]], -int(KK)); iota(A("sc", 0, CAP), [[0, CAP]])
+    iota(A("s", 0, 133, 132), [[0, 2]])
+    for t in range(2):
+        act(A("fk", 40 * t, 40 * t + 40), A("pidx", 0, 40), bias=float(t), scale=3.0)
+    cp(A("lstf", 0, 120), A("lst", 0, 120)); cp(A("lstf", 120, 360), A("lst", 120, 360)); ts(A("thf"), A("thi"), 0.5, OP.add)
+    cp(A("face"), A("pfi")); ts(A("off"), A("face"), float(V), OP.min)
+    pmx = lambda t, r: A("pm", 128 * (3 * t + r), 128 * (3 * t + r + 1))
+    mm(P(2048, 40), [(pmx(0, r), A("lstf", r, 120, 3)) for r in range(3)])
+    cp(A("clu"), P(2048, 40))
+    for k in range(2):
+        tt(A("dd", 120 * k, 120 * k + 120), A("lstf", 120 + 120 * k, 240 + 120 * k), A("pidx", 0, 120), OP.subtract)
+    ts(A("dhi"), A("dd"), RND64, OP.add, RND64, OP.subtract); tt(A("dlo"), A("dd"), A("dhi"), OP.subtract)
+    parts = [A("dhi", 0, 120), A("dlo", 0, 120), A("dhi", 120, 240), A("dlo", 120, 240)]
+    for i in range(16):
+        o = P((3072, 3584, 1024, 1536)[i % 4], 120)
+        mm(o, [(A("zall", 144 * i + 15 - k, 144 * i + 143 - k), parts[k]) for k in range(4)])
+        act(A("tst", i, V, 16), o)
+    send("h", [(A("h", 0, GH), [(prv, A("hl"))])])
+    act(A("w0", V, W), A("hl"), scale=128.0)
+
+    def collapse(t, usrc):
+        for k in range(2):
+            lo, hi, f0, f1 = 320 * k, 320 * k + 320, 960 * k + t, 960 * k + 960
+            tt(A("cx", lo, hi), IX(A(usrc, 0, NP), A("clu", 20 * k, 20 * k + 20)), A("a", f0, f1, 3), OP.subtract)
+            act(A("cy", lo, hi), A("cx", lo, hi), AF.Abs, bias=-128.0)
+            act(A("ok", lo, hi), A("cy", lo, hi), AF.Sign, bias=A("thf", t, t + 1), scale=-1.0)
+            mm(P(2048 + 512 * k, 320), [(A("blk"), A("ok", lo, hi))])
+            ts(A("dead", lo, hi), P(2048 + 512 * k, 320), 1.0, OP.is_ge)
+            tt(A("xa", f0, f1, 3), A("dead", lo, hi), A("a", f0, f1, 3), OP.mult)
+        for x, y in (("xb", "b"), ("xn", "tst")):
+            tt(A(x, t, V, 3), A("dead"), A(y, t, V, 3), OP.mult)
+
+    def factors(t):
+        if t == 0:
+            mm(P(0, 80), [(pmx(0, r), A("lstf", 120 + r, 360, 3)) for r in range(3)])
+            mm(P(512, 120), [(pmx(1, r), A("lstf", r, 360, 3)) for r in range(3)])
+            act(A("cl", 40, 120), P(0, 80)); act(A("cl", 120, 240), P(512, 120))
+        tt(A("de"), A("cl", 120 * t + 80, 120 * t + 120), A("b480"), OP.subtract)
+        k = 40 * t
+        cp(A("n1u", k, k + 40), A("de"))
+        tolist(P(0, 40), "z1", "ok", 0, 640)
+        ts(A("dl"), P(0, 40), 1.0, OP.is_ge)
+        tt(A("de"), A("cl", 120 * t + 40, 120 * t + 80), A("dl"), OP.mult)
+        tt(A("de"), A("de"), A("fk", k, k + 40), OP.max); tt(A("de"), A("de"), A("b480"), OP.subtract)
+        cp(A("n0u", k, k + 40), A("de"))
+        for lo, hi in ((0, 512), (512, 640)):
+            mm(P(1024 + lo, hi - lo), [(A("id256"), A("xa", t + 3 * lo, 3 * hi, 3)), (A("idm"), A("dead", lo, hi))])
+        for b in range(4):
+            c = 320 * b + 160 * t
+            act(A("c0", c, c + 160), P(1024 + 160 * b, 160), bias=1.0)
+            act(A("c1", c, c + 160), A("xb", BL * b + t, BL * b + BL, 3), scale=1.0 / 256)
+
+    def pair(name, pr, base=0):
+        return A(name, base + 1024 * pr, base + 1024 * pr + 1024)
+
+    def hop(ui, vi, uo, vo, unit, after):
+        seen = []
+        for pr in range(2):
+            g0 = NP * pr
+            lead[0] = PAR["lead"] if pr == 0 else 0.0
+            mul_bank = P(2048 + 512 * pr, 512)
+            for tab, got, mul, mu, own, out in (("xa", "ga", vi, unit, ui, uo), ("xb", "gb", uo, "idn", vi, vo)):
+                for c in (2 * pr, 2 * pr + 1):
+                    lo, hi = 512 * c, 512 * c + 512
+                    x = P(lo, 512)
+                    if tab == "xa":
+                        act(A(got, lo, hi), IX(A(tab), A("off", 32 * c, 32 * c + 32)))
+                    elif c % 2 == 0:
+                        act(pair(got, pr), IX(A(tab), A("off", 64 * pr, 64 * pr + 64)))
+                    mm(mul_bank, [(A(mu), A(mul, lo, hi))])
+                    mm(x, [(A("idn"), A("zall", 0, 512))], stop=False)
+                    tt(x, mul_bank, A(got, lo, hi), OP.mult)
+                    mm(x, [(A(unit), A(own, lo, hi))], start=False)
+                wd = PAR["wide"]
+                for lo in range(1024 * pr, 1024 * pr + 1024, wd):
+                    ts(A("q", lo, lo + wd), P(lo, wd), -127.5 / 256, OP.add)
+                    tt(A(out, lo, lo + wd), P(lo, wd), A("q", lo, lo + wd), OP.subtract)
+            act(A("gn", g0 + 1024, g0 + NP), IX(A("xn"), A("off", 64 * pr, 64 * pr + 64)))
+            for c in (2 * pr, 2 * pr + 1):
+                lo, hi = 512 * c, 512 * c + 512
+                x, ge = P(lo, 512), A("gn", g0 + 512 * (c % 2), g0 + 512 * (c % 2) + 512)
+                mm(x, [(A("idn"), A(uo, lo, hi)), (A("idm"), A(vo, lo, hi))])
+                if CMP_ON[c] == "v":
+                    ts(ge, x, 0.0, OP.is_ge, 2.0, OP.mult)
+                else:
+                    act(ge, x, AF.Sign, bias=1.0 / 512)
+            bank = 3072 + 512 * pr
+            f, s = A("face", 64 * pr, 64 * pr + 64), A("sg", 64 * pr, 64 * pr + 64)
+            tolist(P(bank + 128, 64), "z2", "gn", g0 + 1024, g0 + NP)
+            tolist(P(bank + 64, 64), "z1", "gn", g0 + 1024, g0 + NP, [(A("idf"), f)])
+            tolist(P(bank + 192, 64), "z1", "gn", g0, g0 + 1024)
+            kinds = CMP_ON[2 * pr:2 * pr + 2]
+            if kinds[0] == kinds[1]:
+                act(s, P(bank + 192, 64), AF.Sign, bias=-17.0 if kinds[0] == "v" else -1.0)
+            else:
+                for j in range(2):
+                    act(A("sg", 64 * pr + 32 * j, 64 * pr + 32 * j + 32), P(bank + 192 + 32 * j, 32), AF.Sign, bias=-17.0 if kinds[j] == "v" else -1.0)
+            tt(s, P(bank + 128, 64), s, OP.mult)
+            tt(f, P(bank + 64, 64), s, OP.add)
+            if after is None:
+                ts(A("off", 64 * pr, 64 * pr + 64), f, float(V), OP.min)
+            else:
+                after(pr)
+
+    def move(t):
+        s0 = 132 * t
+        sc, rs, rl = "sc", A("rs", CAP * t, CAP * t + CAP), A("rl", CAP * t, CAP * t + CAP)
+        ts(A("on"), A("face"), float(V), OP.is_ge)
+        mm(P(2048, 128), [(A("blk"), A("on"))])
+        mm(P(2176, 128), [(A("blkn"), A("on")), (A("blk"), A("rampb"))])
+        act(A("gj"), A("face"), AF.Relu, bias=1.0 - V)
+        tt(A("v2"), A("on"), A("rampv"), OP.mult)
+        mm(P(2560, 128), [(A("trik"), A("on")), (A("idn"), A("v2")), (A("idmf"), A("gj"))])
+        act(A("val"), P(2560, 128))
+        mm(P(3072, 128), [(A("tri"), A("on")), (A("id4k"), A("on"))])
+        scan(A("s", s0 + 1, s0 + 129), A("one"), P(2048, 128), OP.mult, OP.add)
+        tot = A("s", s0 + 128, s0 + 129)
+        send("c%d" % t, [(tot, [(T.cores[(rank + d) % n], A("land", 16 * t + 4 * d, 16 * t + 4 * d + 1)) for d in range(1, n)])])
+        tt(A("o1"), P(2176, 128), A("s", s0, s0 + 128), OP.max)
+        tt(A("o1"), A("o1"), A("diag"), OP.mult)
+        scan(A("o2"), A("reset"), A("o1"), OP.mult, OP.add)
+        cp(A("offc"), A("o2", 15, 128, 16))
+        win, oc, vl = A(sc), A("offc"), A("val")
+        add("v", lambda: g.vector.tensor_copy(win[0].indirect(oc[0]), vl[0]), [oc, vl], [win], 50 + SC * 128)
+        scan(A("dk"), A("negk"), A(sc, 0, CAP), OP.add, OP.max)
+        act(rs, A("dk"), AF.Relu, bias=KK, scale=-1.0)
+        send("r%d" % t, [(rs, [(nxt, rl)])])
+        if t == 0:
+            iota(A(sc, 0, CAP), [[0, CAP]])
+        act(A("ab"), A("dk"), AF.Abs, bias=-KK / 2)
+        act(A("es"), A("ab"), AF.Sign, bias=KK / 2 - 0.5, scale=-1.0)
+        act(A("e"), A("es"), AF.Relu); act(A("ne"), A("es"), AF.Relu, scale=-1.0)
+        tt(A("o3"), A("s", s0 + 1, s0 + 129), A("diag"), OP.mult)
+        scan(A("o4"), A("reset"), A("o3"), OP.mult, OP.add)
+        ts(A("endc"), A("o4", 15, 128, 16), -1.0, OP.add, CAP - 1.0, OP.min)
+        tt(A("posx"), P(3072, 128), A("s", s0, s0 + 128), OP.add)
+        m, m4, lr = A("m", t, t + 1), A("m", 4, 5), A("land", 16 * t + 4, 16 * t + 16, 4)
+        add("v", lambda: g.vector.tensor_reduce(m[0], lr[0], AX.X, OP.min), [lr], [m], 114)
+        ts(m, m, tot, OP.min, float(CAP), OP.min); ts(m4, m, -4096.0, OP.add)
+        ts(A("hb"), A("posx"), m4, OP.is_lt, 8192.0, OP.mult); tt(A("hb"), A("hb"), A("pid2"), OP.add)
+        ts(A("nlv"), A("posx"), m4, OP.is_ge, 4096.0, OP.mult)
+        sh = m
+        if t == 1:
+            sh = A("m", 2, 3)
+            ts(sh, m, A("m", 0, 1), OP.add)
+        else:
+            ts(A("cli"), A("cl", 120, 160), sh, OP.add); ts(A("clj"), A("cli"), NP - 1, OP.bitwise_and); cp(A("clu"), A("clj"))
+        mm(P(2560, CAP), [(A("blkf"), rl)])
+        tt(A("vv"), P(2560, CAP), A("e"), OP.mult)
+        scan(A("hs"), A("ne"), A("vv"), OP.mult, OP.add)
+        ts(A("y"), IX(A("hs"), A("endc")), -1.0, OP.add)
+        ts(A("y1"), A("y"), 6, OP.logical_shift_right, 0x1FF0, OP.bitwise_and); ts(A("y2"), A("y"), 19, OP.logical_shift_right)
+        tt(A("o1"), A("y1"), A("y2"), OP.add); tt(A("o1"), A("o1"), A("hb"), OP.min); ts(A("idx"), A("o1"), -float(NP), OP.add)
+        ts(A("y3"), A("y"), GH - 1, OP.bitwise_and); tt(A("o3"), A("y3"), A("nlv"), OP.max); tt(A("face"), A("face"), A("o3"), OP.min)
+        return sh
+
+    def xlist(sh):
+        ts(A("xi"), A("lstf", 0, 120), sh, OP.add); ts(A("xj"), A("xi"), NP - 1, OP.bitwise_and); cp(A("xu"), A("xj"))
+
+    def correct(w, usrc, nc, done):
+        for b in range(3, -1, -1):
+            lo, hi = BL * b, BL * b + BL
+            ix = IX(A(usrc), A("xu", 30 * b, 30 * b + 30))
+            if nc == 2 and b == 3:
+                tt(A(w, lo, hi), ix, A("k0", lo, hi), OP.add)
+            else:
+                o = P(512 * b, BL) if nc == 1 else P(1024 + 512 * b, BL)
+                act(A("xg", lo, hi), ix, bias=-128.0 if nc == 1 else 0.0)
+                if nc == 1:
+                    mm(o, [(A("id64"), A("h", lo, hi)), (A("idn"), A("xg", lo, hi))])
+                else:
+                    mm(o, [(A("idf"), A("k0", lo, hi))], stop=False)
+                    mm(o, [(A("idn"), A("xg", lo, hi))], start=False)
+                act(A(w, lo, hi), o)
+        for b in range(3, -1, -1):
+            win, k, c, o = A(w, BL * b, W), 160 * nc, 320 * b, P(3584, 160 * nc)
+            for p, lst, fac in (("p1", "n1u", "c1"), ("p0", "n0u", "c0")):
+                for t in range(nc):
+                    j = 40 * t + 10 * b
+                    tt(A(p, 160 * t, 160 * t + 160), IX(win, A(lst, j, j + 10)), A(fac, c + 160 * t, c + 160 * t + 160), OP.mult)
+            if nc == 2:
+                act(o, A("p1", 0, k))
+            for t in range(nc):
+                tt(A(w, BL * b + t, BL * b + BL, 3), P(3584 + 160 * t, 160) if nc == 2 else A("p1", 0, 160), A("p0", 160 * t, 160 * t + 160), OP.add)
+            done(b)
+
+    collapse(0, "ui")
+    hop("ui", "vi", "um", "vm", "id256", None)
+    hop("um", "vm", "ua", "va", "idn",
+        lambda pr: send("uv0", [(pair(x, pr), [(nxt, pair(x, pr, NP))]) for x in ("ua", "va")]))
+    factors(0)
+    sh = move(0)
+    half = lambda k: A("idx", 64 * k, 64 * k + 64)
+    act(pair("u1", 0), IX(A("ua"), half(0)), scale=256.0); ts(pair("u1", 1), IX(A("ua"), half(1)), 256.0, OP.mult)
+    for c in range(4):
+        o, ix = A("v1", 512 * c, 512 * c + 512), IX(A("va"), A("idx", 32 * c, 32 * c + 32))
+        act(o, ix, scale=256.0)
+    ts(A("off"), A("face"), float(V), OP.min)
+    xlist(sh)
+    collapse(1, "u1")
+    hop("u1", "v1", "um", "vm", "id256", None)
+    hop("um", "vm", "ub", "vc", "idn", lambda pr: send("u1", [(pair("ub", pr), [(nxt, pair("ub", pr, NP))])]))
+    correct("w0", "u1", 1, lambda b: None)
+    factors(1)
+    act(A("hsend"), A("w0", 0, GH), scale=1.0 / 128)
+    send("g1", [(A("hsend"), [(prv, A("w1", V, W))])])
+    act(A("k0"), A("w0", 0, V), scale=1.0 / 256)
+    for c in range(4):
+        lo, hi = 512 * c, 512 * c + 512
+        act(A("uc", lo, hi), A("vc", lo, hi), bias=-0.5)
+        act(P(lo, 512), A("ub", lo, hi), bias=-0.5); tt(A("zz", lo, hi), P(lo, 512), A("uc", lo, hi), OP.mult)
+    send("z1", [(A("zz", 0, NP), [(nxt, A("zz", NP, 2 * NP))])])
+    sh = move(1)
+    xlist(sh)
+    act(pair("u2", 0), IX(A("ub"), half(0)), bias=-1.0, scale=2.0)
+    ts(pair("u2", 1), IX(A("ub"), half(1)), 2.0, OP.mult, -1.0, OP.add)
+    cp(A("fu"), A("face"))
+    act(pair("sig", 1), IX(A("zz"), half(1)), AF.Sigmoid, scale=8.0)
+    act(P(0, 1024), pair("sig", 1))
+    act(pair("sig", 0), IX(A("zz"), half(0)), AF.Sigmoid, scale=8.0)
+    correct("w1", "u2", 2, lambda b: mm(P(3072, BL), [(A("idf"), A("w1", BL * b, BL * b + BL))], start=(b == 3), stop=(b == 0)))
+    for k in range(2):
+        lo, hi = 512 * k, 512 * k + 512
+        act(A("pw", GH + lo, GH + hi), IX(A("w1"), A("fu", 64 + 32 * k, 96 + 32 * k)))
+        tt(A("pw", lo, hi), IX(A("w1"), A("fu", 32 * k, 32 * k + 32)), A("sig", lo, hi), OP.mult)
+    for k in range(2):
+        lo, hi = 512 * k, 512 * k + 512
+        tt(P(lo, 512), P(lo, 512), A("pw", GH + lo, GH + hi), OP.mult)
+        tt(A("ow", lo, hi), P(lo, 512), A("pw", lo, hi), OP.add)
+        store("o%d" % k, T.yw[:, lo:hi], A("ow", lo, hi))
+    act(A("oh"), P(3072, BL))
+    store("o2", T.yh[:], A("oh"))
+    return ops
+
+
+def depend(ops):
+    seen = {}
+    for i, o in enumerate(ops):
+        acc = [(r, False) for r in o["rd"]] + [(r, True) for r in o["wr"]]
+        dep = set()
+        for (nm, lo, hi), w in acc:
+            if nm == "ps":
+                lo, hi = lo // 512 * 512, (hi + 511) // 512 * 512
+            for j, l2, h2, w2 in seen.get(nm, []):
+                if l2 < hi and lo < h2 and (w or w2 or (nm == "ps" and ops[j]["q"] != o["q"])):
+                    dep.add(j)
+        for (nm, lo, hi), w in acc:
+            if nm == "ps":
+                lo, hi = lo // 512 * 512, (hi + 511) // 512 * 512
+            seen.setdefault(nm, []).append((i, lo, hi, w))
+        dep.discard(i)
+        o["dep"] = dep
+    last = {}
+    for i, o in enumerate(ops):
+        if o["kind"] and o["kind"][0] == "rem":
+            last.setdefault(o["kind"][1], []).append(i)
+    for o in ops:
+        for j in list(o["dep"]):
+            if ops[j]["kind"] and ops[j]["kind"][0] == "rem":
+                o["dep"].update(last[ops[j]["kind"][1]])
+
+
+def order(ops):
+    n, lat = len(ops), PAR["lat"]
+    ns = [o["ns"] for o in ops]
+    lag = [lat + (o["kind"][2] if o["kind"] else 0) for o in ops]
+    before = [sorted(o["dep"]) for o in ops]
+    for i in range(n):
+        far = set()
+        for j in before[i]:
+            far.update(ops[j]["dep"])
+        before[i] = [j for j in before[i] if j not in far or ops[j]["kind"]]
+    users = [[] for o in ops]
+    for i in range(n):
+        for j in before[i]:
+            users[j].append(i)
+
+    def place(key, back):
+        pre, post = (users, before) if back else (before, users)
+        left = [len(p) for p in pre]
+        ready = sorted((key[i], i) for i in range(n) if left[i] == 0)
+        busy = {q: [] for q in "vapgs"}
+        at = [0.0] * n
+        while ready:
+            i = ready.pop(0)[1]
+            if back:
+                t = max([lag[i] - lat] + [at[j] + ns[j] + lag[i] for j in pre[i]])
+            else:
+                t = max([0.0] + [at[j] + ns[j] + lag[j] for j in pre[i]])
+            b = busy[ops[i]["q"]]
+            lo, hi = 0, len(b)
+            while lo < hi:
+                mid = (lo + hi) // 2
+                if b[mid][1] <= t:
+                    lo = mid + 1
+                else:
+                    hi = mid
+            while lo < len(b) and b[lo][0] < t + ns[i]:
+                t = max(t, b[lo][1])
+                lo += 1
+            b.insert(lo, (t, t + ns[i]))
+            at[i] = t
+            grew = False
+            for u in post[i]:
+                left[u] -= 1
+                if left[u] == 0:
+                    ready.append((key[u], u))
+                    grew = True
+            if grew:
+                ready.sort()
+        return at, max(at[i] + ns[i] + (0 if back else lag[i] - lat) for i in range(n))
+
+    way = [0.0] * n
+    for i in range(n - 1, -1, -1):
+        way[i] = ns[i] + max([lag[i] + way[u] for u in users[i]] + [lag[i]])
+    first = [-1e9 + i if ops[i]["lead"] > 1e5 else 0.0 for i in range(n)]
+    best, base, r = None, [-w - o["lead"] for w, o in zip(way, ops)], PAR["seed"]
+    for turn in range(PAR["turns"]):
+        key = list(base)
+        if turn:
+            r = (r * 1103515245 + 12345) % 2147483648
+            mid, amp = best[0] * (r >> 8) / 8388608, PAR["shake"] * (1 + r % 4)
+            for i in range(n):
+                if abs(base[i] - mid) < PAR["span"]:
+                    r = (r * 1103515245 + 12345) % 2147483648
+                    key[i] += amp * ((r >> 8) / 8388608 - 0.5)
+        for rep in range(0 if turn % 8 else 1):
+            at, end = place([k + f for k, f in zip(key, first)], False)
+            if best is None or end < best[0]:
+                best = (end, at)
+            bt, _ = place([-(at[i] + ns[i]) for i in range(n)], True)
+            key = [-(bt[i] + ns[i]) for i in range(n)]
+        at, end = place([k + f for k, f in zip(key, first)], False)
+        if end <= best[0]:
+            best = (end, at)
+        base = best[1]
+    for i in range(n):
+        ops[i]["at"] = best[1][i]
+    return sorted(range(n), key=lambda i: (best[1][i], i))
+
+
+def rank_program(g, core, T, topo):
+    if T.rank_of(core) is None:
+        return
+    ops = build(g, T, topo, core)
+    depend(ops)
+    if "seq" not in KEPT:
+        KEPT["seq"] = order(ops)
+    seq = KEPT["seq"]
+    queue = {"v": g.vector, "a": g.scalar, "p": g.tensor, "g": g, "s": g.sync}
+    total, count, mark = {"sent": 0}, {q: 0 for q in "vapg"}, {}
+    for o in ops:
+        k = o["kind"]
+        if k and k[0] == "rem":
+            total[k[1]] = total.get(k[1], 0) + k[3]
+            total["sent"] += k[4]
+        elif k:
+            total[k[1]] = 16
+    waited = {q: {} for q in queue}
+    for i in seq:
+        o = ops[i]
+        need = {}
+        for j in o["dep"]:
+            s, v = mark[j]
+            if not (s == "ep" and o["q"] == "p"):
+                need[s] = max(need.get(s, 0), v)
+        for s, v in sorted(need.items()):
+            if waited[o["q"]].get(s, 0) < v:
+                queue[o["q"]].wait_ge(T.sem[s], v)
+                waited[o["q"]][s] = v
+        ins = o["fn"]()
+        k = o["kind"]
+        if k is None:
+            count[o["q"]] += 1
+            ins.then_inc(T.sem["e" + o["q"]], 1)
+            mark[i] = ("e" + o["q"], count[o["q"]])
+        else:
+            if k[0] == "dma":
+                ins.then_inc(T.sem[k[1]], 16)
+            mark[i] = (k[1], total[k[1]])
+    for q in count:
+        total["e" + q] = count[q]
+    for s, v in sorted(total.items()):
+        g.wait_ge(T.sem[s], v)

@@ -12,28 +12,29 @@ COLS = {
     "ta": 0, "a": (V, B), "b": (V, B), "h": (V, B), "ui": (NP, B), "vi": (NP, B), "lst": (360, I), "pfi": (128, I), "thi": (2, I),
     "lstf": (360, F), "thf": (2, F), "pi": (1, I), "pj": (2, I), "pc": (8, F), "c128": (128, F), "i16": (128, F), "a16": (128, F), "v64": (128, F),
     "blkf": (128, F), "blk": (128, B), "blkn": (128, B), "idn": (128, B), "idm": (128, B), "id256": (128, B), "idf": (128, F), "idmf": (128, F),
-    "trik": (128, B), "tri": (128, B), "id4k": (128, B), "z1": (144, B), "z2": (144, B), "zall": (2304, B), "half": (144, B), "id64": (128, B),
-    "pm": (768, F), "diag": (128, F), "reset": (128, F), "pidx": (128, F), "pid2": (128, F), "rampv": (128, B), "rampb": (128, B), "one": (128, F),
+    "trik": (128, B), "tri": (128, B), "id4k": (128, B), "z1": (144, B), "z2": (144, B), "zall": (2304, B), "half": (144, B), "idh": (128, B),
+    "pm": (768, F), "diag": (128, B), "reset": (128, F), "pidx": (128, F), "pid2": (128, F), "rampv": (128, B), "rampb": (128, B), "one": (128, F),
     "negk": (CAP, F), "dd": (240, F), "dhi": (240, B), "dlo": (240, B), "tst": (V, B), "xa": (1936, B), "xb": (1936, B), "xn": (1936, B),
     "cl": (240, F), "fk": (80, F), "b480": (40, F), "cli": (40, I), "clj": (40, I), "clu": (40, U), "cx": (640, F), "cy": (640, B), "ok": (640, B), "dead": (640, B),
-    "dl": (40, F), "de": (40, F), "n0u": (80, U), "n1u": (80, U), "c0": (1280, B), "c1": (1280, B),
+    "dl": (40, F), "de": (40, F), "n0u": (80, U), "n1u": (80, U), "c0": (1280, B),
     "face": (128, F), "off": (128, U), "ga": (NP, B), "gb": (NP, B), "q": (NP, I), "gn": (2 * NP, B), "um": (NP, B), "vm": (NP, B),
     "ua": (2 * NP, B), "va": (2 * NP, B), "ub": (2 * NP, B), "zz": (2 * NP, F), "u1": (NP, B), "v1": (NP, B),
     "sg": (128, F), "on": (128, B), "s": (2 * 132, F), "land": (32, F), "o1": (128, F), "o2": (128, F), "o3": (128, F), "o4": (128, F),
     "offc": (8, U), "endc": (8, U), "val": (128, F), "v2": (128, B), "gj": (128, F), "sc": (4096, F), "dk": (CAP, F), "rs": (2 * CAP, F), "rl": (2 * CAP, F),
-    "ab": (CAP, F), "e": (CAP, B), "ne": (CAP, B), "es": (CAP, B), "y": (128, I), "y1": (128, I), "y2": (128, I), "y3": (128, I),
+    "ab": (CAP, F), "ne": (CAP, B), "mone": (512, B), "y": (128, I), "y1": (128, I), "y2": (128, I), "y3": (128, I),
     "posx": (128, F), "hb": (128, F), "nlv": (128, F), "m": (8, F), "idx": (128, U), "xi": (120, I), "xj": (120, I), "xu": (120, U),
-    "hl": (GH, B), "k0": (V, F), "w0": (W, F), "w1": (W, F), "hsend": (GH, F), "p0": (320, F), "p1": (320, F),
+    "hl": (GH, B), "pw": (NP, F), "w0": (W, F), "w1": (W, F), "ow": (GH, F), "idhf": (128, F), "p0": (320, F), "p1": (320, F),
     "oh": (BL, F), "fu": (128, U),
 }
-SAME = {"pw": "w0", "sig": "sc", "u2": "um", "vc": "v1", "ow": "k0", "vv": "ab", "hs": "dk", "xg": "tst", "uc": "ga"}
+SAME = {"q2": "q", "sig": "sc", "u2": "um", "vc": "v1", "vv": "ab", "hs": "dk", "xg": "tst", "uc": "ga"}
 del COLS["ta"]
 SCRATCH = {k: ("sbuf", [128, n], d) for k, (n, d) in COLS.items()}
 SCRATCH["ps"] = ("psum", [128, 4096], F)
 LOADS = ["sd", "na", "nb", "pf", "th", "u0", "ta", "v0", "tb", "h0"]
-REMOTE = ["h", "c0", "uv0", "r0", "g1", "c1", "u1", "r1", "z1"]
+REMOTE = ["h", "c0", "uv0", "r0", "g1", "c1", "u1", "r1", "z1", "s0", "s1"]
 SEMAPHORES = ["ev", "ea", "ep", "eg", "sent"] + ["l" + k for k in LOADS] + ["r" + k for k in REMOTE] + ["o0", "o1", "o2"]
-PAR = {"span": 1500.0, "wide": 512, "lead": 7000.0, "lat": 120.0, "seed": 1, "turns": 12000, "shake": 800.0}
+PAR = {"raw": True, "two": True, "swaps": 100000, "heat": 250.0, "reach": 12, "zact": False, "give": 100.0, "vdve": (2,), "span": 1500.0,
+       "lead": 7000.0, "lat": 120.0, "seed": 1, "turns": 500, "shake": 800.0}
 KEPT = {}
 CY, PE, GA, SC = 1.0, 0.5, 1.56, 3.8
 
@@ -85,8 +86,9 @@ def build(g, T, topo, core):
     def cp(o, i):
         add("v", lambda: g.vector.tensor_copy(o[0], i[0]), [i], [o], cost(o, i, wide(o, i)))
 
-    def scan(o, d0, d1, o0, o1):
-        add("v", lambda: g.vector.tensor_tensor_scan(o[0], d0[0], d1[0], 0.0, o0, o1), [d0, d1], [o], cost(o, d0))
+    def scan(o, d0, d1, o0, o1, init=None):
+        add("v", lambda: g.vector.tensor_tensor_scan(o[0], d0[0], d1[0], init[0] if init else 0.0, o0, o1),
+            [d0, d1] + ([init] if init else []), [o], cost(o, d0))
 
     def fill(o, c):
         add("v", lambda: g.vector.memset(o[0], c), [], [o], 50 + CY * max(64, o[2] * wide(o)))
@@ -150,27 +152,36 @@ def build(g, T, topo, core):
     cp(A("pc", 1, 3), A("pj")); ts(p64, pgr, 64.0, OP.mult, pmod, OP.add)
     for t in range(2):
         for r in range(3):
-            ts(A("pm", 128 * (3 * t + r), 128 * (3 * t + r + 1)), A("v64"), float(t - 16 * r), OP.add, p64, OP.is_equal)
+            o = A("pm", 128 * (3 * t + r), 128 * (3 * t + r + 1))
+            if t == 0:
+                ts(o, A("v64"), float(t - 16 * r), OP.add, p64, OP.is_equal)
+            else:
+                act(A("pc", 6, 7), p64, bias=float(t - 16 * r), scale=-1.0)
+                act(o, A("v64"), AF.Abs, bias=A("pc", 6, 7)); act(o, o, AF.Relu, bias=1.0, scale=-1.0)
     ts(A("blk"), A("a16"), pgr, OP.is_equal); ts(A("idn"), A("c128"), pp, OP.is_equal)
-    for name, src, f in (("blkf", "blk", 1.0), ("blkn", "blk", -4096.0), ("idm", "idn", -1.0), ("id256", "idn", 1.0 / 256), ("idf", "idn", 1.0),
-                         ("idmf", "idn", -1.0), ("id4k", "idn", -4096.0), ("id64", "idn", 64.0)):
+    for name, src, f in (("blkf", "blk", -2.0 ** -24), ("blkn", "blk", -4096.0), ("idm", "idn", -1.0), ("id256", "idn", 1.0 / 256), ("idf", "idn", 1.0),
+                         ("idmf", "idn", -1.0), ("id4k", "idn", -4096.0), ("idh", "idn", 0.5), ("idhf", "idn", 0.5)):
         act(A(name), A(src), scale=f)
     add("g", lambda: g.affine_select(T.tri[:], T.blk[:], [[1, 128]], OP.is_gt, 0.0, 0, -1), [A("blk")], [A("tri")], 170 + 256)
     act(A("trik"), A("tri"), scale=KK)
     fill(A("z1"), 0.0); act(A("z1", 15, 128, 16), A("blk", 0, 128, 16))
     ts(pwt, pmod, 2.0, OP.is_lt, 2.0, OP.mult); ts(ptm, pmod, 4.0, OP.is_lt, -1.0, OP.mult); ts(pwt, pwt, ptm, OP.add)
     act(A("z2"), A("z1"), scale=pwt)
-    fill(A("zall"), 0.0); fill(A("half"), 0.5)
+    if PAR["zact"]:
+        for k in range(0, 2304, 128):
+            act(A("zall", k, k + 128), A("c128"), scale=0.0)
+    else:
+        fill(A("zall"), 0.0)
+    fill(A("half"), 0.5)
     add("g", lambda: g.affine_select(T.zall[:, 15:2304:16], T.half[:, 0:144], [[-1, 16], [-16, 9]], OP.is_equal, 0.0, 0, 1),
         [A("half")], [A("zall")], 170 + 288)
     act(A("pidx"), A("c128"), bias=pmod, scale=16.0); act(A("pid2"), A("pidx"), bias=float(NP))
     ts(A("diag"), A("i16"), pmod, OP.is_equal); act(A("reset"), A("i16"), AF.Sign)
     act(A("rampv"), A("c128"), bias=1024.0 * 256, scale=-1024.0); act(A("rampb"), A("c128"), bias=128.0)
     iota(A("one"), [[0, 128]], 1); iota(A("b480"), [[BL, 4], [0, 10]])
-    act(A("xa"), A("ui", 0, 1936), scale=0.0)
-    for x in ("xb", "xn"):
+    for x in ("xa", "xb", "xn"):
         iota(A(x, 1, 1936, 3), [[0, 645]]); iota(A(x, 2, 1936, 3), [[0, 645]]); iota(A(x, V, V + 1), [[0, 1]])
-    iota(A("negk"), [[0, CAP]], -int(KK)); iota(A("sc", 0, CAP), [[0, CAP]])
+    iota(A("negk"), [[0, CAP]], -int(KK)); iota(A("mone"), [[0, 512]], -1); iota(A("sc", 0, CAP), [[0, CAP]])
     iota(A("s", 0, 133, 132), [[0, 2]])
     for t in range(2):
         act(A("fk", 40 * t, 40 * t + 40), A("pidx", 0, 40), bias=float(t), scale=3.0)
@@ -182,13 +193,17 @@ def build(g, T, topo, core):
     for k in range(2):
         tt(A("dd", 120 * k, 120 * k + 120), A("lstf", 120 + 120 * k, 240 + 120 * k), A("pidx", 0, 120), OP.subtract)
     ts(A("dhi"), A("dd"), RND64, OP.add, RND64, OP.subtract); tt(A("dlo"), A("dd"), A("dhi"), OP.subtract)
-    parts = [A("dhi", 0, 120), A("dlo", 0, 120), A("dhi", 120, 240), A("dlo", 120, 240)]
-    for i in range(16):
-        o = P((3072, 3584, 1024, 1536)[i % 4], 120)
-        mm(o, [(A("zall", 144 * i + 15 - k, 144 * i + 143 - k), parts[k]) for k in range(4)])
-        act(A("tst", i, V, 16), o)
+    parts = [("dhi", 0), ("dlo", 0), ("dhi", 120), ("dlo", 120)]
+    def steps(t, banks):
+        for hf in range(2):
+            for i in range(16):
+                r = (t - i) % 3
+                o = P(banks[hf] + (16 * r + i - t) // 3, 305, 16)
+                mm(o, [(A("zall", 144 * i + 15 - k, 144 * i + 143 - k), A(x, lo + 60 * hf + r, lo + 60 * hf + 60, 3)) for k, (x, lo) in enumerate(parts)])
+    tbank = ((3072, 3584), (1024, 1536))
+    steps(0, tbank[0])
     send("h", [(A("h", 0, GH), [(prv, A("hl"))])])
-    act(A("w0", V, W), A("hl"), scale=128.0)
+    act(A("w0", V, W), A("hl"))
 
     def collapse(t, usrc):
         for k in range(2):
@@ -199,8 +214,8 @@ def build(g, T, topo, core):
             mm(P(2048 + 512 * k, 320), [(A("blk"), A("ok", lo, hi))])
             ts(A("dead", lo, hi), P(2048 + 512 * k, 320), 1.0, OP.is_ge)
             tt(A("xa", f0, f1, 3), A("dead", lo, hi), A("a", f0, f1, 3), OP.mult)
-        for x, y in (("xb", "b"), ("xn", "tst")):
-            tt(A(x, t, V, 3), A("dead"), A(y, t, V, 3), OP.mult)
+            tt(A("xn", f0, f1, 3), P(tbank[t][k], 320), A("dead", lo, hi), OP.mult)
+        tt(A("xb", t, V, 3), A("dead"), A("b", t, V, 3), OP.mult)
 
     def factors(t):
         if t == 0:
@@ -209,18 +224,15 @@ def build(g, T, topo, core):
             act(A("cl", 40, 120), P(0, 80)); act(A("cl", 120, 240), P(512, 120))
         tt(A("de"), A("cl", 120 * t + 80, 120 * t + 120), A("b480"), OP.subtract)
         k = 40 * t
-        cp(A("n1u", k, k + 40), A("de"))
+        ts(A("n1u", k, k + 40), A("de"), -float(BL), OP.add)
         tolist(P(0, 40), "z1", "ok", 0, 640)
         ts(A("dl"), P(0, 40), 1.0, OP.is_ge)
         tt(A("de"), A("cl", 120 * t + 40, 120 * t + 80), A("dl"), OP.mult)
         tt(A("de"), A("de"), A("fk", k, k + 40), OP.max); tt(A("de"), A("de"), A("b480"), OP.subtract)
         cp(A("n0u", k, k + 40), A("de"))
         for lo, hi in ((0, 512), (512, 640)):
-            mm(P(1024 + lo, hi - lo), [(A("id256"), A("xa", t + 3 * lo, 3 * hi, 3)), (A("idm"), A("dead", lo, hi))])
-        for b in range(4):
-            c = 320 * b + 160 * t
-            act(A("c0", c, c + 160), P(1024 + 160 * b, 160), bias=1.0)
-            act(A("c1", c, c + 160), A("xb", BL * b + t, BL * b + BL, 3), scale=1.0 / 256)
+            mm(P(lo, hi - lo), [(A("id256"), A("xa", t + 3 * lo, 3 * hi, 3)), (A("idm"), A("dead", lo, hi))])
+        act(A("c0", 640 * t, 640 * t + 640), P(0, 640), bias=1.0)
 
     def pair(name, pr, base=0):
         return A(name, base + 1024 * pr, base + 1024 * pr + 1024)
@@ -231,6 +243,7 @@ def build(g, T, topo, core):
             g0 = NP * pr
             lead[0] = PAR["lead"] if pr == 0 else 0.0
             mul_bank = P(2048 + 512 * pr, 512)
+            second = lambda c: (P(512 * c - 512, 512) if c % 2 else mul_bank) if PAR["raw"] else P(512 * c, 512)
             for tab, got, mul, mu, own, out in (("xa", "ga", vi, unit, ui, uo), ("xb", "gb", uo, "idn", vi, vo)):
                 for c in (2 * pr, 2 * pr + 1):
                     lo, hi = 512 * c, 512 * c + 512
@@ -239,23 +252,24 @@ def build(g, T, topo, core):
                         act(A(got, lo, hi), IX(A(tab), A("off", 32 * c, 32 * c + 32)))
                     elif c % 2 == 0:
                         act(pair(got, pr), IX(A(tab), A("off", 64 * pr, 64 * pr + 64)))
-                    mm(mul_bank, [(A(mu), A(mul, lo, hi))])
-                    mm(x, [(A("idn"), A("zall", 0, 512))], stop=False)
-                    tt(x, mul_bank, A(got, lo, hi), OP.mult)
-                    mm(x, [(A(unit), A(own, lo, hi))], start=False)
-                wd = PAR["wide"]
-                for lo in range(1024 * pr, 1024 * pr + 1024, wd):
-                    ts(A("q", lo, lo + wd), P(lo, wd), -127.5 / 256, OP.add)
-                    tt(A(out, lo, lo + wd), P(lo, wd), A("q", lo, lo + wd), OP.subtract)
+                    src = mul_bank
+                    if tab == "xb" and PAR["raw"]:
+                        src, x = x, second(c)
+                    else:
+                        mm(mul_bank, [(A(mu), A(mul, lo, hi))])
+                    mm(x, [(A("idn"), A(own, lo, hi))], stop=False)
+                    tt(x, src, A(got, lo, hi), OP.mult)
+                    less = vo == "vc" and tab == "xb"
+                    mm(x, [(A(unit), A(own, lo, hi))] + ([(A("idh"), A("mone"))] if less else []), start=False)
+                    q = A("q" if tab == "xa" else "q2", lo, hi)
+                    ts(q, x, (0.5 if less else -127.5) / 256, OP.add)
+                    tt(A(out, lo, hi), x, q, OP.subtract)
             act(A("gn", g0 + 1024, g0 + NP), IX(A("xn"), A("off", 64 * pr, 64 * pr + 64)))
             for c in (2 * pr, 2 * pr + 1):
                 lo, hi = 512 * c, 512 * c + 512
-                x, ge = P(lo, 512), A("gn", g0 + 512 * (c % 2), g0 + 512 * (c % 2) + 512)
+                x, ge = second(c), A("gn", g0 + 512 * (c % 2), g0 + 512 * (c % 2) + 512)
                 mm(x, [(A("idn"), A(uo, lo, hi)), (A("idm"), A(vo, lo, hi))])
-                if CMP_ON[c] == "v":
-                    ts(ge, x, 0.0, OP.is_ge, 2.0, OP.mult)
-                else:
-                    act(ge, x, AF.Sign, bias=1.0 / 512)
+                act(ge, x, AF.Sign, bias=1.0 / 512 - (0.5 if vo == "vc" else 0.0))
             bank = 3072 + 512 * pr
             f, s = A("face", 64 * pr, 64 * pr + 64), A("sg", 64 * pr, 64 * pr + 64)
             tolist(P(bank + 128, 64), "z2", "gn", g0 + 1024, g0 + NP)
@@ -277,6 +291,7 @@ def build(g, T, topo, core):
     def move(t):
         s0 = 132 * t
         sc, rs, rl = "sc", A("rs", CAP * t, CAP * t + CAP), A("rl", CAP * t, CAP * t + CAP)
+        mm(P(2304, 128), [(A("idn"), A("diag"))])
         ts(A("on"), A("face"), float(V), OP.is_ge)
         mm(P(2048, 128), [(A("blk"), A("on"))])
         mm(P(2176, 128), [(A("blkn"), A("on")), (A("blk"), A("rampb"))])
@@ -289,71 +304,84 @@ def build(g, T, topo, core):
         tot = A("s", s0 + 128, s0 + 129)
         send("c%d" % t, [(tot, [(T.cores[(rank + d) % n], A("land", 16 * t + 4 * d, 16 * t + 4 * d + 1)) for d in range(1, n)])])
         tt(A("o1"), P(2176, 128), A("s", s0, s0 + 128), OP.max)
-        tt(A("o1"), A("o1"), A("diag"), OP.mult)
+        tt(A("o1"), P(2304, 128), A("o1"), OP.mult)
         scan(A("o2"), A("reset"), A("o1"), OP.mult, OP.add)
         cp(A("offc"), A("o2", 15, 128, 16))
         win, oc, vl = A(sc), A("offc"), A("val")
         add("v", lambda: g.vector.tensor_copy(win[0].indirect(oc[0]), vl[0]), [oc, vl], [win], 50 + SC * 128)
-        scan(A("dk"), A("negk"), A(sc, 0, CAP), OP.add, OP.max)
-        act(rs, A("dk"), AF.Relu, bias=KK, scale=-1.0)
-        send("r%d" % t, [(rs, [(nxt, rl)])])
+        hc = CAP // 2
+        for k in range(2):
+            lo, hi = hc * k, hc * k + hc
+            scan(A("dk", lo, hi), A("negk", lo, hi), A(sc, lo, hi), OP.add, OP.max, A("dk", lo - 1, lo) if k else None)
+            act(A("rs", CAP * t + lo, CAP * t + hi), A("dk", lo, hi), AF.Relu, bias=KK, scale=-1.0)
+            if PAR["two"]:
+                send("rs"[k] + str(t), [(A("rs", CAP * t + lo, CAP * t + hi), [(nxt, A("rl", CAP * t + lo, CAP * t + hi))])])
+        if not PAR["two"]:
+            send("r%d" % t, [(rs, [(nxt, rl)])])
         if t == 0:
             iota(A(sc, 0, CAP), [[0, CAP]])
         act(A("ab"), A("dk"), AF.Abs, bias=-KK / 2)
-        act(A("es"), A("ab"), AF.Sign, bias=KK / 2 - 0.5, scale=-1.0)
-        act(A("e"), A("es"), AF.Relu); act(A("ne"), A("es"), AF.Relu, scale=-1.0)
-        tt(A("o3"), A("s", s0 + 1, s0 + 129), A("diag"), OP.mult)
+        act(A("ne"), A("ab"), AF.Sign, bias=0.5 - KK / 2)
+        tt(A("o3"), P(2304, 128), A("s", s0 + 1, s0 + 129), OP.mult)
         scan(A("o4"), A("reset"), A("o3"), OP.mult, OP.add)
         ts(A("endc"), A("o4", 15, 128, 16), -1.0, OP.add, CAP - 1.0, OP.min)
         tt(A("posx"), P(3072, 128), A("s", s0, s0 + 128), OP.add)
         m, m4, lr = A("m", t, t + 1), A("m", 4, 5), A("land", 16 * t + 4, 16 * t + 16, 4)
         add("v", lambda: g.vector.tensor_reduce(m[0], lr[0], AX.X, OP.min), [lr], [m], 114)
         ts(m, m, tot, OP.min, float(CAP), OP.min); ts(m4, m, -4096.0, OP.add)
-        ts(A("hb"), A("posx"), m4, OP.is_lt, 8192.0, OP.mult); tt(A("hb"), A("hb"), A("pid2"), OP.add)
-        ts(A("nlv"), A("posx"), m4, OP.is_ge, 4096.0, OP.mult)
+        hb, nlv = P(3200, 128), P(3328, 128)
+        ts(hb, A("posx"), m4, OP.is_lt, 8192.0, OP.mult); tt(hb, hb, A("pid2"), OP.add)
+        ts(nlv, A("posx"), m4, OP.is_ge, 4096.0, OP.mult)
         sh = m
         if t == 1:
             sh = A("m", 2, 3)
             ts(sh, m, A("m", 0, 1), OP.add)
         else:
             ts(A("cli"), A("cl", 120, 160), sh, OP.add); ts(A("clj"), A("cli"), NP - 1, OP.bitwise_and); cp(A("clu"), A("clj"))
-        mm(P(2560, CAP), [(A("blkf"), rl)])
-        tt(A("vv"), P(2560, CAP), A("e"), OP.mult)
-        scan(A("hs"), A("ne"), A("vv"), OP.mult, OP.add)
-        ts(A("y"), IX(A("hs"), A("endc")), -1.0, OP.add)
+        for k in range(2):
+            lo, hi = hc * k, hc * k + hc
+            o = P(2560 + 1024 * k, hc)
+            mm(o, [(A("blkf"), A("rl", CAP * t + lo, CAP * t + hi))])
+            tt(A("vv", lo, hi), o, A("ne", lo, hi), OP.mult)
+            scan(A("hs", lo, hi), A("ne", lo, hi), A("vv", lo, hi), OP.min, OP.max, A("hs", lo - 1, lo) if k else None)
+        ts(A("y"), IX(A("hs"), A("endc")), 2.0 ** 24, OP.mult, -1.0, OP.add)
         ts(A("y1"), A("y"), 6, OP.logical_shift_right, 0x1FF0, OP.bitwise_and); ts(A("y2"), A("y"), 19, OP.logical_shift_right)
-        tt(A("o1"), A("y1"), A("y2"), OP.add); tt(A("o1"), A("o1"), A("hb"), OP.min); ts(A("idx"), A("o1"), -float(NP), OP.add)
-        ts(A("y3"), A("y"), GH - 1, OP.bitwise_and); tt(A("o3"), A("y3"), A("nlv"), OP.max); tt(A("face"), A("face"), A("o3"), OP.min)
+        tt(A("o1"), A("y1"), A("y2"), OP.add); tt(A("o1"), hb, A("o1"), OP.min); ts(A("idx"), A("o1"), -float(NP), OP.add)
+        ts(A("y3"), A("y"), GH - 1, OP.bitwise_and); tt(nlv, nlv, A("y3"), OP.max); tt(A("face"), nlv, A("face"), OP.min)
         return sh
 
     def xlist(sh):
         ts(A("xi"), A("lstf", 0, 120), sh, OP.add); ts(A("xj"), A("xi"), NP - 1, OP.bitwise_and); cp(A("xu"), A("xj"))
 
-    def correct(w, usrc, nc, done):
+    def correct(w, usrc, nc):
         for b in range(3, -1, -1):
             lo, hi = BL * b, BL * b + BL
             ix = IX(A(usrc), A("xu", 30 * b, 30 * b + 30))
             if nc == 2 and b == 3:
-                tt(A(w, lo, hi), ix, A("k0", lo, hi), OP.add)
+                act(A("oh"), A("w0", lo, hi), scale=0.5)
+                tt(A(w, lo, hi), ix, A("oh"), OP.add)
             else:
-                o = P(512 * b, BL) if nc == 1 else P(1024 + 512 * b, BL)
-                act(A("xg", lo, hi), ix, bias=-128.0 if nc == 1 else 0.0)
+                o = P(3072 + 512 * (b % 2), BL) if nc == 1 else P(1024 + 512 * b, BL)
+                act(A("xg", lo, hi), ix, bias=-1.0 if nc == 1 else 0.0, scale=1.0 / 128 if nc == 1 else 1.0)
                 if nc == 1:
-                    mm(o, [(A("id64"), A("h", lo, hi)), (A("idn"), A("xg", lo, hi))])
+                    mm(o, [(A("idh"), A("h", lo, hi)), (A("idn"), A("xg", lo, hi))])
                 else:
-                    mm(o, [(A("idf"), A("k0", lo, hi))], stop=False)
+                    mm(o, [(A("idhf"), A("w0", lo, hi))], stop=False)
                     mm(o, [(A("idn"), A("xg", lo, hi))], start=False)
                 act(A(w, lo, hi), o)
+
+    def follow(w, nc, done):
         for b in range(3, -1, -1):
             win, k, c, o = A(w, BL * b, W), 160 * nc, 320 * b, P(3584, 160 * nc)
-            for p, lst, fac in (("p1", "n1u", "c1"), ("p0", "n0u", "c0")):
-                for t in range(nc):
-                    j = 40 * t + 10 * b
-                    tt(A(p, 160 * t, 160 * t + 160), IX(win, A(lst, j, j + 10)), A(fac, c + 160 * t, c + 160 * t + 160), OP.mult)
-            if nc == 2:
-                act(o, A("p1", 0, k))
+            bank = (3584, 2560)[b % 2] if nc == 2 else 512 * (b % 2)
             for t in range(nc):
-                tt(A(w, BL * b + t, BL * b + BL, 3), P(3584 + 160 * t, 160) if nc == 2 else A("p1", 0, 160), A("p0", 160 * t, 160 * t + 160), OP.add)
+                j, c = 40 * t + 10 * b, 640 * t + 160 * b
+                mm(P(bank + 160 * t, 160), [(A("id256"), A("xb", BL * b + t, BL * b + BL, 3))])
+                act(A("p1", 160 * t, 160 * t + 160), IX(A(w, BL * b + BL, W), A("n1u", j, j + 10)))
+                tt(A("p0", 160 * t, 160 * t + 160), IX(win, A("n0u", j, j + 10)), A("c0", c, c + 160), OP.mult)
+            tt(P(bank, k), P(bank, k), A("p1", 0, k), OP.mult)
+            for t in range(nc):
+                tt(A(w, BL * b + t, BL * b + BL, 3), P(bank + 160 * t, 160), A("p0", 160 * t, 160 * t + 160), OP.add)
             done(b)
 
     collapse(0, "ui")
@@ -361,26 +389,29 @@ def build(g, T, topo, core):
     hop("um", "vm", "ua", "va", "idn",
         lambda pr: send("uv0", [(pair(x, pr), [(nxt, pair(x, pr, NP))]) for x in ("ua", "va")]))
     factors(0)
+    steps(1, tbank[1])
     sh = move(0)
     half = lambda k: A("idx", 64 * k, 64 * k + 64)
     act(pair("u1", 0), IX(A("ua"), half(0)), scale=256.0); ts(pair("u1", 1), IX(A("ua"), half(1)), 256.0, OP.mult)
     for c in range(4):
         o, ix = A("v1", 512 * c, 512 * c + 512), IX(A("va"), A("idx", 32 * c, 32 * c + 32))
-        act(o, ix, scale=256.0)
+        if c in PAR["vdve"]:
+            ts(o, ix, 256.0, OP.mult)
+        else:
+            act(o, ix, scale=256.0)
     ts(A("off"), A("face"), float(V), OP.min)
     xlist(sh)
     collapse(1, "u1")
     hop("u1", "v1", "um", "vm", "id256", None)
+    correct("w0", "u1", 1)
     hop("um", "vm", "ub", "vc", "idn", lambda pr: send("u1", [(pair("ub", pr), [(nxt, pair("ub", pr, NP))])]))
-    correct("w0", "u1", 1, lambda b: None)
+    follow("w0", 1, lambda b: None)
     factors(1)
-    act(A("hsend"), A("w0", 0, GH), scale=1.0 / 128)
-    send("g1", [(A("hsend"), [(prv, A("w1", V, W))])])
-    act(A("k0"), A("w0", 0, V), scale=1.0 / 256)
+    send("g1", [(A("w0", 0, GH), [(prv, A("w1", V, W))])])
     for c in range(4):
         lo, hi = 512 * c, 512 * c + 512
-        act(A("uc", lo, hi), A("vc", lo, hi), bias=-0.5)
-        act(P(lo, 512), A("ub", lo, hi), bias=-0.5); tt(A("zz", lo, hi), P(lo, 512), A("uc", lo, hi), OP.mult)
+        mm(P(lo, 512), [(A("idn"), A("ub", lo, hi)), (A("idh"), A("mone"))])
+        tt(A("zz", lo, hi), P(lo, 512), A("vc", lo, hi), OP.mult)
     send("z1", [(A("zz", 0, NP), [(nxt, A("zz", NP, 2 * NP))])])
     sh = move(1)
     xlist(sh)
@@ -390,7 +421,8 @@ def build(g, T, topo, core):
     act(pair("sig", 1), IX(A("zz"), half(1)), AF.Sigmoid, scale=8.0)
     act(P(0, 1024), pair("sig", 1))
     act(pair("sig", 0), IX(A("zz"), half(0)), AF.Sigmoid, scale=8.0)
-    correct("w1", "u2", 2, lambda b: mm(P(3072, BL), [(A("idf"), A("w1", BL * b, BL * b + BL))], start=(b == 3), stop=(b == 0)))
+    correct("w1", "u2", 2)
+    follow("w1", 2, lambda b: mm(P(3072, BL), [(A("idf"), A("w1", BL * b, BL * b + BL))], start=(b == 3), stop=(b == 0)))
     for k in range(2):
         lo, hi = 512 * k, 512 * k + 512
         act(A("pw", GH + lo, GH + hi), IX(A("w1"), A("fu", 64 + 32 * k, 96 + 32 * k)))
@@ -487,6 +519,7 @@ def order(ops):
         way[i] = ns[i] + max([lag[i] + way[u] for u in users[i]] + [lag[i]])
     first = [-1e9 + i if ops[i]["lead"] > 1e5 else 0.0 for i in range(n)]
     best, base, r = None, [-w - o["lead"] for w, o in zip(way, ops)], PAR["seed"]
+    now = 1e18
     for turn in range(PAR["turns"]):
         key = list(base)
         if turn:
@@ -505,10 +538,78 @@ def order(ops):
         at, end = place([k + f for k, f in zip(key, first)], False)
         if end <= best[0]:
             best = (end, at)
-        base = best[1]
+        if end <= min(now, best[0] + 1e9 * (turn > 0)) + PAR["give"] * (1.0 - turn / PAR["turns"]):
+            base, now = at, end
+        if best[0] < now - PAR["give"] * 4:
+            now, base = best
+    seq = sorted(range(n), key=lambda i: (best[1][i], i))
+    qs = ["vapgs".index(o["q"]) for o in ops]
+    bset = [set(b) for b in before]
+
+    def run(sq):
+        free, last, done, why = [0.0] * 5, [-1] * 5, [0.0] * n, [0] * n
+        for i in sq:
+            q = qs[i]
+            t, w = free[q], -2 - last[q]
+            for j in before[i]:
+                if done[j] > t:
+                    t, w = done[j], j
+            why[i] = w
+            free[q] = t = t + ns[i]
+            last[q] = i
+            done[i] = t + lag[i]
+        i = max(range(n), key=lambda x: done[x])
+        end, arcs = done[i] - lat, []
+        while i >= 0:
+            w = why[i]
+            if w <= -2:
+                w = -2 - w
+                if ops[w]["lead"] < 1e5:
+                    arcs.append((w, i))
+            i = w
+        return end, arcs, done
+
+    now, arcs, done = run(seq)
+    top = (now, seq)
+    for turn in range(PAR["swaps"]):
+        r = (r * 1103515245 + 12345) % 2147483648
+        j, i = arcs[(r >> 8) % len(arcs)]
+        a, b = seq.index(j), seq.index(i)
+        r = (r * 1103515245 + 12345) % 2147483648
+        if (r >> 9) % 2:
+            a = max(0, a - (r >> 12) % PAR["reach"] * ((r >> 10) % 2))
+            need, up, rest = set(bset[i]), [i], []
+            for x in reversed(seq[a:b]):
+                if x in need:
+                    up.append(x)
+                    need.update(bset[x])
+                else:
+                    rest.append(x)
+            if j in need:
+                continue
+            new = seq[:a] + up[::-1] + rest[::-1] + seq[b + 1:]
+        else:
+            b = min(n - 1, b + (r >> 12) % PAR["reach"] * ((r >> 10) % 2))
+            gone, down, rest = {j}, [j], []
+            for x in seq[a + 1:b + 1]:
+                if bset[x] & gone:
+                    gone.add(x)
+                    down.append(x)
+                else:
+                    rest.append(x)
+            if i in gone:
+                continue
+            new = seq[:a] + rest + down + seq[b + 1:]
+        end, ar, dn = run(new)
+        r = (r * 1103515245 + 12345) % 2147483648
+        if end <= now + PAR["heat"] * (1.0 - turn / PAR["swaps"]) * (r >> 8) / 8388608:
+            now, arcs, seq = end, ar, new
+            if end < top[0]:
+                top = (end, new)
+    done = run(top[1])[2]
     for i in range(n):
-        ops[i]["at"] = best[1][i]
-    return sorted(range(n), key=lambda i: (best[1][i], i))
+        ops[i]["at"] = done[i] - lag[i] - ns[i]
+    return top[1]
 
 
 def rank_program(g, core, T, topo):

@@ -3,9 +3,11 @@ from concourse.mybir import AluOpType as OP, AxisListType as AX, ActivationFunct
 
 V, GH, BL, NP, CAP, W = 1920, 1024, 480, 2048, 512, 2944
 KK = float(2 ** 19)
-RND = 1.5 * 2.0 ** 31
 RND64 = 1.5 * 2.0 ** 29
-CMP_ON = "aaaa"
+CONV_U = ["gggg", "gggg", "gggg", "gggg"]
+CONV_V = ["gggg", "gggg", "gggg", "aaaa"]
+CMP_ON = ["vvva", "vvva", "vvva", "vvvv"]
+GN_ON = ["aa", "aa", "aa", "aa"]
 
 F, B, I, U = "float32", "bfloat16", "int32", "uint16"
 COLS = {
@@ -17,23 +19,23 @@ COLS = {
     "negk": (CAP, F), "dd": (240, F), "dhi": (240, B), "dlo": (240, B), "tst": (V, B), "xa": (1936, B), "xb": (1936, B), "xn": (1936, B),
     "cl": (240, F), "fk": (80, F), "b480": (40, F), "cli": (40, I), "clj": (40, I), "clu": (40, U), "cx": (640, F), "cy": (640, B), "ok": (640, B), "dead": (640, B),
     "dl": (40, F), "de": (40, F), "n0u": (80, U), "n1u": (80, U), "c0": (1280, B),
-    "face": (128, F), "off": (128, U), "ga": (NP, B), "gb": (NP, B), "q": (NP, I), "gn": (2 * NP, B), "um": (NP, B), "vm": (NP, B),
-    "ua": (2 * NP, B), "va": (2 * NP, B), "ub": (2 * NP, B), "zz": (2 * NP, F), "u1": (NP, B), "v1": (NP, B),
+    "face": (128, F), "off": (128, U), "ga": (NP, F), "gb": (NP, F), "q": (NP, I), "q2": (NP, I), "gn": (2 * NP, B), "um": (NP, B), "vm": (NP, B),
+    "ua": (2 * NP, B), "va": (2 * NP, B), "ub": (2 * NP, B), "zz": (2 * NP, F), "id512": (128, B),
     "sg": (128, F), "on": (128, B), "s": (2 * 132, F), "land": (32, F), "o1": (128, F), "o2": (128, F), "o3": (128, F), "o4": (128, F),
-    "offc": (8, U), "endc": (8, U), "val": (128, F), "v2": (128, B), "gj": (128, F), "sc": (4096, F), "dk": (CAP, F), "rs": (2 * CAP, F), "rl": (2 * CAP, F),
-    "ab": (CAP, F), "ne": (CAP, B), "mone": (512, B), "y": (128, I), "y1": (128, I), "y2": (128, I), "y3": (128, I),
+    "offc": (8, U), "endc": (8, U), "val": (128, F), "v2": (128, B), "gj": (128, F), "sc": (NP + 128, F), "dk": (CAP, F), "rs": (2 * CAP, F), "rl": (2 * CAP, F),
+    "ab": (CAP, F), "ne": (CAP, B), "quart": (512, B), "y": (128, I), "y1": (128, I), "y2": (128, I), "y3": (128, I),
     "posx": (128, F), "hb": (128, F), "nlv": (128, F), "m": (8, F), "idx": (128, U), "xi": (120, I), "xj": (120, I), "xu": (120, U),
-    "hl": (GH, B), "pw": (NP, F), "w0": (W, F), "w1": (W, F), "ow": (GH, F), "idhf": (128, F), "p0": (320, F), "p1": (320, F),
+    "hl": (GH, B), "w0": (W, F), "w1": (W, F), "ow": (GH, F), "idhf": (128, F), "p0": (320, F), "p1": (320, F),
     "oh": (BL, F), "fu": (128, U),
 }
-SAME = {"q2": "q", "sig": "sc", "u2": "um", "vc": "v1", "vv": "ab", "hs": "dk", "xg": "tst", "uc": "ga"}
+SAME = {"sig": "sc", "u2": "um", "u1": "ui", "v1": "vi", "vc": "vi", "vv": "ab", "hs": "dk", "xg": "tst", "pw": "ga"}
 del COLS["ta"]
 SCRATCH = {k: ("sbuf", [128, n], d) for k, (n, d) in COLS.items()}
 SCRATCH["ps"] = ("psum", [128, 4096], F)
 LOADS = ["sd", "na", "nb", "pf", "th", "u0", "ta", "v0", "tb", "h0"]
 REMOTE = ["h", "c0", "uv0", "r0", "g1", "c1", "u1", "r1", "z1", "s0", "s1"]
-SEMAPHORES = ["ev", "ea", "ep", "eg", "sent"] + ["l" + k for k in LOADS] + ["r" + k for k in REMOTE] + ["o0", "o1", "o2"]
-PAR = {"raw": True, "two": True, "swaps": 100000, "heat": 250.0, "reach": 12, "zact": False, "give": 100.0, "vdve": (2,), "span": 1500.0,
+SEMAPHORES = ["ev", "ea", "ep", "eg", "sent"] + ["l" + k for k in LOADS] + ["r" + k for k in REMOTE] + ["o0", "o1", "o2", "zxb", "zxn"]
+PAR = {"zdma": ("xb", "xn"), "two": True, "swaps": 100000, "heat": 250.0, "reach": 12, "zact": False, "give": 100.0, "vdve": (2,), "span": 1500.0,
        "lead": 7000.0, "lat": 120.0, "seed": 1, "turns": 500, "shake": 800.0}
 KEPT = {}
 CY, PE, GA, SC = 1.0, 0.5, 1.56, 3.8
@@ -123,6 +125,17 @@ def build(g, T, topo, core):
     def store(sem, dst, i):
         add("s", lambda: g.sync.dma_start(dst, i[0]), [i], [], 60, ("dma", sem, 2000 + i[2]))
 
+    def copy(sem, o, i):
+        add("s", lambda: g.sync.dma_start(o[0], i[0]), [i], [o], 60, ("dma", sem, 3000))
+
+    def conv(e, o, i, bias=0.0):
+        if e == "g":
+            add("g", lambda: g.affine_select(o[0], i[0], [[0, o[2]]], OP.is_ge, 0.0, 0, 0), [i], [o], 170 + 2 * CY * o[2])
+        elif e == "a":
+            act(o, i, bias=bias)
+        else:
+            ts(o, i, bias, OP.add)
+
     def send(sem, items):
         engs = [e for e in topo.engines(core, items[0][1][0][0]) if all(e in topo.engines(core, c) for s, ds in items for c, d in ds)]
         per = len(engs) // len(items)
@@ -160,7 +173,7 @@ def build(g, T, topo, core):
                 act(o, A("v64"), AF.Abs, bias=A("pc", 6, 7)); act(o, o, AF.Relu, bias=1.0, scale=-1.0)
     ts(A("blk"), A("a16"), pgr, OP.is_equal); ts(A("idn"), A("c128"), pp, OP.is_equal)
     for name, src, f in (("blkf", "blk", -2.0 ** -24), ("blkn", "blk", -4096.0), ("idm", "idn", -1.0), ("id256", "idn", 1.0 / 256), ("idf", "idn", 1.0),
-                         ("idmf", "idn", -1.0), ("id4k", "idn", -4096.0), ("idh", "idn", 0.5), ("idhf", "idn", 0.5)):
+                         ("idmf", "idn", -1.0), ("id4k", "idn", -4096.0), ("idh", "idn", 0.5), ("idhf", "idn", 0.5), ("id512", "idn", 512.0)):
         act(A(name), A(src), scale=f)
     add("g", lambda: g.affine_select(T.tri[:], T.blk[:], [[1, 128]], OP.is_gt, 0.0, 0, -1), [A("blk")], [A("tri")], 170 + 256)
     act(A("trik"), A("tri"), scale=KK)
@@ -177,15 +190,21 @@ def build(g, T, topo, core):
         [A("half")], [A("zall")], 170 + 288)
     act(A("pidx"), A("c128"), bias=pmod, scale=16.0); act(A("pid2"), A("pidx"), bias=float(NP))
     ts(A("diag"), A("i16"), pmod, OP.is_equal); act(A("reset"), A("i16"), AF.Sign)
-    act(A("rampv"), A("c128"), bias=1024.0 * 256, scale=-1024.0); act(A("rampb"), A("c128"), bias=128.0)
+    act(A("rampv"), A("c128"), bias=1024.0 * 256, scale=-1024.0)
+    ts(A("pc", 6, 7), pmod, 0.0, OP.is_equal); ts(A("pc", 7, 8), pmod, 1.0, OP.is_equal, float(NP), OP.mult)
+    act(A("rampb"), A("c128"), bias=A("pc", 7, 8), scale=A("pc", 6, 7))
     iota(A("one"), [[0, 128]], 1); iota(A("b480"), [[BL, 4], [0, 10]])
-    for x in ("xa", "xb", "xn"):
-        iota(A(x, 1, 1936, 3), [[0, 645]]); iota(A(x, 2, 1936, 3), [[0, 645]]); iota(A(x, V, V + 1), [[0, 1]])
-    iota(A("negk"), [[0, CAP]], -int(KK)); iota(A("mone"), [[0, 512]], -1); iota(A("sc", 0, CAP), [[0, CAP]])
+    fill(A("xa"), 0.0)
+    for x in ("xb", "xn"):
+        if x in PAR["zdma"]:
+            copy("z" + x, A(x), A("xa"))
+        else:
+            fill(A(x), 0.0)
+    iota(A("negk"), [[0, CAP]], -int(KK)); fill(A("quart"), -0.25); iota(A("sc", 0, CAP), [[0, CAP]])
     iota(A("s", 0, 133, 132), [[0, 2]])
     for t in range(2):
         act(A("fk", 40 * t, 40 * t + 40), A("pidx", 0, 40), bias=float(t), scale=3.0)
-    cp(A("lstf", 0, 120), A("lst", 0, 120)); cp(A("lstf", 120, 360), A("lst", 120, 360)); ts(A("thf"), A("thi"), 0.5, OP.add)
+    cp(A("lstf", 0, 120), A("lst", 0, 120)); cp(A("lstf", 120, 360), A("lst", 120, 360)); act(A("thf"), A("thi"), bias=0.5)
     cp(A("face"), A("pfi")); ts(A("off"), A("face"), float(V), OP.min)
     pmx = lambda t, r: A("pm", 128 * (3 * t + r), 128 * (3 * t + r + 1))
     mm(P(2048, 40), [(pmx(0, r), A("lstf", r, 120, 3)) for r in range(3)])
@@ -203,7 +222,7 @@ def build(g, T, topo, core):
     tbank = ((3072, 3584), (1024, 1536))
     steps(0, tbank[0])
     send("h", [(A("h", 0, GH), [(prv, A("hl"))])])
-    act(A("w0", V, W), A("hl"))
+    conv("g", A("w0", V, W), A("hl"))
 
     def collapse(t, usrc):
         for k in range(2):
@@ -237,50 +256,52 @@ def build(g, T, topo, core):
     def pair(name, pr, base=0):
         return A(name, base + 1024 * pr, base + 1024 * pr + 1024)
 
-    def hop(ui, vi, uo, vo, unit, after):
-        seen = []
+    def hop(k, ui, vi, uo, vo, after):
+        last = vo == "vc"
         for pr in range(2):
             g0 = NP * pr
             lead[0] = PAR["lead"] if pr == 0 else 0.0
-            mul_bank = P(2048 + 512 * pr, 512)
-            second = lambda c: (P(512 * c - 512, 512) if c % 2 else mul_bank) if PAR["raw"] else P(512 * c, 512)
-            for tab, got, mul, mu, own, out in (("xa", "ga", vi, unit, ui, uo), ("xb", "gb", uo, "idn", vi, vo)):
+            for tab, got, mul, own, out, q, bank, on in (("xa", "ga", vi, ui, uo, "q", 0, CONV_U), ("xb", "gb", uo, vi, vo, "q2", 1024, CONV_V)):
                 for c in (2 * pr, 2 * pr + 1):
                     lo, hi = 512 * c, 512 * c + 512
-                    x = P(lo, 512)
+                    x = P(bank + 512 * (c % 2), 512)
                     if tab == "xa":
-                        act(A(got, lo, hi), IX(A(tab), A("off", 32 * c, 32 * c + 32)))
+                        act(A(got, lo, hi), IX(A(tab), A("off", 32 * c, 32 * c + 32)), bias=1.0 / 256, scale=2.0)
                     elif c % 2 == 0:
-                        act(pair(got, pr), IX(A(tab), A("off", 64 * pr, 64 * pr + 64)))
-                    src = mul_bank
-                    if tab == "xb" and PAR["raw"]:
-                        src, x = x, second(c)
-                    else:
-                        mm(mul_bank, [(A(mu), A(mul, lo, hi))])
-                    mm(x, [(A("idn"), A(own, lo, hi))], stop=False)
-                    tt(x, src, A(got, lo, hi), OP.mult)
-                    less = vo == "vc" and tab == "xb"
-                    mm(x, [(A(unit), A(own, lo, hi))] + ([(A("idh"), A("mone"))] if less else []), start=False)
-                    q = A("q" if tab == "xa" else "q2", lo, hi)
-                    ts(q, x, (0.5 if less else -127.5) / 256, OP.add)
-                    tt(A(out, lo, hi), x, q, OP.subtract)
-            act(A("gn", g0 + 1024, g0 + NP), IX(A("xn"), A("off", 64 * pr, 64 * pr + 64)))
+                        act(pair(got, pr), IX(A(tab), A("off", 64 * pr, 64 * pr + 64)), bias=1.0 / 256, scale=2.0)
+                    mm(x, [(A("id512"), A(own, lo, hi)), (A("idn"), A(mul, lo, hi))])
+                    tt(A(q, lo, hi), x, A(got, lo, hi), OP.mult)
+                    ts(A(q, lo, hi), A(q, lo, hi), 1, OP.arith_shift_right, 255, OP.bitwise_and)
+                    conv(on[k][c], A(out, lo, hi), A(q, lo, hi), -128.0 if out == "vc" else 0.0)
+            ix = IX(A("xn"), A("off", 64 * pr, 64 * pr + 64))
+            if GN_ON[k][pr] == "a":
+                act(A("gn", g0 + 1024, g0 + NP), ix)
+            else:
+                cp(A("gn", g0 + 1024, g0 + NP), ix)
+            kinds = CMP_ON[k][2 * pr:2 * pr + 2]
             for c in (2 * pr, 2 * pr + 1):
                 lo, hi = 512 * c, 512 * c + 512
-                x, ge = second(c), A("gn", g0 + 512 * (c % 2), g0 + 512 * (c % 2) + 512)
-                mm(x, [(A("idn"), A(uo, lo, hi)), (A("idm"), A(vo, lo, hi))])
-                act(ge, x, AF.Sign, bias=1.0 / 512 - (0.5 if vo == "vc" else 0.0))
+                x, ge = P(2048 + 512 * (c % 2), 512), A("gn", g0 + 512 * (c % 2), g0 + 512 * (c % 2) + 512)
+                if kinds[c % 2] == "a":
+                    y = P(1024 + 512 * (c % 2), 512) if last else x
+                    mm(y, [(A("idn"), A(uo, lo, hi)), (A("idm"), A(vo, lo, hi))])
+                    act(ge, y, AF.Sign, bias=-127.5 if last else 0.5)
+                if kinds[c % 2] == "v" or last:
+                    mm(x, [(A("idn"), A(uo, lo, hi))] + ([(A("id512"), A("quart"))] if last else []))
+                if kinds[c % 2] == "v":
+                    tt(ge, x, A(vo if last else "q2", lo, hi), OP.is_ge)
+                if last:
+                    tt(A("zz", lo, hi), x, A(vo, lo, hi), OP.mult)
             bank = 3072 + 512 * pr
             f, s = A("face", 64 * pr, 64 * pr + 64), A("sg", 64 * pr, 64 * pr + 64)
             tolist(P(bank + 128, 64), "z2", "gn", g0 + 1024, g0 + NP)
             tolist(P(bank + 64, 64), "z1", "gn", g0 + 1024, g0 + NP, [(A("idf"), f)])
             tolist(P(bank + 192, 64), "z1", "gn", g0, g0 + 1024)
-            kinds = CMP_ON[2 * pr:2 * pr + 2]
             if kinds[0] == kinds[1]:
-                act(s, P(bank + 192, 64), AF.Sign, bias=-17.0 if kinds[0] == "v" else -1.0)
+                act(s, P(bank + 192, 64), AF.Sign, bias=-8.5 if kinds[0] == "v" else -1.0)
             else:
                 for j in range(2):
-                    act(A("sg", 64 * pr + 32 * j, 64 * pr + 32 * j + 32), P(bank + 192 + 32 * j, 32), AF.Sign, bias=-17.0 if kinds[j] == "v" else -1.0)
+                    act(A("sg", 64 * pr + 32 * j, 64 * pr + 32 * j + 32), P(bank + 192 + 32 * j, 32), AF.Sign, bias=-8.5 if kinds[j] == "v" else -1.0)
             tt(s, P(bank + 128, 64), s, OP.mult)
             tt(f, P(bank + 64, 64), s, OP.add)
             if after is None:
@@ -385,42 +406,38 @@ def build(g, T, topo, core):
             done(b)
 
     collapse(0, "ui")
-    hop("ui", "vi", "um", "vm", "id256", None)
-    hop("um", "vm", "ua", "va", "idn",
+    hop(0, "ui", "vi", "um", "vm", None)
+    hop(1, "um", "vm", "ua", "va",
         lambda pr: send("uv0", [(pair(x, pr), [(nxt, pair(x, pr, NP))]) for x in ("ua", "va")]))
     factors(0)
     steps(1, tbank[1])
     sh = move(0)
     half = lambda k: A("idx", 64 * k, 64 * k + 64)
-    act(pair("u1", 0), IX(A("ua"), half(0)), scale=256.0); ts(pair("u1", 1), IX(A("ua"), half(1)), 256.0, OP.mult)
+    act(pair("u1", 0), IX(A("ua"), half(0))); cp(pair("u1", 1), IX(A("ua"), half(1)))
     for c in range(4):
         o, ix = A("v1", 512 * c, 512 * c + 512), IX(A("va"), A("idx", 32 * c, 32 * c + 32))
         if c in PAR["vdve"]:
-            ts(o, ix, 256.0, OP.mult)
+            cp(o, ix)
         else:
-            act(o, ix, scale=256.0)
+            act(o, ix)
     ts(A("off"), A("face"), float(V), OP.min)
     xlist(sh)
     collapse(1, "u1")
-    hop("u1", "v1", "um", "vm", "id256", None)
+    hop(2, "u1", "v1", "um", "vm", None)
     correct("w0", "u1", 1)
-    hop("um", "vm", "ub", "vc", "idn", lambda pr: send("u1", [(pair("ub", pr), [(nxt, pair("ub", pr, NP))])]))
+    hop(3, "um", "vm", "ub", "vc", lambda pr: send("u1", [(pair("ub", pr), [(nxt, pair("ub", pr, NP))])]))
     follow("w0", 1, lambda b: None)
     factors(1)
     send("g1", [(A("w0", 0, GH), [(prv, A("w1", V, W))])])
-    for c in range(4):
-        lo, hi = 512 * c, 512 * c + 512
-        mm(P(lo, 512), [(A("idn"), A("ub", lo, hi)), (A("idh"), A("mone"))])
-        tt(A("zz", lo, hi), P(lo, 512), A("vc", lo, hi), OP.mult)
     send("z1", [(A("zz", 0, NP), [(nxt, A("zz", NP, 2 * NP))])])
     sh = move(1)
     xlist(sh)
-    act(pair("u2", 0), IX(A("ub"), half(0)), bias=-1.0, scale=2.0)
-    ts(pair("u2", 1), IX(A("ub"), half(1)), 2.0, OP.mult, -1.0, OP.add)
+    act(pair("u2", 0), IX(A("ub"), half(0)), bias=-1.0, scale=1.0 / 128)
+    ts(pair("u2", 1), IX(A("ub"), half(1)), 1.0 / 128, OP.mult, -1.0, OP.add)
     cp(A("fu"), A("face"))
-    act(pair("sig", 1), IX(A("zz"), half(1)), AF.Sigmoid, scale=8.0)
+    act(pair("sig", 1), IX(A("zz"), half(1)), AF.Sigmoid, scale=2.0 ** -13)
     act(P(0, 1024), pair("sig", 1))
-    act(pair("sig", 0), IX(A("zz"), half(0)), AF.Sigmoid, scale=8.0)
+    act(pair("sig", 0), IX(A("zz"), half(0)), AF.Sigmoid, scale=2.0 ** -13)
     correct("w1", "u2", 2)
     follow("w1", 2, lambda b: mm(P(3072, BL), [(A("idf"), A("w1", BL * b, BL * b + BL))], start=(b == 3), stop=(b == 0)))
     for k in range(2):

@@ -3,29 +3,29 @@ from concourse.mybir import AluOpType as OP, AxisListType as AX, ActivationFunct
 
 V, GH, BL, NP, CAP, W = 1920, 1024, 480, 2048, 512, 2944
 KK = float(2 ** 19)
+BIG = float(2 ** 26)
 RND64 = 1.5 * 2.0 ** 29
-CONV_U = ["gggg", "gggg", "gggg", "gggg"]
-CONV_V = ["gggg", "gggg", "gggg", "aaaa"]
-CMP_ON = ["vvva", "vvva", "vvva", "vvvv"]
-GN_ON = ["aa", "aa", "aa", "aa"]
+CMP_ON = ["avvv", "avvv", "avvv", "vvvv"]
+TEST_ON = ["aa", "av"]
+LIVE_ON = list("aavv")
 
 F, B, I, U = "float32", "bfloat16", "int32", "uint16"
 COLS = {
-    "ta": 0, "a": (V, B), "b": (V, B), "h": (V, B), "ui": (NP, B), "vi": (NP, B), "lst": (360, I), "pfi": (128, I), "thi": (2, I),
-    "lstf": (360, F), "thf": (2, F), "pi": (1, I), "pj": (2, I), "pc": (8, F), "c128": (128, F), "i16": (128, F), "a16": (128, F), "v64": (128, F),
+    "ta": 0, "a": (V, B), "b": (V, B), "h": (V, B), "ui": (NP + 16, B), "vi": (NP, B), "lst": (360, I), "pfi": (128, I), "thi": (2, I),
+    "lstf": (360, F), "thf": (6, F), "pi": (1, I), "pj": (3, I), "pc": (24, F), "c128": (128, F), "i16": (128, F), "id8m": (128, B), "v64": (128, F),
     "blkf": (128, F), "blk": (128, B), "blkn": (128, B), "idn": (128, B), "idm": (128, B), "id256": (128, B), "idf": (128, F), "idmf": (128, F),
-    "trik": (128, B), "tri": (128, B), "id4k": (128, B), "z1": (144, B), "z2": (144, B), "zall": (2304, B), "half": (144, B), "idh": (128, B),
-    "pm": (768, F), "diag": (128, B), "reset": (128, F), "pidx": (128, F), "pid2": (128, F), "rampv": (128, B), "rampb": (128, B), "one": (128, F),
-    "negk": (CAP, F), "dd": (240, F), "dhi": (240, B), "dlo": (240, B), "tst": (V, B), "xa": (1936, B), "xb": (1936, B), "xn": (1936, B),
-    "cl": (240, F), "fk": (80, F), "b480": (40, F), "cli": (40, I), "clj": (40, I), "clu": (40, U), "cx": (640, F), "cy": (640, B), "ok": (640, B), "dead": (640, B),
-    "dl": (40, F), "de": (40, F), "n0u": (80, U), "n1u": (80, U), "c0": (1280, B),
-    "face": (128, F), "off": (128, U), "ga": (NP, F), "gb": (NP, F), "q": (NP, I), "q2": (NP, I), "gn": (2 * NP, B), "um": (NP, B), "vm": (NP, B),
+    "trik": (128, B), "tri": (128, B), "id4k": (128, B), "z1": (144, B), "z2": (144, B), "pick": (512, B), "four": (608, B), "wide": (152, F), "idw": (152, B), "stack": (480, B), "z3": (144, B), "sb": (128, B), "idh": (128, B),
+    "pm": (768, F), "diag": (128, B), "reset": (128, B), "pidx": (128, F), "ownc": (128, F), "rampv": (128, B), "rampb": (128, B), "one": (128, F),
+    "posk": (CAP // 2, F), "zero": (CAP // 2, F), "mask": (130, B), "dmask": (128, B), "dd": (240, F), "dhi": (240, B), "dlo": (240, B), "tst": (V, B), "xa": (1936, B), "xb": (1936, B), "xn": (1936, B),
+    "cl": (200, F), "fk": (160, F), "b480": (80, F), "ten": (40, F), "cli": (40, I), "clj": (40, I), "clu": (40, U), "cx": (640, F), "cy": (640, B), "ok": (640, B), "dead": (V, B),
+    "dl": (80, B), "dz": (60, F), "de": (80, F), "nu": (160, U), "c0": (1280, B),
+    "face": (128, F), "off": (128, U), "ga": (NP, F), "gb": (NP, F), "q": (NP, I), "q2": (NP, I), "gn": (2 * NP, B), "um": (NP + 16, B), "vm": (NP, B),
     "ua": (2 * NP, B), "va": (2 * NP, B), "ub": (2 * NP, B), "zz": (2 * NP, F), "id512": (128, B),
     "sg": (128, F), "on": (128, B), "s": (2 * 132, F), "land": (32, F), "o1": (128, F), "o2": (128, F), "o3": (128, F), "o4": (128, F),
     "offc": (8, U), "endc": (8, U), "val": (128, F), "v2": (128, B), "gj": (128, F), "sc": (NP + 128, F), "dk": (CAP, F), "rs": (2 * CAP, F), "rl": (2 * CAP, F),
     "ab": (CAP, F), "ne": (CAP, B), "quart": (512, B), "y": (128, I), "y1": (128, I), "y2": (128, I), "y3": (128, I),
-    "posx": (128, F), "hb": (128, F), "nlv": (128, F), "m": (8, F), "idx": (128, U), "xi": (120, I), "xj": (120, I), "xu": (120, U),
-    "hl": (GH, B), "w0": (W, F), "w1": (W, F), "ow": (GH, F), "idhf": (128, F), "p0": (320, F), "p1": (320, F),
+    "hb": (128, F), "m": (8, F), "idx": (128, U), "xi": (120, I), "xj": (120, I), "xu": (240, U),
+    "hl": (GH, B), "w0": (W + 8, F), "w1": (W + 8, F), "ow": (GH, F), "idhf": (128, F), "p0": (320, F), "p1": (320, F),
     "oh": (BL, F), "fu": (128, U),
 }
 SAME = {"sig": "sc", "u2": "um", "u1": "ui", "v1": "vi", "vc": "vi", "vv": "ab", "hs": "dk", "xg": "tst", "pw": "ga"}
@@ -34,18 +34,19 @@ SCRATCH = {k: ("sbuf", [128, n], d) for k, (n, d) in COLS.items()}
 SCRATCH["ps"] = ("psum", [128, 4096], F)
 LOADS = ["sd", "na", "nb", "pf", "th", "u0", "ta", "v0", "tb", "h0"]
 REMOTE = ["h", "c0", "uv0", "r0", "g1", "c1", "u1", "r1", "z1", "s0", "s1"]
-SEMAPHORES = ["ev", "ea", "ep", "eg", "sent"] + ["l" + k for k in LOADS] + ["r" + k for k in REMOTE] + ["o0", "o1", "o2", "zxb", "zxn"]
-PAR = {"zdma": ("xb", "xn"), "two": True, "swaps": 100000, "heat": 250.0, "reach": 12, "zact": False, "give": 100.0, "vdve": (2,), "span": 1500.0,
-       "lead": 7000.0, "lat": 120.0, "seed": 1, "turns": 500, "shake": 800.0}
+SEMAPHORES = ["ev", "ea", "ep", "eg", "sent"] + ["l" + k for k in LOADS] + ["r" + k for k in REMOTE] + ["o0", "o1", "o2", "zxb", "lh1"]
+PAR = {"gb": 1024, "gn": 1024, "flip": 6, "drop": 500.0, "zb": 3072, "ints": "va", "early": 0.0, "marks": (), "sort": 200, "hns": 3000, "wide": True, "gz": False, "two": True, "halves": "v1", "swaps": 150000, "heat": 300.0, "reach": 30, "zact": False, "give": 100.0, "vdve": (2,), "span": 1500.0,
+       "lead": 7000.0, "lat": 120.0, "seed": 2, "turns": 30, "shake": 800.0}
 KEPT = {}
 CY, PE, GA, SC = 1.0, 0.5, 1.56, 3.8
+CASES = [(GA, SC, 120.0, 1.0, 2000.0, 0.4), (1.2, 2.5, 120.0, 2.0, 2600.0, 0.6), (1.95, 4.0, 110.0, 1.0, 1700.0, 0.3)]
 
 
 def build(g, T, topo, core):
     rank = T.rank_of(core)
     n = len(T.cores)
     nxt, prv = T.cores[(rank + 1) % n], T.cores[(rank - 1) % n]
-    ops, lead = [], [0.0]
+    ops, lead, moved = [], [0.0], [0]
 
     def A(name, lo=0, hi=None, st=1):
         name = SAME.get(name, name)
@@ -63,8 +64,16 @@ def build(g, T, topo, core):
     def wide(*xs):
         return 0.5 if all(x[3] != "*" and SCRATCH[x[3]][2] in (B, U) for x in xs) else 1.0
 
-    def add(q, fn, rd, wr, ns, kind=None):
-        ops.append(dict(q=q, fn=fn, rd=[r for x in rd for r in x[1]], wr=[r for x in wr for r in x[1]], ns=ns, kind=kind, lead=lead[0]))
+    def add(q, fn, rd, wr, ns, kind=None, se=0):
+        ops.append(dict(q=q, fn=fn, rd=[r for x in rd for r in x[1]], wr=[r for x in wr for r in x[1]], ns=ns, kind=kind, lead=lead[0],
+                        ge=sum(x[2] for x in rd if x[3] == "*"), se=se, ways=[(q, fn, ns)]))
+
+    def either(*calls):
+        for call in calls:
+            call()
+        ways = [ops.pop() for call in calls[1:]][::-1]
+        ops[-1]["ways"] += [o["ways"][0] for o in ways]
+        ops[-1]["rd"] += [r for o in ways for r in o["rd"] if r not in ops[-1]["rd"]]
 
     def cost(o, i, f=1.0):
         if i[3] == "*":
@@ -85,17 +94,23 @@ def build(g, T, topo, core):
         f = 1.0 if "ps" in (x[3], y[3]) else 2.0 * wide(o, x, y)
         add("v", lambda: g.vector.tensor_tensor(o[0], x[0], y[0], op), [x, y], [o], cost(o, x, f))
 
-    def cp(o, i):
-        add("v", lambda: g.vector.tensor_copy(o[0], i[0]), [i], [o], cost(o, i, wide(o, i)))
+    def cp(o, i, bias=0.0):
+        lin(o, i, 1.0, bias, PAR["ints"])
 
-    def scan(o, d0, d1, o0, o1, init=None):
-        add("v", lambda: g.vector.tensor_tensor_scan(o[0], d0[0], d1[0], init[0] if init else 0.0, o0, o1),
+    def scan(o, d0, d1, o0, o1, init=None, first=0.0):
+        add("v", lambda: g.vector.tensor_tensor_scan(o[0], d0[0], d1[0], init[0] if init else first, o0, o1),
             [d0, d1] + ([init] if init else []), [o], cost(o, d0))
 
     def fill(o, c):
         add("v", lambda: g.vector.memset(o[0], c), [], [o], 50 + CY * max(64, o[2] * wide(o)))
 
-    def act(o, i, f=AF.Identity, bias=0.0, scale=1.0):
+    def act(o, i, f=None, bias=0.0, scale=1.0):
+        if f is None:
+            lin(o, i, scale, bias)
+        else:
+            act1(o, i, f, bias, scale)
+
+    def act1(o, i, f, bias, scale):
         cols = [s for s in (bias, scale) if isinstance(s, tuple)]
         bb = bias[0] if isinstance(bias, tuple) else bias
         ss = scale[0] if isinstance(scale, tuple) else scale
@@ -117,141 +132,177 @@ def build(g, T, topo, core):
             fn = lambda: g.iota(o[0], pat, base, cm, allow_small_or_imprecise_dtypes=True)
         add("g", fn, [], [o], 130 + 2 * CY * o[2])
 
-    def load(q, name, o):
+    def load(q, name, o, sem=None):
         e = g.sync if q == "s" else g.scalar
         bts = o[2] * (2 if SCRATCH[o[3]][2] == B else 4)
-        add(q, lambda: e.dma_start(o[0], T[name][:]), [], [o], 60, ("dma", "l" + name, 2000 + 0.25 * bts))
+        moved[0] += bts
+        src = T[name][:, o[1][0][1]:o[1][0][2]] if name == "h0" else T[name][:]
+        add(q, lambda: e.dma_start(o[0], src), [], [o], 60, ("dma", sem or "l" + name, 2000 + 0.21 * moved[0]))
 
     def store(sem, dst, i):
         add("s", lambda: g.sync.dma_start(dst, i[0]), [i], [], 60, ("dma", sem, 2000 + i[2]))
 
     def copy(sem, o, i):
-        add("s", lambda: g.sync.dma_start(o[0], i[0]), [i], [o], 60, ("dma", sem, 3000))
+        moved[0] += 2 * o[2]
+        add("s", lambda: g.sync.dma_start(o[0], i[0]), [i], [o], 60, ("dma", sem, 1000 + 0.21 * moved[0]))
 
-    def conv(e, o, i, bias=0.0):
-        if e == "g":
-            add("g", lambda: g.affine_select(o[0], i[0], [[0, o[2]]], OP.is_ge, 0.0, 0, 0), [i], [o], 170 + 2 * CY * o[2])
-        elif e == "a":
-            act(o, i, bias=bias)
-        else:
-            ts(o, i, bias, OP.add)
+    def sel(o, i, pat, op, base, cm):
+        add("g", lambda: g.affine_select(o[0], i[0], pat, op, 0.0, base, cm), [i], [o], 170 + 2 * CY * o[2])
 
-    def send(sem, items):
+    def step(o, i, at, first=False):
+        add("a", lambda: g.scalar.activation(o[0], i[0], AF.Sigmoid, bias=-256.0 * at, scale=256.0), [i] + ([] if first else [A("reset")]), [o],
+            15 + cost(o, i) + (1300 if first else 0))
+
+    def lin(o, i, scale=1.0, bias=0.0, on="av"):
+        calls = {"a": lambda: act1(o, i, AF.Identity, bias, scale), "v": lambda: ts(o, i, scale, OP.mult, bias, OP.add),
+                 "g": lambda: sel(o, i, [[0, o[2]]], OP.is_ge, 0, 0)}
+        either(*[calls[e] for e in on])
+
+    def over(o, i, at, on="av"):
+        calls = {"a": lambda: step(o, i, at), "v": lambda: ts(o, i, at, OP.is_ge)}
+        either(*[calls[e] for e in on])
+
+    def send(sem, items, shares=None, own="sent", ns=500, floor=None):
         engs = [e for e in topo.engines(core, items[0][1][0][0]) if all(e in topo.engines(core, c) for s, ds in items for c, d in ds)]
-        per = len(engs) // len(items)
+        shares = shares or [1] * len(items)
+        per = [len(engs) * x // sum(shares) for x in shares]
         def fn():
             trs = []
             for k, (s, ds) in enumerate(items):
-                mask = sum(1 << e for e in engs[k * per:(k + 1) * per])
+                mask = sum(1 << e for e in engs[sum(per[:k]):sum(per[:k + 1])])
                 ids = [DstId(rid=topo.addr(c)[0], pnc=topo.addr(c)[1]) for c, d in ds]
-                trs.append(RemoteDMATransfer(dst_ids=ids, dma_engine_mask=mask, remote_sem=T.sem["r" + sem], srcs=[s[0]], dsts=[d[0] for c, d in ds]))
-            return g.remote_dma_fused(trs, local_sem=T.sem.sent)
+                trs.append(RemoteDMATransfer(dst_ids=ids, dma_engine_mask=mask, remote_sem=T.sem["r" + sem], srcs=[s[0]] + ([floor[0]] if floor else []),
+                                             dsts=[d[0] for c, d in ds], alu_op=2 if floor else 0))
+            return g.remote_dma_fused(trs, local_sem=T.sem[own])
         bts = sum(s[2] * (2 if SCRATCH[s[3]][2] == B else 4) for s, ds in items)
-        add("g", fn, [s for s, ds in items], [d for s, ds in items for c, d in ds], 500,
-            ("rem", "r" + sem, 2000 + 0.4 * bts, per * sum(len(ds) for s, ds in items), per * len(items)))
+        add("g", fn, [s for s, ds in items] + ([floor] if floor else []), [d for s, ds in items for c, d in ds], ns,
+            ("rem", "r" + sem, 2000 + 0.4 * bts, sum(x * len(ds) for x, (s, ds) in zip(per, items)), sum(per), own, bts))
 
     def tolist(o, z, src, lo, hi, more=()):
         mm(o, [(A(z, 15 - i, 143 - i), A(src, lo + i, hi, 16)) for i in range(16)] + list(more))
 
-    load("s", "sd", A("lst", 0, 120)); load("a", "na", A("lst", 120, 240)); load("s", "nb", A("lst", 240, 360))
-    load("a", "u0", A("ui")); load("s", "ta", A("a")); load("a", "th", A("thi")); load("s", "pf", A("pfi"))
-    load("a", "v0", A("vi")); load("s", "tb", A("b")); load("s", "h0", A("h"))
-    for k in range(10):
+    load("s", "sd", A("lst", 0, 120)); load("a", "h0", A("h", 0, GH), "lh1"); load("a", "u0", A("ui", 0, NP)); load("s", "ta", A("a"))
+    load("a", "th", A("thi")); load("s", "nb", A("lst", 240, 360)); load("a", "na", A("lst", 120, 240)); load("s", "pf", A("pfi"))
+    fill(A("xn"), 0.0)
+    load("a", "v0", A("vi")); load("s", "tb", A("b"))
+    copy("zxb", A("xb"), A("xn"))
+    load("s", "h0", A("h", GH, V))
+    for k in range(len(ops)):
         ops[k]["lead"] = 1e6 - 1e4 * k
-    iota(A("pi"), [[0, 1]], 0, 1); iota(A("v64"), [[64, 8], [3, 16]]); iota(A("a16"), [[1, 8], [0, 16]])
-    iota(A("c128"), [[1, 128]]); iota(A("i16"), [[0, 8], [1, 16]])
-    pp, pmod, pgr, p64, pwt, ptm = (A("pc", k, k + 1) for k in range(6))
-    cp(pp, A("pi")); ts(A("pj", 0, 1), A("pi"), 15, OP.bitwise_and); ts(A("pj", 1, 2), A("pi"), 4, OP.arith_shift_right)
-    cp(A("pc", 1, 3), A("pj")); ts(p64, pgr, 64.0, OP.mult, pmod, OP.add)
+    fill(A("xa"), 0.0); fill(A("dead", 3 * BL, V), 0.0)
+    lead[0] = 2e5
+    iota(A("pi"), [[0, 1]], 0, 1); iota(A("i16"), [[0, 8], [1, 16]]); iota(A("v64"), [[64, 8], [3, 16]]); iota(A("c128"), [[1, 128]])
+    iota(A("wide"), [[1, 152]], -12, -1); iota(A("o1"), [[1, 8], [0, 16]])
+    send("h", [(A("h", 0, GH), [(prv, A("hl"))])], ns=PAR["hns"])
+    lead[0] = 0.0
+    iota(A("one"), [[0, 128]], 1)
+    step(A("reset"), A("i16"), 0.5, first=True)
+    pp, pmod, pgr, p64, pwt, ptm = (A("pc", k, k + 1) for k in (0, 1, 2, 8, 4, 5))
+    ts(A("pj", 0, 1), A("pi"), 15, OP.bitwise_and); ts(A("pj", 1, 2), A("pi"), 4, OP.arith_shift_right)
+    ts(A("pj", 2, 3), A("pi"), 2, OP.arith_shift_right, 3, OP.bitwise_and)
+    cp(A("pc", 1, 4), A("pj")); ts(p64, pgr, 64.0, OP.mult, pmod, OP.add)
+    ts(A("idw"), A("wide"), 0.0, OP.is_equal); act(A("idn"), A("idw", 12, 140)); ts(A("blk"), A("o1"), pgr, OP.is_equal)
     for t in range(2):
         for r in range(3):
             o = A("pm", 128 * (3 * t + r), 128 * (3 * t + r + 1))
             if t == 0:
                 ts(o, A("v64"), float(t - 16 * r), OP.add, p64, OP.is_equal)
             else:
-                act(A("pc", 6, 7), p64, bias=float(t - 16 * r), scale=-1.0)
-                act(o, A("v64"), AF.Abs, bias=A("pc", 6, 7)); act(o, o, AF.Relu, bias=1.0, scale=-1.0)
-    ts(A("blk"), A("a16"), pgr, OP.is_equal); ts(A("idn"), A("c128"), pp, OP.is_equal)
-    for name, src, f in (("blkf", "blk", -2.0 ** -24), ("blkn", "blk", -4096.0), ("idm", "idn", -1.0), ("id256", "idn", 1.0 / 256), ("idf", "idn", 1.0),
-                         ("idmf", "idn", -1.0), ("id4k", "idn", -4096.0), ("idh", "idn", 0.5), ("idhf", "idn", 0.5), ("id512", "idn", 512.0)):
+                sel(o, A("blk"), [[-16, 8], [-3, 16]], OP.is_equal, 16 * r - t, 1)
+    for name, src, f in (("blkf", "blk", 1.0), ("blkn", "blk", -4096.0), ("idm", "idn", -1.0), ("id256", "idn", 1.0 / 256), ("idf", "idn", 1.0),
+                         ("idmf", "idn", -1.0), ("id4k", "idn", -4096.0), ("idh", "idn", 0.5), ("idhf", "idn", 0.5), ("id512", "idn", 512.0),
+                         ("id8m", "idn", -16 * KK)):
         act(A(name), A(src), scale=f)
-    add("g", lambda: g.affine_select(T.tri[:], T.blk[:], [[1, 128]], OP.is_gt, 0.0, 0, -1), [A("blk")], [A("tri")], 170 + 256)
+    sel(A("tri"), A("blk"), [[1, 128]], OP.is_gt, 0, -1)
     act(A("trik"), A("tri"), scale=KK)
     fill(A("z1"), 0.0); act(A("z1", 15, 128, 16), A("blk", 0, 128, 16))
     ts(pwt, pmod, 2.0, OP.is_lt, 2.0, OP.mult); ts(ptm, pmod, 4.0, OP.is_lt, -1.0, OP.mult); ts(pwt, pwt, ptm, OP.add)
     act(A("z2"), A("z1"), scale=pwt)
-    if PAR["zact"]:
-        for k in range(0, 2304, 128):
-            act(A("zall", k, k + 128), A("c128"), scale=0.0)
-    else:
-        fill(A("zall"), 0.0)
-    fill(A("half"), 0.5)
-    add("g", lambda: g.affine_select(T.zall[:, 15:2304:16], T.half[:, 0:144], [[-1, 16], [-16, 9]], OP.is_equal, 0.0, 0, 1),
-        [A("half")], [A("zall")], 170 + 288)
-    act(A("pidx"), A("c128"), bias=pmod, scale=16.0); act(A("pid2"), A("pidx"), bias=float(NP))
-    ts(A("diag"), A("i16"), pmod, OP.is_equal); act(A("reset"), A("i16"), AF.Sign)
+    ts(A("pc", 12, 16), A("c128", 0, 4), A("pc", 3, 4), OP.is_equal)
+    act(A("pc", 9, 10), pwt, AF.Relu, scale=-1.0); act(A("z3"), A("z1"), scale=A("pc", 9, 10))
+    for k in range(4):
+        sel(A("pick", 128 * k, 128 * k + 128), A("blk"), [[-16, 8], [-4, 16]], OP.is_equal, -k, 1)
+    for m in range(4):
+        act(A("four", 152 * m, 152 * m + 152), A("idw"), scale=A("pc", 12 + m, 13 + m))
+    act(A("pidx"), A("c128"), bias=pmod, scale=16.0)
+    act(pp, pmod, bias=KK / 4, scale=KK); act(A("ownc"), A("c128"), bias=pp, scale=1024.0)
+    ts(A("diag"), A("i16"), pmod, OP.is_equal)
     act(A("rampv"), A("c128"), bias=1024.0 * 256, scale=-1024.0)
-    ts(A("pc", 6, 7), pmod, 0.0, OP.is_equal); ts(A("pc", 7, 8), pmod, 1.0, OP.is_equal, float(NP), OP.mult)
+    act(A("pc", 6, 7), pmod, AF.Relu, bias=1.0, scale=-1.0); ts(A("pc", 7, 8), pmod, 1.0, OP.is_equal, float(NP), OP.mult)
     act(A("rampb"), A("c128"), bias=A("pc", 7, 8), scale=A("pc", 6, 7))
-    iota(A("one"), [[0, 128]], 1); iota(A("b480"), [[BL, 4], [0, 10]])
-    fill(A("xa"), 0.0)
-    for x in ("xb", "xn"):
-        if x in PAR["zdma"]:
-            copy("z" + x, A(x), A("xa"))
-        else:
-            fill(A(x), 0.0)
-    iota(A("negk"), [[0, CAP]], -int(KK)); fill(A("quart"), -0.25); iota(A("sc", 0, CAP), [[0, CAP]])
-    iota(A("s", 0, 133, 132), [[0, 2]])
+    iota(A("b480"), [[BL, 2], [BL, 4], [0, 10]]); iota(A("ten"), [[0, 4], [48, 10]])
+    iota(A("w0", W), [[0, 8]]); iota(A("w1", W), [[0, 8]])
+    iota(A("posk"), [[0, CAP // 2]], int(KK)); iota(A("zero"), [[0, CAP // 2]]); fill(A("quart"), -0.25); iota(A("sc", 0, CAP), [[0, CAP]], int(KK))
+    iota(A("mask", 128, 129), [[0, 1]]); act(A("mask", 0, 128), A("diag"), bias=-8192.0, scale=8192.0)
+    tt(A("dmask"), A("mask", 1, 129), A("mask", 0, 128), OP.subtract)
     for t in range(2):
-        act(A("fk", 40 * t, 40 * t + 40), A("pidx", 0, 40), bias=float(t), scale=3.0)
-    cp(A("lstf", 0, 120), A("lst", 0, 120)); cp(A("lstf", 120, 360), A("lst", 120, 360)); act(A("thf"), A("thi"), bias=0.5)
-    cp(A("face"), A("pfi")); ts(A("off"), A("face"), float(V), OP.min)
+        act(A("s", 132 * t, 132 * t + 1), A("mask", 0, 1))
+    iota(A("ui", NP), [[0, 16]], 128); iota(A("um", NP), [[0, 16]])
+    for t in range(2):
+        act(A("pc", 23, 24), pmod, bias=float(t), scale=3.0); act(A("fk", 80 * t, 80 * t + 40), A("ten"), bias=A("pc", 23, 24))
+        iota(A("fk", 80 * t + 40, 80 * t + 80), [[-BL, 4], [0, 10]], W - BL)
+    act(A("lstf", 0, 120), A("lst", 0, 120)); act(A("lstf", 120, 360), A("lst", 120, 360)); act(A("thf", 0, 2), A("thi"), bias=0.5)
+    act(A("thf", 2, 4), A("thi"), bias=128.0, scale=-1.0); act(A("thf", 4, 6), A("thi"), bias=128.0)
+    act(A("face"), A("pfi")); ts(A("off"), A("pfi"), float(V), OP.min)
     pmx = lambda t, r: A("pm", 128 * (3 * t + r), 128 * (3 * t + r + 1))
-    mm(P(2048, 40), [(pmx(0, r), A("lstf", r, 120, 3)) for r in range(3)])
-    cp(A("clu"), P(2048, 40))
+    mm(P(1024, 40), [(pmx(0, r), A("lstf", r, 120, 3)) for r in range(3)])
+    cp(A("clu"), P(1024, 40))
     for k in range(2):
         tt(A("dd", 120 * k, 120 * k + 120), A("lstf", 120 + 120 * k, 240 + 120 * k), A("pidx", 0, 120), OP.subtract)
     ts(A("dhi"), A("dd"), RND64, OP.add, RND64, OP.subtract); tt(A("dlo"), A("dd"), A("dhi"), OP.subtract)
     parts = [("dhi", 0), ("dlo", 0), ("dhi", 120), ("dlo", 120)]
+    for m in range(4):
+        mm(P(1536 + 120 * m, 120), [(A("four", 152 * m + 12 - 4 * (k - m), 152 * m + 140 - 4 * (k - m)), A(x, lo, lo + 120)) for k, (x, lo) in enumerate(parts)])
+    act(A("stack"), P(1536, 480))
     def steps(t, banks):
         for hf in range(2):
-            for i in range(16):
-                r = (t - i) % 3
-                o = P(banks[hf] + (16 * r + i - t) // 3, 305, 16)
-                mm(o, [(A("zall", 144 * i + 15 - k, 144 * i + 143 - k), A(x, lo + 60 * hf + r, lo + 60 * hf + 60, 3)) for k, (x, lo) in enumerate(parts)])
-    tbank = ((3072, 3584), (1024, 1536))
+            for m in range(4):
+                outs = []
+                for i in range(4 * m, 4 * m + 4):
+                    r, lo = (t - i) % 3, 120 * m + 60 * hf
+                    outs.append((P(banks[hf] + (16 * r + i - t) // 3, 305, 16), A("pick", 128 * (i % 4), 128 * (i % 4) + 128), A("stack", lo + r, lo + 60, 3)))
+                add("p", lambda outs=outs: [g.tensor.matmul(o[0], l[0], x[0], True, True) for o, l, x in outs][-1],
+                    [y for o, l, x in outs for y in (l, x)], [o for o, l, x in outs], 60 + 4 * 64 * PE)
+    tbank = ((2048, 2560), (2048, 2560))
     steps(0, tbank[0])
-    send("h", [(A("h", 0, GH), [(prv, A("hl"))])])
-    conv("g", A("w0", V, W), A("hl"))
+    lin(A("w0", V, W), A("hl"), on="gav")
 
     def collapse(t, usrc):
         for k in range(2):
             lo, hi, f0, f1 = 320 * k, 320 * k + 320, 960 * k + t, 960 * k + 960
             tt(A("cx", lo, hi), IX(A(usrc, 0, NP), A("clu", 20 * k, 20 * k + 20)), A("a", f0, f1, 3), OP.subtract)
-            act(A("cy", lo, hi), A("cx", lo, hi), AF.Abs, bias=-128.0)
-            act(A("ok", lo, hi), A("cy", lo, hi), AF.Sign, bias=A("thf", t, t + 1), scale=-1.0)
-            mm(P(2048 + 512 * k, 320), [(A("blk"), A("ok", lo, hi))])
-            ts(A("dead", lo, hi), P(2048 + 512 * k, 320), 1.0, OP.is_ge)
-            tt(A("xa", f0, f1, 3), A("dead", lo, hi), A("a", f0, f1, 3), OP.mult)
-            tt(A("xn", f0, f1, 3), P(tbank[t][k], 320), A("dead", lo, hi), OP.mult)
-        tt(A("xb", t, V, 3), A("dead"), A("b", t, V, 3), OP.mult)
+            if TEST_ON[t][k] == "a":
+                act(A("cy", lo, hi), A("cx", lo, hi), AF.Abs, bias=-128.0)
+                act(A("ok", lo, hi), A("cy", lo, hi), AF.Sign, bias=A("thf", t, t + 1), scale=-1.0)
+                mm(P(512 * k, 320), [(A("blk"), A("ok", lo, hi))])
+                at = 1.0
+            else:
+                ts(A("cy", lo, hi), A("cx", lo, hi), A("thf", 2 + t, 3 + t), OP.is_ge)
+                ts(A("ok", lo, hi), A("cx", lo, hi), A("thf", 4 + t, 5 + t), OP.is_le)
+                mm(P(512 * k, 320), [(A("blk"), A("cy", lo, hi)), (A("blk"), A("ok", lo, hi))])
+                at = 24.5
+            over(A("dead", f0, f1, 3), P(512 * k, 320), at, "av" if k else "va")
+            tt(A("xa", f0, f1, 3), A("dead", f0, f1, 3), A("a", f0, f1, 3), OP.mult)
+            tt(A("xn", f0, f1, 3), P(tbank[t][k], 320), A("dead", f0, f1, 3), OP.mult)
+        tt(A("xb", t, V, 3), A("dead", t, V, 3), A("b", t, V, 3), OP.mult)
 
     def factors(t):
         if t == 0:
-            mm(P(0, 80), [(pmx(0, r), A("lstf", 120 + r, 360, 3)) for r in range(3)])
-            mm(P(512, 120), [(pmx(1, r), A("lstf", r, 360, 3)) for r in range(3)])
-            act(A("cl", 40, 120), P(0, 80)); act(A("cl", 120, 240), P(512, 120))
-        tt(A("de"), A("cl", 120 * t + 80, 120 * t + 120), A("b480"), OP.subtract)
-        k = 40 * t
-        ts(A("n1u", k, k + 40), A("de"), -float(BL), OP.add)
-        tolist(P(0, 40), "z1", "ok", 0, 640)
-        ts(A("dl"), P(0, 40), 1.0, OP.is_ge)
-        tt(A("de"), A("cl", 120 * t + 40, 120 * t + 80), A("dl"), OP.mult)
-        tt(A("de"), A("de"), A("fk", k, k + 40), OP.max); tt(A("de"), A("de"), A("b480"), OP.subtract)
-        cp(A("n0u", k, k + 40), A("de"))
+            mm(P(2560, 40), [(pmx(1, r), A("lstf", r, 120, 3)) for r in range(3)])
+            for k in range(2):
+                mm(P(2600 + 80 * k, 80), [(pmx(k, r), A("lstf", 120 + r, 360, 3)) for r in range(3)]
+                   + [(A("idmf"), A("fk", 80 * k, 80 * k + 80)), (A("idmf"), A("b480"))])
+            act(A("cl"), P(2560, 200))
+        mm(P(2048, 40), [(A("z1", 15 - i, 143 - i), A("dead", t + 3 * i, V, 48)) for i in range(16)])
+        tolist(P(2112, 30), "z1", "dead", 3 * BL, V)
+        over(A("dl", 0, 40), P(2048, 40), 8.0); over(A("dl", 40, 80), P(2048, 40), 8.0)
+        act(A("dz", 30 * t, 30 * t + 30), P(2112, 30), scale=NP / 16.0)
+        tt(A("de"), A("cl", 40 + 80 * t, 120 + 80 * t), A("dl"), OP.mult)
+        tt(A("de"), A("de"), A("fk", 80 * t, 80 * t + 80), OP.add)
+        cp(A("nu", 80 * t, 80 * t + 80), A("de"))
         for lo, hi in ((0, 512), (512, 640)):
-            mm(P(lo, hi - lo), [(A("id256"), A("xa", t + 3 * lo, 3 * hi, 3)), (A("idm"), A("dead", lo, hi))])
-        act(A("c0", 640 * t, 640 * t + 640), P(0, 640), bias=1.0)
+            mm(P(2048 + lo, hi - lo), [(A("id256"), A("xa", t + 3 * lo, 3 * hi, 3)), (A("idm"), A("dead", t + 3 * lo, 3 * hi, 3))])
+        act(A("c0", 640 * t, 640 * t + 640), P(2048, 640), bias=1.0)
 
     def pair(name, pr, base=0):
         return A(name, base + 1024 * pr, base + 1024 * pr + 1024)
@@ -261,7 +312,8 @@ def build(g, T, topo, core):
         for pr in range(2):
             g0 = NP * pr
             lead[0] = PAR["lead"] if pr == 0 else 0.0
-            for tab, got, mul, own, out, q, bank, on in (("xa", "ga", vi, ui, uo, "q", 0, CONV_U), ("xb", "gb", uo, vi, vo, "q2", 1024, CONV_V)):
+            kinds = CMP_ON[k][2 * pr:2 * pr + 2]
+            for tab, got, mul, own, out, q, bank in (("xa", "ga", vi, ui, uo, "q", 0), ("xb", "gb", uo, vi, vo, "q2", 1024)):
                 for c in (2 * pr, 2 * pr + 1):
                     lo, hi = 512 * c, 512 * c + 512
                     x = P(bank + 512 * (c % 2), 512)
@@ -272,37 +324,35 @@ def build(g, T, topo, core):
                     mm(x, [(A("id512"), A(own, lo, hi)), (A("idn"), A(mul, lo, hi))])
                     tt(A(q, lo, hi), x, A(got, lo, hi), OP.mult)
                     ts(A(q, lo, hi), A(q, lo, hi), 1, OP.arith_shift_right, 255, OP.bitwise_and)
-                    conv(on[k][c], A(out, lo, hi), A(q, lo, hi), -128.0 if out == "vc" else 0.0)
-            ix = IX(A("xn"), A("off", 64 * pr, 64 * pr + 64))
-            if GN_ON[k][pr] == "a":
-                act(A("gn", g0 + 1024, g0 + NP), ix)
-            else:
-                cp(A("gn", g0 + 1024, g0 + NP), ix)
-            kinds = CMP_ON[k][2 * pr:2 * pr + 2]
+                    if tab == "xb" and kinds == "vv" and PAR["wide"]:
+                        if c % 2 == 0:
+                            continue
+                        lo -= 512
+                    if out == "vc":
+                        lin(A(out, lo, hi), A(q, lo, hi), bias=-128.0)
+                    else:
+                        lin(A(out, lo, hi), A(q, lo, hi), on="gav")
+            act(A("gn", g0 + 1024, g0 + NP), IX(A("xn"), A("off", 64 * pr, 64 * pr + 64)))
             for c in (2 * pr, 2 * pr + 1):
                 lo, hi = 512 * c, 512 * c + 512
-                x, ge = P(2048 + 512 * (c % 2), 512), A("gn", g0 + 512 * (c % 2), g0 + 512 * (c % 2) + 512)
+                x, ge = P(1024 + 512 * (c % 2), 512), A("gn", g0 + 512 * (c % 2), g0 + 512 * (c % 2) + 512)
                 if kinds[c % 2] == "a":
-                    y = P(1024 + 512 * (c % 2), 512) if last else x
-                    mm(y, [(A("idn"), A(uo, lo, hi)), (A("idm"), A(vo, lo, hi))])
-                    act(ge, y, AF.Sign, bias=-127.5 if last else 0.5)
-                if kinds[c % 2] == "v" or last:
-                    mm(x, [(A("idn"), A(uo, lo, hi))] + ([(A("id512"), A("quart"))] if last else []))
-                if kinds[c % 2] == "v":
-                    tt(ge, x, A(vo if last else "q2", lo, hi), OP.is_ge)
-                if last:
-                    tt(A("zz", lo, hi), x, A(vo, lo, hi), OP.mult)
+                    mm(x, [(A("idn"), A(uo, lo, hi)), (A("idm"), A(vo, lo, hi))])
+                    act(ge, x, AF.Sign, bias=-127.5 if last else 0.5)
+                else:
+                    mm(x, [(A("idn"), A(uo, lo, hi))])
+                    tt(ge, x, A("q2", lo, hi), OP.is_ge)
             bank = 3072 + 512 * pr
             f, s = A("face", 64 * pr, 64 * pr + 64), A("sg", 64 * pr, 64 * pr + 64)
             tolist(P(bank + 128, 64), "z2", "gn", g0 + 1024, g0 + NP)
-            tolist(P(bank + 64, 64), "z1", "gn", g0 + 1024, g0 + NP, [(A("idf"), f)])
+            tolist(P(bank + 64, 64), "z3", "gn", g0 + 1024, g0 + NP, [(A("idf"), f)])
             tolist(P(bank + 192, 64), "z1", "gn", g0, g0 + 1024)
             if kinds[0] == kinds[1]:
-                act(s, P(bank + 192, 64), AF.Sign, bias=-8.5 if kinds[0] == "v" else -1.0)
+                over(A("sb", 64 * pr, 64 * pr + 64), P(bank + 192, 64), 8.5 if kinds[0] == "v" else 1.0)
             else:
                 for j in range(2):
-                    act(A("sg", 64 * pr + 32 * j, 64 * pr + 32 * j + 32), P(bank + 192 + 32 * j, 32), AF.Sign, bias=-8.5 if kinds[j] == "v" else -1.0)
-            tt(s, P(bank + 128, 64), s, OP.mult)
+                    over(A("sb", 64 * pr + 32 * j, 64 * pr + 32 * j + 32), P(bank + 192 + 32 * j, 32), 8.5 if kinds[j] == "v" else 1.0)
+            tt(s, P(bank + 128, 64), A("sb", 64 * pr, 64 * pr + 64), OP.mult)
             tt(f, P(bank + 64, 64), s, OP.add)
             if after is None:
                 ts(A("off", 64 * pr, 64 * pr + 64), f, float(V), OP.min)
@@ -311,95 +361,98 @@ def build(g, T, topo, core):
 
     def move(t):
         s0 = 132 * t
-        sc, rs, rl = "sc", A("rs", CAP * t, CAP * t + CAP), A("rl", CAP * t, CAP * t + CAP)
-        mm(P(2304, 128), [(A("idn"), A("diag"))])
-        ts(A("on"), A("face"), float(V), OP.is_ge)
-        mm(P(2048, 128), [(A("blk"), A("on"))])
-        mm(P(2176, 128), [(A("blkn"), A("on")), (A("blk"), A("rampb"))])
-        act(A("gj"), A("face"), AF.Relu, bias=1.0 - V)
+        mm(P(256, 128), [(A("idn"), A("dmask"))])
+        over(A("on"), A("face"), V - 0.5, "va")
+        mm(P(0, 128), [(A("idn"), A("dmask")), (A("blk"), A("on"))])
+        mm(P(128, 128), [(A("idn"), A("mask", 0, 128)), (A("blk"), A("rampb")), (A("blkn"), A("on"))])
+        act(A("gj"), A("face"), AF.Relu, bias=-float(V))
         tt(A("v2"), A("on"), A("rampv"), OP.mult)
-        mm(P(2560, 128), [(A("trik"), A("on")), (A("idn"), A("v2")), (A("idmf"), A("gj"))])
-        act(A("val"), P(2560, 128))
-        mm(P(3072, 128), [(A("tri"), A("on")), (A("id4k"), A("on"))])
-        scan(A("s", s0 + 1, s0 + 129), A("one"), P(2048, 128), OP.mult, OP.add)
+        mm(P(512, 128), [(A("trik"), A("on")), (A("idn"), A("v2")), (A("idmf"), A("gj"))])
+        act(A("val"), P(512, 128), bias=KK, scale=-1.0)
+        scan(A("s", s0 + 1, s0 + 129), A("one"), P(0, 128), OP.mult, OP.add, A("s", s0, s0 + 1))
+        posx = P(1024, 128)
+        mm(posx, [(A("tri"), A("on")), (A("id4k"), A("on")), (A("idm"), A("mask", 0, 128)), (A("idf"), A("s", s0, s0 + 128))])
         tot = A("s", s0 + 128, s0 + 129)
         send("c%d" % t, [(tot, [(T.cores[(rank + d) % n], A("land", 16 * t + 4 * d, 16 * t + 4 * d + 1)) for d in range(1, n)])])
-        tt(A("o1"), P(2176, 128), A("s", s0, s0 + 128), OP.max)
-        tt(A("o1"), P(2304, 128), A("o1"), OP.mult)
-        scan(A("o2"), A("reset"), A("o1"), OP.mult, OP.add)
+        tt(A("o1"), P(128, 128), A("s", s0, s0 + 128), OP.max)
+        scan(A("o2"), A("reset"), A("o1"), OP.mult, OP.max)
         cp(A("offc"), A("o2", 15, 128, 16))
-        win, oc, vl = A(sc), A("offc"), A("val")
-        add("v", lambda: g.vector.tensor_copy(win[0].indirect(oc[0]), vl[0]), [oc, vl], [win], 50 + SC * 128)
+        win, oc, vl = A("sc"), A("offc"), A("val")
+        add("v", lambda: g.vector.tensor_copy(win[0].indirect(oc[0]), vl[0]), [oc, vl], [win], 50 + SC * 128, se=128)
         hc = CAP // 2
         for k in range(2):
-            lo, hi = hc * k, hc * k + hc
-            scan(A("dk", lo, hi), A("negk", lo, hi), A(sc, lo, hi), OP.add, OP.max, A("dk", lo - 1, lo) if k else None)
-            act(A("rs", CAP * t + lo, CAP * t + hi), A("dk", lo, hi), AF.Relu, bias=KK, scale=-1.0)
+            lo, hi = CAP * t + hc * k, CAP * t + hc * k + hc
+            scan(A("rs", lo, hi), A("posk"), A("sc", hc * k, hc * k + hc), OP.add, OP.min, A("rs", lo - 1, lo) if k else None)
             if PAR["two"]:
-                send("rs"[k] + str(t), [(A("rs", CAP * t + lo, CAP * t + hi), [(nxt, A("rl", CAP * t + lo, CAP * t + hi))])])
+                send("rs"[k] + str(t), [(A("rs", lo, hi), [(nxt, A("rl", lo, hi))])], floor=A("zero"))
         if not PAR["two"]:
-            send("r%d" % t, [(rs, [(nxt, rl)])])
+            send("r%d" % t, [(A("rs", x, x + hc), [(nxt, A("rl", x, x + hc))]) for x in (CAP * t, CAP * t + hc)], floor=A("zero"))
         if t == 0:
-            iota(A(sc, 0, CAP), [[0, CAP]])
-        act(A("ab"), A("dk"), AF.Abs, bias=-KK / 2)
+            iota(A("sc", 0, CAP), [[0, CAP]], int(KK))
+        act(A("ab"), A("rs", CAP * t, CAP * t + CAP), AF.Abs, bias=-KK / 2)
         act(A("ne"), A("ab"), AF.Sign, bias=0.5 - KK / 2)
-        tt(A("o3"), P(2304, 128), A("s", s0 + 1, s0 + 129), OP.mult)
-        scan(A("o4"), A("reset"), A("o3"), OP.mult, OP.add)
+        act(A("ab"), A("ab"), bias=BIG * (0.5 - KK / 2), scale=BIG)
+        tt(A("o3"), A("s", s0 + 1, s0 + 129), P(256, 128), OP.subtract)
+        scan(A("o4"), A("reset"), A("o3"), OP.mult, OP.max)
         ts(A("endc"), A("o4", 15, 128, 16), -1.0, OP.add, CAP - 1.0, OP.min)
-        tt(A("posx"), P(3072, 128), A("s", s0, s0 + 128), OP.add)
-        m, m4, lr = A("m", t, t + 1), A("m", 4, 5), A("land", 16 * t + 4, 16 * t + 16, 4)
+        m, lr = A("m", t, t + 1), A("land", 16 * t + 4, 16 * t + 16, 4)
         add("v", lambda: g.vector.tensor_reduce(m[0], lr[0], AX.X, OP.min), [lr], [m], 114)
-        ts(m, m, tot, OP.min, float(CAP), OP.min); ts(m4, m, -4096.0, OP.add)
-        hb, nlv = P(3200, 128), P(3328, 128)
-        ts(hb, A("posx"), m4, OP.is_lt, 8192.0, OP.mult); tt(hb, hb, A("pid2"), OP.add)
-        ts(nlv, A("posx"), m4, OP.is_ge, 4096.0, OP.mult)
+        ts(m, m, tot, OP.min, float(CAP), OP.min)
+        up, down, goes, stays = A("m", 4, 5), A("m", 5, 6), P(1152, 128), P(1280, 128)
+        act(up, m, bias=-4096.5 * BIG, scale=BIG); act(down, m, bias=4096.5 * BIG, scale=-BIG)
+        act(goes, posx, bias=up, scale=-BIG); act(stays, posx, bias=down, scale=BIG)
+        tt(A("hb"), goes, A("ownc"), OP.max); tt(stays, stays, A("face"), OP.min)
         sh = m
         if t == 1:
             sh = A("m", 2, 3)
-            ts(sh, m, A("m", 0, 1), OP.add)
+            act(sh, m, bias=A("m", 0, 1))
         else:
-            ts(A("cli"), A("cl", 120, 160), sh, OP.add); ts(A("clj"), A("cli"), NP - 1, OP.bitwise_and); cp(A("clu"), A("clj"))
+            cp(A("cli"), A("cl", 0, 40), sh); ts(A("clj"), A("cli"), NP - 1, OP.bitwise_and); cp(A("clu"), A("clj"))
         for k in range(2):
             lo, hi = hc * k, hc * k + hc
-            o = P(2560 + 1024 * k, hc)
-            mm(o, [(A("blkf"), A("rl", CAP * t + lo, CAP * t + hi))])
-            tt(A("vv", lo, hi), o, A("ne", lo, hi), OP.mult)
-            scan(A("hs", lo, hi), A("ne", lo, hi), A("vv", lo, hi), OP.min, OP.max, A("hs", lo - 1, lo) if k else None)
-        ts(A("y"), IX(A("hs"), A("endc")), 2.0 ** 24, OP.mult, -1.0, OP.add)
-        ts(A("y1"), A("y"), 6, OP.logical_shift_right, 0x1FF0, OP.bitwise_and); ts(A("y2"), A("y"), 19, OP.logical_shift_right)
-        tt(A("o1"), A("y1"), A("y2"), OP.add); tt(A("o1"), hb, A("o1"), OP.min); ts(A("idx"), A("o1"), -float(NP), OP.add)
-        ts(A("y3"), A("y"), GH - 1, OP.bitwise_and); tt(nlv, nlv, A("y3"), OP.max); tt(A("face"), nlv, A("face"), OP.min)
+            o = P(512 + 1024 * k, hc)
+            mm(o, [(A("id8m"), A("ne", lo, hi))], stop=False)
+            mm(o, [(A("blkf"), A("rl", CAP * t + lo, CAP * t + hi))], start=False)
+            scan(A("hs", lo, hi), A("ab", lo, hi), o, OP.min, OP.max, A("hs", lo - 1, lo) if k else None, BIG / 4)
+        tt(A("y"), IX(A("hs"), A("endc")), A("hb"), OP.min)
+        ts(A("y1"), A("y"), 6, OP.logical_shift_right, 0x1FF0, OP.bitwise_and); ts(A("y2"), A("y"), 19, OP.logical_shift_right, 15, OP.bitwise_and)
+        tt(A("o1"), A("y1"), A("y2"), OP.add); cp(A("idx"), A("o1"), -float(NP))
+        ts(A("y3"), A("y"), GH - 1, OP.bitwise_and); tt(A("face"), stays, A("y3"), OP.max)
         return sh
 
-    def xlist(sh):
-        ts(A("xi"), A("lstf", 0, 120), sh, OP.add); ts(A("xj"), A("xi"), NP - 1, OP.bitwise_and); cp(A("xu"), A("xj"))
+    def xlist(sh, t):
+        cp(A("xi"), A("lstf", 0, 120), sh); ts(A("xj"), A("xi"), NP - 1, OP.bitwise_and)
+        tt(A("xj", 90, 120), A("xj", 90, 120), A("dz", 30 * t, 30 * t + 30), OP.max); cp(A("xu", 120 * t, 120 * t + 120), A("xj"))
 
     def correct(w, usrc, nc):
         for b in range(3, -1, -1):
             lo, hi = BL * b, BL * b + BL
-            ix = IX(A(usrc), A("xu", 30 * b, 30 * b + 30))
-            if nc == 2 and b == 3:
-                act(A("oh"), A("w0", lo, hi), scale=0.5)
-                tt(A(w, lo, hi), ix, A("oh"), OP.add)
+            ix = IX(A(usrc), A("xu", 120 * nc - 120 + 30 * b, 120 * nc - 90 + 30 * b))
+            if nc == 2 and LIVE_ON[b] == "v":
+                if b < 3:
+                    act(A(w, lo, hi), A("w0", lo, hi), scale=0.5)
+                tt(A(w, lo, hi), ix, A(w, lo, hi), OP.add)
             else:
-                o = P(3072 + 512 * (b % 2), BL) if nc == 1 else P(1024 + 512 * b, BL)
+                o = P(2048 + 512 * (b % 2), BL)
                 act(A("xg", lo, hi), ix, bias=-1.0 if nc == 1 else 0.0, scale=1.0 / 128 if nc == 1 else 1.0)
-                if nc == 1:
-                    mm(o, [(A("idh"), A("h", lo, hi)), (A("idn"), A("xg", lo, hi))])
-                else:
-                    mm(o, [(A("idhf"), A("w0", lo, hi))], stop=False)
-                    mm(o, [(A("idn"), A("xg", lo, hi))], start=False)
+                old = ("idf", "w0") if b == 3 else ("idh", "h") if nc == 1 else ("idhf", "w0")
+                mm(o, [(A(old[0]), A(old[1], lo, hi))], stop=False)
+                mm(o, [(A("idn"), A("xg", lo, hi))], start=False)
                 act(A(w, lo, hi), o)
 
-    def follow(w, nc, done):
-        for b in range(3, -1, -1):
-            win, k, c, o = A(w, BL * b, W), 160 * nc, 320 * b, P(3584, 160 * nc)
-            bank = (3584, 2560)[b % 2] if nc == 2 else 512 * (b % 2)
+    def ahead(w, old, nc):
+        act(A(w, 3 * BL, V), A(old, 3 * BL, V), scale=0.5)
+        follow(w, nc, (3,), lambda b: None)
+
+    def follow(w, nc, blocks, done):
+        for b in blocks:
+            win, k = A(w, BL * b, W), 160 * nc
+            bank = (3072 if (nc == 1) == (b == 3) else 2048) + 512 * (b % 2)
             for t in range(nc):
-                j, c = 40 * t + 10 * b, 640 * t + 160 * b
-                mm(P(bank + 160 * t, 160), [(A("id256"), A("xb", BL * b + t, BL * b + BL, 3))])
-                act(A("p1", 160 * t, 160 * t + 160), IX(A(w, BL * b + BL, W), A("n1u", j, j + 10)))
-                tt(A("p0", 160 * t, 160 * t + 160), IX(win, A("n0u", j, j + 10)), A("c0", c, c + 160), OP.mult)
+                j, c = 80 * t + 10 * b, 640 * t + 160 * b
+                mm(P(bank + 160 * t, 160), [(A("id256"), A("b", BL * b + t, BL * b + BL, 3))])
+                lin(A("p1", 160 * t, 160 * t + 160), IX(A(w, BL * b + BL), A("nu", j + 40, j + 50)), on="a")
+                tt(A("p0", 160 * t, 160 * t + 160), IX(win, A("nu", j, j + 10)), A("c0", c, c + 160), OP.mult)
             tt(P(bank, k), P(bank, k), A("p1", 0, k), OP.mult)
             for t in range(nc):
                 tt(A(w, BL * b + t, BL * b + BL, 3), P(bank + 160 * t, 160), A("p0", 160 * t, 160 * t + 160), OP.add)
@@ -407,49 +460,65 @@ def build(g, T, topo, core):
 
     collapse(0, "ui")
     hop(0, "ui", "vi", "um", "vm", None)
-    hop(1, "um", "vm", "ua", "va",
-        lambda pr: send("uv0", [(pair(x, pr), [(nxt, pair(x, pr, NP))]) for x in ("ua", "va")]))
+    def give(sem, names, pr):
+        if sem[1] in PAR["halves"]:
+            send(sem, [(pair(x, pr), [(nxt, pair(x, pr, NP))]) for x in names])
+        elif pr:
+            send(sem, [(A(x, 0, NP), [(nxt, A(x, NP, 2 * NP))]) for x in names])
+
+    hop(1, "um", "vm", "ua", "va", lambda pr: give("uv0", ["ua", "va"], pr))
     factors(0)
+    ahead("w0", "h", 1)
     steps(1, tbank[1])
     sh = move(0)
     half = lambda k: A("idx", 64 * k, 64 * k + 64)
-    act(pair("u1", 0), IX(A("ua"), half(0))); cp(pair("u1", 1), IX(A("ua"), half(1)))
+    lin(pair("u1", 0), IX(A("ua"), half(0)), on="a"); lin(pair("u1", 1), IX(A("ua"), half(1)), on="v")
     for c in range(4):
-        o, ix = A("v1", 512 * c, 512 * c + 512), IX(A("va"), A("idx", 32 * c, 32 * c + 32))
-        if c in PAR["vdve"]:
-            cp(o, ix)
-        else:
-            act(o, ix)
+        act(A("v1", 512 * c, 512 * c + 512), IX(A("va"), A("idx", 32 * c, 32 * c + 32)))
     ts(A("off"), A("face"), float(V), OP.min)
-    xlist(sh)
+    xlist(sh, 0)
     collapse(1, "u1")
-    hop(2, "u1", "v1", "um", "vm", None)
-    correct("w0", "u1", 1)
-    hop(3, "um", "vm", "ub", "vc", lambda pr: send("u1", [(pair("ub", pr), [(nxt, pair("ub", pr, NP))])]))
-    follow("w0", 1, lambda b: None)
     factors(1)
-    send("g1", [(A("w0", 0, GH), [(prv, A("w1", V, W))])])
-    send("z1", [(A("zz", 0, NP), [(nxt, A("zz", NP, 2 * NP))])])
+    correct("w0", "u1", 1)
+    follow("w0", 1, (2, 1, 0), lambda b: None)
+    if not PAR["gz"]:
+        send("g1", [(A("w0", 0, GH), [(prv, A("w1", V, W))])])
+        ahead("w1", "w0", 2)
+    hop(2, "u1", "v1", "um", "vm", None)
+    hop(3, "um", "vm", "ub", "vc", lambda pr: give("u1", ["ub"], pr))
+    for c in range(4):
+        lo, hi, x = 512 * c, 512 * c + 512, P(PAR["zb"] + 512 * (c % 2), 512)
+        mm(x, [(A("idn"), A("ub", lo, hi)), (A("id512"), A("quart"))])
+        tt(A("zz", lo, hi), x, A("vc", lo, hi), OP.mult)
+    if PAR["gz"]:
+        hw = GH // 2
+        send("g1", [(A("w0", 0, hw), [(prv, A("w1", V, V + hw))]), (A("w0", hw, GH), [(prv, A("w1", V + hw, W))])]
+             + [(A("zz", x, x + hw), [(nxt, A("zz", NP + x, NP + x + hw))]) for x in range(0, NP, hw)], (4, 4, 2, 2, 2, 2))
+        ahead("w1", "w0", 2)
+    else:
+        send("z1", [(A("zz", 0, NP), [(nxt, A("zz", NP, 2 * NP))])])
     sh = move(1)
-    xlist(sh)
-    act(pair("u2", 0), IX(A("ub"), half(0)), bias=-1.0, scale=1.0 / 128)
-    ts(pair("u2", 1), IX(A("ub"), half(1)), 1.0 / 128, OP.mult, -1.0, OP.add)
+    xlist(sh, 1)
+    lin(pair("u2", 0), IX(A("ub"), half(0)), 1.0 / 128, -1.0, "a"); lin(pair("u2", 1), IX(A("ub"), half(1)), 1.0 / 128, -1.0, "v")
     cp(A("fu"), A("face"))
     act(pair("sig", 1), IX(A("zz"), half(1)), AF.Sigmoid, scale=2.0 ** -13)
-    act(P(0, 1024), pair("sig", 1))
+    for k in range(2):
+        mm(P(512 * k, 512), [(A("idf"), A("sig", GH + 512 * k, GH + 512 * k + 512))])
     act(pair("sig", 0), IX(A("zz"), half(0)), AF.Sigmoid, scale=2.0 ** -13)
     correct("w1", "u2", 2)
-    follow("w1", 2, lambda b: mm(P(3072, BL), [(A("idf"), A("w1", BL * b, BL * b + BL))], start=(b == 3), stop=(b == 0)))
+    total = lambda b: mm(P(1536, BL), [(A("idf"), A("w1", BL * b, BL * b + BL))], start=(b == 3), stop=(b == 0))
+    total(3)
+    follow("w1", 2, (2, 1, 0), total)
     for k in range(2):
         lo, hi = 512 * k, 512 * k + 512
-        act(A("pw", GH + lo, GH + hi), IX(A("w1"), A("fu", 64 + 32 * k, 96 + 32 * k)))
+        lin(A("pw", GH + lo, GH + hi), IX(A("w1"), A("fu", 64 + 32 * k, 96 + 32 * k)), on="a")
         tt(A("pw", lo, hi), IX(A("w1"), A("fu", 32 * k, 32 * k + 32)), A("sig", lo, hi), OP.mult)
     for k in range(2):
         lo, hi = 512 * k, 512 * k + 512
         tt(P(lo, 512), P(lo, 512), A("pw", GH + lo, GH + hi), OP.mult)
         tt(A("ow", lo, hi), P(lo, 512), A("pw", lo, hi), OP.add)
         store("o%d" % k, T.yw[:, lo:hi], A("ow", lo, hi))
-    act(A("oh"), P(3072, BL))
+    act(A("oh"), P(1536, BL))
     store("o2", T.yh[:], A("oh"))
     return ops
 
@@ -463,7 +532,7 @@ def depend(ops):
             if nm == "ps":
                 lo, hi = lo // 512 * 512, (hi + 511) // 512 * 512
             for j, l2, h2, w2 in seen.get(nm, []):
-                if l2 < hi and lo < h2 and (w or w2 or (nm == "ps" and ops[j]["q"] != o["q"])):
+                if l2 < hi and lo < h2 and (w or w2 or (nm == "ps" and (ops[j]["q"] != o["q"] or len(ops[j]["ways"]) + len(o["ways"]) > 2))):
                     dep.add(j)
         for (nm, lo, hi), w in acc:
             if nm == "ps":
@@ -562,37 +631,96 @@ def order(ops):
     seq = sorted(range(n), key=lambda i: (best[1][i], i))
     qs = ["vapgs".index(o["q"]) for o in ops]
     bset = [set(b) for b in before]
+    head = [i for i in range(n) if ops[i]["lead"] > 1e5]
+    seq = head + [i for i in seq if i not in head]
+    for i in head:
+        bset[i].update(j for j in head if j < i and qs[j] == qs[i])
 
-    def run(sq):
-        free, last, done, why = [0.0] * 5, [-1] * 5, [0.0] * n, [0] * n
-        for i in sq:
-            q = qs[i]
-            t, w = free[q], -2 - last[q]
-            for j in before[i]:
-                if done[j] > t:
-                    t, w = done[j], j
-            why[i] = w
-            free[q] = t = t + ns[i]
-            last[q] = i
-            done[i] = t + lag[i]
-        i = max(range(n), key=lambda x: done[x])
-        end, arcs = done[i] - lat, []
-        while i >= 0:
-            w = why[i]
-            if w <= -2:
-                w = -2 - w
-                if ops[w]["lead"] < 1e5:
-                    arcs.append((w, i))
-            i = w
-        return end, arcs, done
+    waits = [[j for j in before[i] if not qs[i] == qs[j] == 2] for i in range(n)]
+    ends = [i for i in range(n) if not users[i]]
+    marks = [i for i in range(n) if ops[i]["kind"] and ops[i]["kind"][1] in PAR["marks"]]
+    far = [o["kind"][6] if o["kind"] and o["kind"][0] == "rem" else 0 for o in ops]
+    cases = [([o["ns"] * (call if f else 1) + (ga - GA) * o["ge"] + (sc - SC) * o["se"] for o, f in zip(ops, far)],
+              [la + (start if f else o["kind"][2] if o["kind"] else 0) for o, f in zip(ops, far)], [rate * f for f in far])
+             for ga, sc, la, call, start, rate in CASES]
 
-    now, arcs, done = run(seq)
-    top = (now, seq)
+    def run(sq, a, old):
+        last0, k = [-1] * 5, a - 1
+        while k >= 0 and -1 in last0:
+            if last0[qs[sq[k]]] < 0:
+                last0[qs[sq[k]]] = sq[k]
+            k -= 1
+        total, arcs, new, rest = 0.0, [], [], sq[a:]
+        sent = [x for x in sq[:a] if far[x]]
+        for (tm, lg, fly), (was, why, left) in zip(cases, old):
+            done, why, left, last = list(was), list(why), list(left), list(last0)
+            free = [left[x] if x >= 0 else 0.0 for x in last]
+            line = done[sent[-1]] if sent else 0.0
+            for i in rest:
+                q = qs[i]
+                t, w = free[q], -2 - last[q]
+                for j in waits[i]:
+                    if done[j] > t:
+                        t, w = done[j], j
+                why[i] = w
+                left[i] = free[q] = t = t + tm[i]
+                last[q] = i
+                if fly[i]:
+                    done[i] = line = max(line, t + lg[i]) + fly[i]
+                else:
+                    done[i] = t + lg[i]
+            i = max(ends, key=lambda x: done[x])
+            total += done[i] + PAR["early"] * sum(done[x] for x in marks)
+            if done[i] > was[i] + PAR["drop"] > PAR["drop"]:
+                return 1e18, None, None
+            seen = set()
+            for i in [i] + marks:
+                while i >= 0 and i not in seen:
+                    seen.add(i)
+                    w = why[i]
+                    if w <= -2:
+                        w = -2 - w
+                        if ops[w]["lead"] < 1e5:
+                            arcs.append((w, i))
+                    i = w
+            new.append((done, why, left))
+        return total / len(cases), arcs, new
+
+    blank = [([0.0] * n, [0] * n, [0.0] * n) for c in cases]
+    way = [0] * n
+
+    def engine(i, k):
+        way[i], d = k, ops[i]["ways"][k][2] - ops[i]["ways"][way[i]][2]
+        qs[i] = "vapgs".index(ops[i]["ways"][k][0])
+        for c in cases:
+            c[0][i] += d
+
+    now, arcs, times = run(seq, 0, blank)
+    top = (now, seq, list(way))
     for turn in range(PAR["swaps"]):
+        if turn % PAR["sort"] == 0:
+            left, tm = times[turn // PAR["sort"] % len(cases)][2], cases[turn // PAR["sort"] % len(cases)][0]
+            place_of = {x: k for k, x in enumerate(seq)}
+            seq = sorted(seq, key=lambda x: (left[x] - tm[x], place_of[x]))
         r = (r * 1103515245 + 12345) % 2147483648
         j, i = arcs[(r >> 8) % len(arcs)]
         a, b = seq.index(j), seq.index(i)
         r = (r * 1103515245 + 12345) % 2147483648
+        if (r >> 16) % PAR["flip"] == 0:
+            x, a = (j, a) if (r >> 9) % 2 else (i, b)
+            if len(ops[x]["ways"]) < 2:
+                continue
+            was = way[x]
+            engine(x, (was + 1 + (r >> 10) % (len(ops[x]["ways"]) - 1)) % len(ops[x]["ways"]))
+            end, ar, tms = run(seq, a, times)
+            r = (r * 1103515245 + 12345) % 2147483648
+            if end <= now + PAR["heat"] * (1.0 - turn / PAR["swaps"]) * (r >> 8) / 8388608:
+                now, arcs, times = end, ar, tms
+                if end < top[0]:
+                    top = (end, seq, list(way))
+            else:
+                engine(x, was)
+            continue
         if (r >> 9) % 2:
             a = max(0, a - (r >> 12) % PAR["reach"] * ((r >> 10) % 2))
             need, up, rest = set(bset[i]), [i], []
@@ -617,15 +745,18 @@ def order(ops):
             if i in gone:
                 continue
             new = seq[:a] + rest + down + seq[b + 1:]
-        end, ar, dn = run(new)
+        end, ar, tms = run(new, a, times)
         r = (r * 1103515245 + 12345) % 2147483648
         if end <= now + PAR["heat"] * (1.0 - turn / PAR["swaps"]) * (r >> 8) / 8388608:
-            now, arcs, seq = end, ar, new
+            now, arcs, seq, times = end, ar, new, tms
             if end < top[0]:
-                top = (end, new)
-    done = run(top[1])[2]
+                top = (end, new, list(way))
     for i in range(n):
-        ops[i]["at"] = done[i] - lag[i] - ns[i]
+        engine(i, top[2][i])
+    times = run(top[1], 0, blank)[2]
+    for i in range(n):
+        ops[i]["at"] = times[0][2][i] - cases[0][0][i]
+    KEPT["ends"], KEPT["way"] = [int(max(x[0])) for x in times], top[2]
     return top[1]
 
 
@@ -637,13 +768,15 @@ def rank_program(g, core, T, topo):
     if "seq" not in KEPT:
         KEPT["seq"] = order(ops)
     seq = KEPT["seq"]
+    for o, k in zip(ops, KEPT["way"]):
+        o["q"], o["fn"], o["ns"] = o["ways"][k]
     queue = {"v": g.vector, "a": g.scalar, "p": g.tensor, "g": g, "s": g.sync}
     total, count, mark = {"sent": 0}, {q: 0 for q in "vapg"}, {}
     for o in ops:
         k = o["kind"]
         if k and k[0] == "rem":
             total[k[1]] = total.get(k[1], 0) + k[3]
-            total["sent"] += k[4]
+            total[k[5]] = total.get(k[5], 0) + k[4]
         elif k:
             total[k[1]] = 16
     waited = {q: {} for q in queue}
@@ -654,6 +787,9 @@ def rank_program(g, core, T, topo):
             s, v = mark[j]
             if not (s == "ep" and o["q"] == "p"):
                 need[s] = max(need.get(s, 0), v)
+            k = ops[j]["kind"]
+            if k and k[0] == "rem" and k[5] != "sent":
+                need[k[5]] = total[k[5]]
         for s, v in sorted(need.items()):
             if waited[o["q"]].get(s, 0) < v:
                 queue[o["q"]].wait_ge(T.sem[s], v)

from concourse.bass import DstId, RemoteDMATransfer
from concourse.mybir import AluOpType as OP, AxisListType as AX, ActivationFunctionType as AF

V, GH, BL, NP, CAP, W = 1920, 1024, 480, 2048, 512, 2944
KK = float(2 ** 19)
BIG = float(2 ** 26)
RND64 = 1.5 * 2.0 ** 29
CMP_ON = ["avvv", "avvv", "avvv", "vvvv"]
TEST_ON = ["aa", "av"]
LIVE_ON = list("aavv")

F, B, I, U = "float32", "bfloat16", "int32", "uint16"
COLS = {
    "ta": 0, "a": (V, B), "b": (V, B), "h": (V, B), "ui": (NP + 16, B), "vi": (NP, B), "lst": (360, I), "pfi": (128, I), "thi": (2, I),
    "lstf": (360, F), "thf": (6, F), "pi": (1, I), "pj": (3, I), "pc": (24, F), "c128": (128, F), "i16": (128, F), "id8m": (128, B), "v64": (128, F),
    "blkf": (128, F), "blk": (128, B), "blkn": (128, B), "idn": (128, B), "idm": (128, B), "id256": (128, B), "idf": (128, F), "idmf": (128, F),
    "trik": (128, B), "tri": (128, B), "id4k": (128, B), "z1": (144, B), "z2": (144, B), "pick": (512, B), "four": (608, B), "wide": (152, F), "idw": (152, B), "stack": (480, B), "z3": (144, B), "sb": (128, B), "idh": (128, B),
    "pm": (768, F), "diag": (128, B), "reset": (128, B), "pidx": (128, F), "ownc": (128, F), "rampv": (128, B), "rampb": (128, B), "one": (128, F),
    "posk": (CAP // 2, F), "zero": (CAP // 2, F), "mask": (130, B), "dmask": (128, B), "dd": (240, F), "dhi": (240, B), "dlo": (240, B), "tst": (V, B), "xa": (1936, B), "xb": (1936, B), "xn": (1936, B),
    "cl": (200, F), "fk": (160, F), "b480": (80, F), "ten": (40, F), "cli": (40, I), "clj": (40, I), "clu": (40, U), "cx": (640, F), "cy": (640, B), "ok": (640, B), "dead": (V, B),
    "dl": (80, B), "dz": (60, F), "de": (80, F), "nu": (160, U), "c0": (1280, B),
    "face": (128, F), "off": (128, U), "ga": (NP, F), "gb": (NP, F), "q": (NP, I), "q2": (NP, I), "gn": (2 * NP, B), "um": (NP + 16, B), "vm": (NP, B),
    "ua": (2 * NP, B), "va": (2 * NP, B), "ub": (2 * NP, B), "zz": (2 * NP, F), "id512": (128, B),
    "sg": (128, F), "on": (128, B), "s": (2 * 132, F), "land": (32, F), "o1": (128, F), "o2": (128, F), "o3": (128, F), "o4": (128, F),
    "offc": (8, U), "endc": (8, U), "val": (128, F), "v2": (128, B), "gj": (128, F), "sc": (NP + 128, F), "dk": (CAP, F), "rs": (2 * CAP, F), "rl": (2 * CAP, F),
    "ab": (CAP, F), "ne": (CAP, B), "quart": (512, B), "y": (128, I), "y1": (128, I), "y2": (128, I), "y3": (128, I),
    "hb": (128, F), "m": (8, F), "idx": (128, U), "xi": (120, I), "xj": (120, I), "xu": (240, U),
    "hl": (GH, B), "w0": (W + 8, F), "w1": (W + 8, F), "ow": (GH, F), "idhf": (128, F), "p0": (320, F), "p1": (320, F),
    "oh": (BL, F), "fu": (128, U),
}
SAME = {"sig": "sc", "u2": "um", "u1": "ui", "v1": "vi", "vc": "vi", "vv": "ab", "hs": "dk", "xg": "tst", "pw": "ga"}
del COLS["ta"]
SCRATCH = {k: ("sbuf", [128, n], d) for k, (n, d) in COLS.items()}
SCRATCH["ps"] = ("psum", [128, 4096], F)
LOADS = ["sd", "na", "nb", "pf", "th", "u0", "ta", "v0", "tb", "h0"]
REMOTE = ["h", "c0", "uv0", "r0", "g1", "c1", "u1", "r1", "z1", "s0", "s1"]
SEMAPHORES = ["ev", "ea", "ep", "eg", "sent"] + ["l" + k for k in LOADS] + ["r" + k for k in REMOTE] + ["o0", "o1", "o2", "zxb", "lh1"]
PAR = {"gb": 1024, "gn": 1024, "flip": 6, "drop": 500.0, "zb": 3072, "ints": "va", "early": 0.0, "marks": (), "sort": 200, "hns": 3000, "wide": True, "gz": False, "two": True, "halves": "v1", "swaps": 150000, "heat": 300.0, "reach": 30, "zact": False, "give": 100.0, "vdve": (2,), "span": 1500.0,
       "lead": 7000.0, "lat": 120.0, "seed": 2, "turns": 30, "shake": 800.0}
KEPT = {}
CY, PE, GA, SC = 1.0, 0.5, 1.56, 3.8
CASES = [(GA, SC, 120.0, 1.0, 2000.0, 0.4), (1.2, 2.5, 120.0, 2.0, 2600.0, 0.6), (1.95, 4.0, 110.0, 1.0, 1700.0, 0.3)]


def build(g, T, topo, core):
    rank = T.rank_of(core)
    n = len(T.cores)
    nxt, prv = T.cores[(rank + 1) % n], T.cores[(rank - 1) % n]
    ops, lead, moved = [], [0.0], [0]

    def A(name, lo=0, hi=None, st=1):
        name = SAME.get(name, name)
        if hi is None:
            hi = SCRATCH[name][1][1]
        ap = T[name][:, lo:hi] if st == 1 else T[name][:, lo:hi:st]
        return (ap, [(name, lo, hi)], len(range(lo, hi, st)), name)

    def P(lo, k, st=1):
        return A("ps", lo, lo + k, st)

    def IX(win, offs):
        return (win[0].indirect(offs[0]), win[1] + offs[1], 16 * offs[2], "*")

    def wide(*xs):
        return 0.5 if all(x[3] != "*" and SCRATCH[x[3]][2] in (B, U) for x in xs) else 1.0

    def add(q, fn, rd, wr, ns, kind=None, se=0):
        ops.append(dict(q=q, fn=fn, rd=[r for x in rd for r in x[1]], wr=[r for x in wr for r in x[1]], ns=ns, kind=kind, lead=lead[0],
                        ge=sum(x[2] for x in rd if x[3] == "*"), se=se, ways=[(q, fn, ns)]))

    def either(*calls):
        for call in calls:
            call()
        ways = [ops.pop() for call in calls[1:]][::-1]
        ops[-1]["ways"] += [o["ways"][0] for o in ways]
        ops[-1]["rd"] += [r for o in ways for r in o["rd"] if r not in ops[-1]["rd"]]

    def cost(o, i, f=1.0):
        if i[3] == "*":
            return 50 + GA * CY * i[2]
        return 50 + CY * max(64, f * o[2])

    def ts(o, i, s1, o1, s2=None, o2=None):
        cols = [s for s in (s1, s2) if isinstance(s, tuple)]
        a1 = s1[0] if isinstance(s1, tuple) else s1
        a2 = s2[0] if isinstance(s2, tuple) else s2
        if o2 is None:
            fn = lambda: g.vector.tensor_scalar(o[0], i[0], a1, None, o1)
        else:
            fn = lambda: g.vector.tensor_scalar(o[0], i[0], a1, a2, o1, o2)
        add("v", fn, [i] + cols, [o], cost(o, i, wide(o, i)))

    def tt(o, x, y, op):
        f = 1.0 if "ps" in (x[3], y[3]) else 2.0 * wide(o, x, y)
        add("v", lambda: g.vector.tensor_tensor(o[0], x[0], y[0], op), [x, y], [o], cost(o, x, f))

    def cp(o, i, bias=0.0):
        lin(o, i, 1.0, bias, PAR["ints"])

    def scan(o, d0, d1, o0, o1, init=None, first=0.0):
        add("v", lambda: g.vector.tensor_tensor_scan(o[0], d0[0], d1[0], init[0] if init else first, o0, o1),
            [d0, d1] + ([init] if init else []), [o], cost(o, d0))

    def fill(o, c):
        add("v", lambda: g.vector.memset(o[0], c), [], [o], 50 + CY * max(64, o[2] * wide(o)))

    def act(o, i, f=None, bias=0.0, scale=1.0):
        if f is None:
            lin(o, i, scale, bias)
        else:
            act1(o, i, f, bias, scale)

    def act1(o, i, f, bias, scale):
        cols = [s for s in (bias, scale) if isinstance(s, tuple)]
        bb = bias[0] if isinstance(bias, tuple) else bias
        ss = scale[0] if isinstance(scale, tuple) else scale
        add("a", lambda: g.scalar.activation(o[0], i[0], f, bias=bb, scale=ss), [i] + cols, [o], 15 + cost(o, i))

    def mm(o, pairs, start=True, stop=True):
        def fn():
            last = None
            for k, (l, r) in enumerate(pairs):
                last = g.tensor.matmul(o[0], l[0], r[0], start and k == 0, stop and k == len(pairs) - 1)
            return last
        ns = 60 + sum(PE * max(64, r[2]) * (4 if SCRATCH[r[3]][2] == F else 1) for l, r in pairs)
        add("p", fn, [x for pr in pairs for x in pr], [o], ns)

    def iota(o, pat, base=0, cm=0):
        if SCRATCH[o[3]][2] == I:
            fn = lambda: g.iota(o[0], pat, base, cm)
        else:
            fn = lambda: g.iota(o[0], pat, base, cm, allow_small_or_imprecise_dtypes=True)
        add("g", fn, [], [o], 130 + 2 * CY * o[2])

    def load(q, name, o, sem=None):
        e = g.sync if q == "s" else g.scalar
        bts = o[2] * (2 if SCRATCH[o[3]][2] == B else 4)
        moved[0] += bts
        src = T[name][:, o[1][0][1]:o[1][0][2]] if name == "h0" else T[name][:]
        add(q, lambda: e.dma_start(o[0], src), [], [o], 60, ("dma", sem or "l" + name, 2000 + 0.21 * moved[0]))

    def store(sem, dst, i):
        add("s", lambda: g.sync.dma_start(dst, i[0]), [i], [], 60, ("dma", sem, 2000 + i[2]))

    def copy(sem, o, i):
        moved[0] += 2 * o[2]
        add("s", lambda: g.sync.dma_start(o[0], i[0]), [i], [o], 60, ("dma", sem, 1000 + 0.21 * moved[0]))

    def sel(o, i, pat, op, base, cm):
        add("g", lambda: g.affine_select(o[0], i[0], pat, op, 0.0, base, cm), [i], [o], 170 + 2 * CY * o[2])

    def step(o, i, at, first=False):
        add("a", lambda: g.scalar.activation(o[0], i[0], AF.Sigmoid, bias=-256.0 * at, scale=256.0), [i] + ([] if first else [A("reset")]), [o],
            15 + cost(o, i) + (1300 if first else 0))

    def lin(o, i, scale=1.0, bias=0.0, on="av"):
        calls = {"a": lambda: act1(o, i, AF.Identity, bias, scale), "v": lambda: ts(o, i, scale, OP.mult, bias, OP.add),
                 "g": lambda: sel(o, i, [[0, o[2]]], OP.is_ge, 0, 0)}
        either(*[calls[e] for e in on])

    def over(o, i, at, on="av"):
        calls = {"a": lambda: step(o, i, at), "v": lambda: ts(o, i, at, OP.is_ge)}
        either(*[calls[e] for e in on])

    def send(sem, items, shares=None, own="sent", ns=500, floor=None):
        engs = [e for e in topo.engines(core, items[0][1][0][0]) if all(e in topo.engines(core, c) for s, ds in items for c, d in ds)]
        shares = shares or [1] * len(items)
        per = [len(engs) * x // sum(shares) for x in shares]
        def fn():
            trs = []
            for k, (s, ds) in enumerate(items):
                mask = sum(1 << e for e in engs[sum(per[:k]):sum(per[:k + 1])])
                ids = [DstId(rid=topo.addr(c)[0], pnc=topo.addr(c)[1]) for c, d in ds]
                trs.append(RemoteDMATransfer(dst_ids=ids, dma_engine_mask=mask, remote_sem=T.sem["r" + sem], srcs=[s[0]] + ([floor[0]] if floor else []),
                                             dsts=[d[0] for c, d in ds], alu_op=2 if floor else 0))
            return g.remote_dma_fused(trs, local_sem=T.sem[own])
        bts = sum(s[2] * (2 if SCRATCH[s[3]][2] == B else 4) for s, ds in items)
        add("g", fn, [s for s, ds in items] + ([floor] if floor else []), [d for s, ds in items for c, d in ds], ns,
            ("rem", "r" + sem, 2000 + 0.4 * bts, sum(x * len(ds) for x, (s, ds) in zip(per, items)), sum(per), own, bts))

    def tolist(o, z, src, lo, hi, more=()):
        mm(o, [(A(z, 15 - i, 143 - i), A(src, lo + i, hi, 16)) for i in range(16)] + list(more))

    load("s", "sd", A("lst", 0, 120)); load("a", "h0", A("h", 0, GH), "lh1"); load("a", "u0", A("ui", 0, NP)); load("s", "ta", A("a"))
    load("a", "th", A("thi")); load("s", "nb", A("lst", 240, 360)); load("a", "na", A("lst", 120, 240)); load("s", "pf", A("pfi"))
    fill(A("xn"), 0.0)
    load("a", "v0", A("vi")); load("s", "tb", A("b"))
    copy("zxb", A("xb"), A("xn"))
    load("s", "h0", A("h", GH, V))
    for k in range(len(ops)):
        ops[k]["lead"] = 1e6 - 1e4 * k
    fill(A("xa"), 0.0); fill(A("dead", 3 * BL, V), 0.0)
    lead[0] = 2e5
    iota(A("pi"), [[0, 1]], 0, 1); iota(A("i16"), [[0, 8], [1, 16]]); iota(A("v64"), [[64, 8], [3, 16]]); iota(A("c128"), [[1, 128]])
    iota(A("wide"), [[1, 152]], -12, -1); iota(A("o1"), [[1, 8], [0, 16]])
    send("h", [(A("h", 0, GH), [(prv, A("hl"))])], ns=PAR["hns"])
    lead[0] = 0.0
    iota(A("one"), [[0, 128]], 1)
    step(A("reset"), A("i16"), 0.5, first=True)
    pp, pmod, pgr, p64, pwt, ptm = (A("pc", k, k + 1) for k in (0, 1, 2, 8, 4, 5))
    ts(A("pj", 0, 1), A("pi"), 15, OP.bitwise_and); ts(A("pj", 1, 2), A("pi"), 4, OP.arith_shift_right)
    ts(A("pj", 2, 3), A("pi"), 2, OP.arith_shift_right, 3, OP.bitwise_and)
    cp(A("pc", 1, 4), A("pj")); ts(p64, pgr, 64.0, OP.mult, pmod, OP.add)
    ts(A("idw"), A("wide"), 0.0, OP.is_equal); act(A("idn"), A("idw", 12, 140)); ts(A("blk"), A("o1"), pgr, OP.is_equal)
    for t in range(2):
        for r in range(3):
            o = A("pm", 128 * (3 * t + r), 128 * (3 * t + r + 1))
            if t == 0:
                ts(o, A("v64"), float(t - 16 * r), OP.add, p64, OP.is_equal)
            else:
                sel(o, A("blk"), [[-16, 8], [-3, 16]], OP.is_equal, 16 * r - t, 1)
    for name, src, f in (("blkf", "blk", 1.0), ("blkn", "blk", -4096.0), ("idm", "idn", -1.0), ("id256", "idn", 1.0 / 256), ("idf", "idn", 1.0),
                         ("idmf", "idn", -1.0), ("id4k", "idn", -4096.0), ("idh", "idn", 0.5), ("idhf", "idn", 0.5), ("id512", "idn", 512.0),
                         ("id8m", "idn", -16 * KK)):
        act(A(name), A(src), scale=f)
    sel(A("tri"), A("blk"), [[1, 128]], OP.is_gt, 0, -1)
    act(A("trik"), A("tri"), scale=KK)
    fill(A("z1"), 0.0); act(A("z1", 15, 128, 16), A("blk", 0, 128, 16))
    ts(pwt, pmod, 2.0, OP.is_lt, 2.0, OP.mult); ts(ptm, pmod, 4.0, OP.is_lt, -1.0, OP.mult); ts(pwt, pwt, ptm, OP.add)
    act(A("z2"), A("z1"), scale=pwt)
    ts(A("pc", 12, 16), A("c128", 0, 4), A("pc", 3, 4), OP.is_equal)
    act(A("pc", 9, 10), pwt, AF.Relu, scale=-1.0); act(A("z3"), A("z1"), scale=A("pc", 9, 10))
    for k in range(4):
        sel(A("pick", 128 * k, 128 * k + 128), A("blk"), [[-16, 8], [-4, 16]], OP.is_equal, -k, 1)
    for m in range(4):
        act(A("four", 152 * m, 152 * m + 152), A("idw"), scale=A("pc", 12 + m, 13 + m))
    act(A("pidx"), A("c128"), bias=pmod, scale=16.0)
    act(pp, pmod, bias=KK / 4, scale=KK); act(A("ownc"), A("c128"), bias=pp, scale=1024.0)
    ts(A("diag"), A("i16"), pmod, OP.is_equal)
    act(A("rampv"), A("c128"), bias=1024.0 * 256, scale=-1024.0)
    act(A("pc", 6, 7), pmod, AF.Relu, bias=1.0, scale=-1.0); ts(A("pc", 7, 8), pmod, 1.0, OP.is_equal, float(NP), OP.mult)
    act(A("rampb"), A("c128"), bias=A("pc", 7, 8), scale=A("pc", 6, 7))
    iota(A("b480"), [[BL, 2], [BL, 4], [0, 10]]); iota(A("ten"), [[0, 4], [48, 10]])
    iota(A("w0", W), [[0, 8]]); iota(A("w1", W), [[0, 8]])
    iota(A("posk"), [[0, CAP // 2]], int(KK)); iota(A("zero"), [[0, CAP // 2]]); fill(A("quart"), -0.25); iota(A("sc", 0, CAP), [[0, CAP]], int(KK))
    iota(A("mask", 128, 129), [[0, 1]]); act(A("mask", 0, 128), A("diag"), bias=-8192.0, scale=8192.0)
    tt(A("dmask"), A("mask", 1, 129), A("mask", 0, 128), OP.subtract)
    for t in range(2):
        act(A("s", 132 * t, 132 * t + 1), A("mask", 0, 1))
    iota(A("ui", NP), [[0, 16]], 128); iota(A("um", NP), [[0, 16]])
    for t in range(2):
        act(A("pc", 23, 24), pmod, bias=float(t), scale=3.0); act(A("fk", 80 * t, 80 * t + 40), A("ten"), bias=A("pc", 23, 24))
        iota(A("fk", 80 * t + 40, 80 * t + 80), [[-BL, 4], [0, 10]], W - BL)
    act(A("lstf", 0, 120), A("lst", 0, 120)); act(A("lstf", 120, 360), A("lst", 120, 360)); act(A("thf", 0, 2), A("thi"), bias=0.5)
    act(A("thf", 2, 4), A("thi"), bias=128.0, scale=-1.0); act(A("thf", 4, 6), A("thi"), bias=128.0)
    act(A("face"), A("pfi")); ts(A("off"), A("pfi"), float(V), OP.min)
    pmx = lambda t, r: A("pm", 128 * (3 * t + r), 128 * (3 * t + r + 1))
    mm(P(1024, 40), [(pmx(0, r), A("lstf", r, 120, 3)) for r in range(3)])
    cp(A("clu"), P(1024, 40))
    for k in range(2):
        tt(A("dd", 120 * k, 120 * k + 120), A("lstf", 120 + 120 * k, 240 + 120 * k), A("pidx", 0, 120), OP.subtract)
    ts(A("dhi"), A("dd"), RND64, OP.add, RND64, OP.subtract); tt(A("dlo"), A("dd"), A("dhi"), OP.subtract)
    parts = [("dhi", 0), ("dlo", 0), ("dhi", 120), ("dlo", 120)]
    for m in range(4):
        mm(P(1536 + 120 * m, 120), [(A("four", 152 * m + 12 - 4 * (k - m), 152 * m + 140 - 4 * (k - m)), A(x, lo, lo + 120)) for k, (x, lo) in enumerate(parts)])
    act(A("stack"), P(1536, 480))
    def steps(t, banks):
        for hf in range(2):
            for m in range(4):
                outs = []
                for i in range(4 * m, 4 * m + 4):
                    r, lo = (t - i) % 3, 120 * m + 60 * hf
                    outs.append((P(banks[hf] + (16 * r + i - t) // 3, 305, 16), A("pick", 128 * (i % 4), 128 * (i % 4) + 128), A("stack", lo + r, lo + 60, 3)))
                add("p", lambda outs=outs: [g.tensor.matmul(o[0], l[0], x[0], True, True) for o, l, x in outs][-1],
                    [y for o, l, x in outs for y in (l, x)], [o for o, l, x in outs], 60 + 4 * 64 * PE)
    tbank = ((2048, 2560), (2048, 2560))
    steps(0, tbank[0])
    lin(A("w0", V, W), A("hl"), on="gav")

    def collapse(t, usrc):
        for k in range(2):
            lo, hi, f0, f1 = 320 * k, 320 * k + 320, 960 * k + t, 960 * k + 960
            tt(A("cx", lo, hi), IX(A(usrc, 0, NP), A("clu", 20 * k, 20 * k + 20)), A("a", f0, f1, 3), OP.subtract)
            if TEST_ON[t][k] == "a":
                act(A("cy", lo, hi), A("cx", lo, hi), AF.Abs, bias=-128.0)
                act(A("ok", lo, hi), A("cy", lo, hi), AF.Sign, bias=A("thf", t, t + 1), scale=-1.0)
                mm(P(512 * k, 320), [(A("blk"), A("ok", lo, hi))])
                at = 1.0
            else:
                ts(A("cy", lo, hi), A("cx", lo, hi), A("thf", 2 + t, 3 + t), OP.is_ge)
                ts(A("ok", lo, hi), A("cx", lo, hi), A("thf", 4 + t, 5 + t), OP.is_le)
                mm(P(512 * k, 320), [(A("blk"), A("cy", lo, hi)), (A("blk"), A("ok", lo, hi))])
                at = 24.5
            over(A("dead", f0, f1, 3), P(512 * k, 320), at, "av" if k else "va")
            tt(A("xa", f0, f1, 3), A("dead", f0, f1, 3), A("a", f0, f1, 3), OP.mult)
            tt(A("xn", f0, f1, 3), P(tbank[t][k], 320), A("dead", f0, f1, 3), OP.mult)
        tt(A("xb", t, V, 3), A("dead", t, V, 3), A("b", t, V, 3), OP.mult)

    def factors(t):
        if t == 0:
            mm(P(2560, 40), [(pmx(1, r), A("lstf", r, 120, 3)) for r in range(3)])
            for k in range(2):
                mm(P(2600 + 80 * k, 80), [(pmx(k, r), A("lstf", 120 + r, 360, 3)) for r in range(3)]
                   + [(A("idmf"), A("fk", 80 * k, 80 * k + 80)), (A("idmf"), A("b480"))])
            act(A("cl"), P(2560, 200))
        mm(P(2048, 40), [(A("z1", 15 - i, 143 - i), A("dead", t + 3 * i, V, 48)) for i in range(16)])
        tolist(P(2112, 30), "z1", "dead", 3 * BL, V)
        over(A("dl", 0, 40), P(2048, 40), 8.0); over(A("dl", 40, 80), P(2048, 40), 8.0)
        act(A("dz", 30 * t, 30 * t + 30), P(2112, 30), scale=NP / 16.0)
        tt(A("de"), A("cl", 40 + 80 * t, 120 + 80 * t), A("dl"), OP.mult)
        tt(A("de"), A("de"), A("fk", 80 * t, 80 * t + 80), OP.add)
        cp(A("nu", 80 * t, 80 * t + 80), A("de"))
        for lo, hi in ((0, 512), (512, 640)):
            mm(P(2048 + lo, hi - lo), [(A("id256"), A("xa", t + 3 * lo, 3 * hi, 3)), (A("idm"), A("dead", t + 3 * lo, 3 * hi, 3))])
        act(A("c0", 640 * t, 640 * t + 640), P(2048, 640), bias=1.0)

    def pair(name, pr, base=0):
        return A(name, base + 1024 * pr, base + 1024 * pr + 1024)

    def hop(k, ui, vi, uo, vo, after):
        last = vo == "vc"
        for pr in range(2):
            g0 = NP * pr
            lead[0] = PAR["lead"] if pr == 0 else 0.0
            kinds = CMP_ON[k][2 * pr:2 * pr + 2]
            for tab, got, mul, own, out, q, bank in (("xa", "ga", vi, ui, uo, "q", 0), ("xb", "gb", uo, vi, vo, "q2", 1024)):
                for c in (2 * pr, 2 * pr + 1):
                    lo, hi = 512 * c, 512 * c + 512
                    x = P(bank + 512 * (c % 2), 512)
                    if tab == "xa":
                        act(A(got, lo, hi), IX(A(tab), A("off", 32 * c, 32 * c + 32)), bias=1.0 / 256, scale=2.0)
                    elif c % 2 == 0:
                        act(pair(got, pr), IX(A(tab), A("off", 64 * pr, 64 * pr + 64)), bias=1.0 / 256, scale=2.0)
                    mm(x, [(A("id512"), A(own, lo, hi)), (A("idn"), A(mul, lo, hi))])
                    tt(A(q, lo, hi), x, A(got, lo, hi), OP.mult)
                    ts(A(q, lo, hi), A(q, lo, hi), 1, OP.arith_shift_right, 255, OP.bitwise_and)
                    if tab == "xb" and kinds == "vv" and PAR["wide"]:
                        if c % 2 == 0:
                            continue
                        lo -= 512
                    if out == "vc":
                        lin(A(out, lo, hi), A(q, lo, hi), bias=-128.0)
                    else:
                        lin(A(out, lo, hi), A(q, lo, hi), on="gav")
            act(A("gn", g0 + 1024, g0 + NP), IX(A("xn"), A("off", 64 * pr, 64 * pr + 64)))
            for c in (2 * pr, 2 * pr + 1):
                lo, hi = 512 * c, 512 * c + 512
                x, ge = P(1024 + 512 * (c % 2), 512), A("gn", g0 + 512 * (c % 2), g0 + 512 * (c % 2) + 512)
                if kinds[c % 2] == "a":
                    mm(x, [(A("idn"), A(uo, lo, hi)), (A("idm"), A(vo, lo, hi))])
                    act(ge, x, AF.Sign, bias=-127.5 if last else 0.5)
                else:
                    mm(x, [(A("idn"), A(uo, lo, hi))])
                    tt(ge, x, A("q2", lo, hi), OP.is_ge)
            bank = 3072 + 512 * pr
            f, s = A("face", 64 * pr, 64 * pr + 64), A("sg", 64 * pr, 64 * pr + 64)
            tolist(P(bank + 128, 64), "z2", "gn", g0 + 1024, g0 + NP)
            tolist(P(bank + 64, 64), "z3", "gn", g0 + 1024, g0 + NP, [(A("idf"), f)])
            tolist(P(bank + 192, 64), "z1", "gn", g0, g0 + 1024)
            if kinds[0] == kinds[1]:
                over(A("sb", 64 * pr, 64 * pr + 64), P(bank + 192, 64), 8.5 if kinds[0] == "v" else 1.0)
            else:
                for j in range(2):
                    over(A("sb", 64 * pr + 32 * j, 64 * pr + 32 * j + 32), P(bank + 192 + 32 * j, 32), 8.5 if kinds[j] == "v" else 1.0)
            tt(s, P(bank + 128, 64), A("sb", 64 * pr, 64 * pr + 64), OP.mult)
            tt(f, P(bank + 64, 64), s, OP.add)
            if after is None:
                ts(A("off", 64 * pr, 64 * pr + 64), f, float(V), OP.min)
            else:
                after(pr)

    def move(t):
        s0 = 132 * t
        mm(P(256, 128), [(A("idn"), A("dmask"))])
        over(A("on"), A("face"), V - 0.5, "va")
        mm(P(0, 128), [(A("idn"), A("dmask")), (A("blk"), A("on"))])
        mm(P(128, 128), [(A("idn"), A("mask", 0, 128)), (A("blk"), A("rampb")), (A("blkn"), A("on"))])
        act(A("gj"), A("face"), AF.Relu, bias=-float(V))
        tt(A("v2"), A("on"), A("rampv"), OP.mult)
        mm(P(512, 128), [(A("trik"), A("on")), (A("idn"), A("v2")), (A("idmf"), A("gj"))])
        act(A("val"), P(512, 128), bias=KK, scale=-1.0)
        scan(A("s", s0 + 1, s0 + 129), A("one"), P(0, 128), OP.mult, OP.add, A("s", s0, s0 + 1))
        posx = P(1024, 128)
        mm(posx, [(A("tri"), A("on")), (A("id4k"), A("on")), (A("idm"), A("mask", 0, 128)), (A("idf"), A("s", s0, s0 + 128))])
        tot = A("s", s0 + 128, s0 + 129)
        send("c%d" % t, [(tot, [(T.cores[(rank + d) % n], A("land", 16 * t + 4 * d, 16 * t + 4 * d + 1)) for d in range(1, n)])])
        tt(A("o1"), P(128, 128), A("s", s0, s0 + 128), OP.max)
        scan(A("o2"), A("reset"), A("o1"), OP.mult, OP.max)
        cp(A("offc"), A("o2", 15, 128, 16))
        win, oc, vl = A("sc"), A("offc"), A("val")
        add("v", lambda: g.vector.tensor_copy(win[0].indirect(oc[0]), vl[0]), [oc, vl], [win], 50 + SC * 128, se=128)
        hc = CAP // 2
        for k in range(2):
            lo, hi = CAP * t + hc * k, CAP * t + hc * k + hc
            scan(A("rs", lo, hi), A("posk"), A("sc", hc * k, hc * k + hc), OP.add, OP.min, A("rs", lo - 1, lo) if k else None)
            if PAR["two"]:
                send("rs"[k] + str(t), [(A("rs", lo, hi), [(nxt, A("rl", lo, hi))])], floor=A("zero"))
        if not PAR["two"]:
            send("r%d" % t, [(A("rs", x, x + hc), [(nxt, A("rl", x, x + hc))]) for x in (CAP * t, CAP * t + hc)], floor=A("zero"))
        if t == 0:
            iota(A("sc", 0, CAP), [[0, CAP]], int(KK))
        act(A("ab"), A("rs", CAP * t, CAP * t + CAP), AF.Abs, bias=-KK / 2)
        act(A("ne"), A("ab"), AF.Sign, bias=0.5 - KK / 2)
        act(A("ab"), A("ab"), bias=BIG * (0.5 - KK / 2), scale=BIG)
        tt(A("o3"), A("s", s0 + 1, s0 + 129), P(256, 128), OP.subtract)
        scan(A("o4"), A("reset"), A("o3"), OP.mult, OP.max)
        ts(A("endc"), A("o4", 15, 128, 16), -1.0, OP.add, CAP - 1.0, OP.min)
        m, lr = A("m", t, t + 1), A("land", 16 * t + 4, 16 * t + 16, 4)
        add("v", lambda: g.vector.tensor_reduce(m[0], lr[0], AX.X, OP.min), [lr], [m], 114)
        ts(m, m, tot, OP.min, float(CAP), OP.min)
        up, down, goes, stays = A("m", 4, 5), A("m", 5, 6), P(1152, 128), P(1280, 128)
        act(up, m, bias=-4096.5 * BIG, scale=BIG); act(down, m, bias=4096.5 * BIG, scale=-BIG)
        act(goes, posx, bias=up, scale=-BIG); act(stays, posx, bias=down, scale=BIG)
        tt(A("hb"), goes, A("ownc"), OP.max); tt(stays, stays, A("face"), OP.min)
        sh = m
        if t == 1:
            sh = A("m", 2, 3)
            act(sh, m, bias=A("m", 0, 1))
        else:
            cp(A("cli"), A("cl", 0, 40), sh); ts(A("clj"), A("cli"), NP - 1, OP.bitwise_and); cp(A("clu"), A("clj"))
        for k in range(2):
            lo, hi = hc * k, hc * k + hc
            o = P(512 + 1024 * k, hc)
            mm(o, [(A("id8m"), A("ne", lo, hi))], stop=False)
            mm(o, [(A("blkf"), A("rl", CAP * t + lo, CAP * t + hi))], start=False)
            scan(A("hs", lo, hi), A("ab", lo, hi), o, OP.min, OP.max, A("hs", lo - 1, lo) if k else None, BIG / 4)
        tt(A("y"), IX(A("hs"), A("endc")), A("hb"), OP.min)
        ts(A("y1"), A("y"), 6, OP.logical_shift_right, 0x1FF0, OP.bitwise_and); ts(A("y2"), A("y"), 19, OP.logical_shift_right, 15, OP.bitwise_and)
        tt(A("o1"), A("y1"), A("y2"), OP.add); cp(A("idx"), A("o1"), -float(NP))
        ts(A("y3"), A("y"), GH - 1, OP.bitwise_and); tt(A("face"), stays, A("y3"), OP.max)
        return sh

    def xlist(sh, t):
        cp(A("xi"), A("lstf", 0, 120), sh); ts(A("xj"), A("xi"), NP - 1, OP.bitwise_and)
        tt(A("xj", 90, 120), A("xj", 90, 120), A("dz", 30 * t, 30 * t + 30), OP.max); cp(A("xu", 120 * t, 120 * t + 120), A("xj"))

    def correct(w, usrc, nc):
        for b in range(3, -1, -1):
            lo, hi = BL * b, BL * b + BL
            ix = IX(A(usrc), A("xu", 120 * nc - 120 + 30 * b, 120 * nc - 90 + 30 * b))
            if nc == 2 and LIVE_ON[b] == "v":
                if b < 3:
                    act(A(w, lo, hi), A("w0", lo, hi), scale=0.5)
                tt(A(w, lo, hi), ix, A(w, lo, hi), OP.add)
            else:
                o = P(2048 + 512 * (b % 2), BL)
                act(A("xg", lo, hi), ix, bias=-1.0 if nc == 1 else 0.0, scale=1.0 / 128 if nc == 1 else 1.0)
                old = ("idf", "w0") if b == 3 else ("idh", "h") if nc == 1 else ("idhf", "w0")
                mm(o, [(A(old[0]), A(old[1], lo, hi))], stop=False)
                mm(o, [(A("idn"), A("xg", lo, hi))], start=False)
                act(A(w, lo, hi), o)

    def ahead(w, old, nc):
        act(A(w, 3 * BL, V), A(old, 3 * BL, V), scale=0.5)
        follow(w, nc, (3,), lambda b: None)

    def follow(w, nc, blocks, done):
        for b in blocks:
            win, k = A(w, BL * b, W), 160 * nc
            bank = (3072 if (nc == 1) == (b == 3) else 2048) + 512 * (b % 2)
            for t in range(nc):
                j, c = 80 * t + 10 * b, 640 * t + 160 * b
                mm(P(bank + 160 * t, 160), [(A("id256"), A("b", BL * b + t, BL * b + BL, 3))])
                lin(A("p1", 160 * t, 160 * t + 160), IX(A(w, BL * b + BL), A("nu", j + 40, j + 50)), on="a")
                tt(A("p0", 160 * t, 160 * t + 160), IX(win, A("nu", j, j + 10)), A("c0", c, c + 160), OP.mult)
            tt(P(bank, k), P(bank, k), A("p1", 0, k), OP.mult)
            for t in range(nc):
                tt(A(w, BL * b + t, BL * b + BL, 3), P(bank + 160 * t, 160), A("p0", 160 * t, 160 * t + 160), OP.add)
            done(b)

    collapse(0, "ui")
    hop(0, "ui", "vi", "um", "vm", None)
    def give(sem, names, pr):
        if sem[1] in PAR["halves"]:
            send(sem, [(pair(x, pr), [(nxt, pair(x, pr, NP))]) for x in names])
        elif pr:
            send(sem, [(A(x, 0, NP), [(nxt, A(x, NP, 2 * NP))]) for x in names])

    hop(1, "um", "vm", "ua", "va", lambda pr: give("uv0", ["ua", "va"], pr))
    factors(0)
    ahead("w0", "h", 1)
    steps(1, tbank[1])
    sh = move(0)
    half = lambda k: A("idx", 64 * k, 64 * k + 64)
    lin(pair("u1", 0), IX(A("ua"), half(0)), on="a"); lin(pair("u1", 1), IX(A("ua"), half(1)), on="v")
    for c in range(4):
        act(A("v1", 512 * c, 512 * c + 512), IX(A("va"), A("idx", 32 * c, 32 * c + 32)))
    ts(A("off"), A("face"), float(V), OP.min)
    xlist(sh, 0)
    collapse(1, "u1")
    factors(1)
    correct("w0", "u1", 1)
    follow("w0", 1, (2, 1, 0), lambda b: None)
    if not PAR["gz"]:
        send("g1", [(A("w0", 0, GH), [(prv, A("w1", V, W))])])
        ahead("w1", "w0", 2)
    hop(2, "u1", "v1", "um", "vm", None)
    hop(3, "um", "vm", "ub", "vc", lambda pr: give("u1", ["ub"], pr))
    for c in range(4):
        lo, hi, x = 512 * c, 512 * c + 512, P(PAR["zb"] + 512 * (c % 2), 512)
        mm(x, [(A("idn"), A("ub", lo, hi)), (A("id512"), A("quart"))])
        tt(A("zz", lo, hi), x, A("vc", lo, hi), OP.mult)
    if PAR["gz"]:
        hw = GH // 2
        send("g1", [(A("w0", 0, hw), [(prv, A("w1", V, V + hw))]), (A("w0", hw, GH), [(prv, A("w1", V + hw, W))])]
             + [(A("zz", x, x + hw), [(nxt, A("zz", NP + x, NP + x + hw))]) for x in range(0, NP, hw)], (4, 4, 2, 2, 2, 2))
        ahead("w1", "w0", 2)
    else:
        send("z1", [(A("zz", 0, NP), [(nxt, A("zz", NP, 2 * NP))])])
    sh = move(1)
    xlist(sh, 1)
    lin(pair("u2", 0), IX(A("ub"), half(0)), 1.0 / 128, -1.0, "a"); lin(pair("u2", 1), IX(A("ub"), half(1)), 1.0 / 128, -1.0, "v")
    cp(A("fu"), A("face"))
    act(pair("sig", 1), IX(A("zz"), half(1)), AF.Sigmoid, scale=2.0 ** -13)
    for k in range(2):
        mm(P(512 * k, 512), [(A("idf"), A("sig", GH + 512 * k, GH + 512 * k + 512))])
    act(pair("sig", 0), IX(A("zz"), half(0)), AF.Sigmoid, scale=2.0 ** -13)
    correct("w1", "u2", 2)
    total = lambda b: mm(P(1536, BL), [(A("idf"), A("w1", BL * b, BL * b + BL))], start=(b == 3), stop=(b == 0))
    total(3)
    follow("w1", 2, (2, 1, 0), total)
    for k in range(2):
        lo, hi = 512 * k, 512 * k + 512
        lin(A("pw", GH + lo, GH + hi), IX(A("w1"), A("fu", 64 + 32 * k, 96 + 32 * k)), on="a")
        tt(A("pw", lo, hi), IX(A("w1"), A("fu", 32 * k, 32 * k + 32)), A("sig", lo, hi), OP.mult)
    for k in range(2):
        lo, hi = 512 * k, 512 * k + 512
        tt(P(lo, 512), P(lo, 512), A("pw", GH + lo, GH + hi), OP.mult)
        tt(A("ow", lo, hi), P(lo, 512), A("pw", lo, hi), OP.add)
        store("o%d" % k, T.yw[:, lo:hi], A("ow", lo, hi))
    act(A("oh"), P(1536, BL))
    store("o2", T.yh[:], A("oh"))
    return ops


def depend(ops):
    seen = {}
    for i, o in enumerate(ops):
        acc = [(r, False) for r in o["rd"]] + [(r, True) for r in o["wr"]]
        dep = set()
        for (nm, lo, hi), w in acc:
            if nm == "ps":
                lo, hi = lo // 512 * 512, (hi + 511) // 512 * 512
            for j, l2, h2, w2 in seen.get(nm, []):
                if l2 < hi and lo < h2 and (w or w2 or (nm == "ps" and (ops[j]["q"] != o["q"] or len(ops[j]["ways"]) + len(o["ways"]) > 2))):
                    dep.add(j)
        for (nm, lo, hi), w in acc:
            if nm == "ps":
                lo, hi = lo // 512 * 512, (hi + 511) // 512 * 512
            seen.setdefault(nm, []).append((i, lo, hi, w))
        dep.discard(i)
        o["dep"] = dep
    last = {}
    for i, o in enumerate(ops):
        if o["kind"] and o["kind"][0] == "rem":
            last.setdefault(o["kind"][1], []).append(i)
    for o in ops:
        for j in list(o["dep"]):
            if ops[j]["kind"] and ops[j]["kind"][0] == "rem":
                o["dep"].update(last[ops[j]["kind"][1]])


def order(ops):
    n, lat = len(ops), PAR["lat"]
    ns = [o["ns"] for o in ops]
    lag = [lat + (o["kind"][2] if o["kind"] else 0) for o in ops]
    before = [sorted(o["dep"]) for o in ops]
    for i in range(n):
        far = set()
        for j in before[i]:
            far.update(ops[j]["dep"])
        before[i] = [j for j in before[i] if j not in far or ops[j]["kind"]]
    users = [[] for o in ops]
    for i in range(n):
        for j in before[i]:
            users[j].append(i)

    def place(key, back):
        pre, post = (users, before) if back else (before, users)
        left = [len(p) for p in pre]
        ready = sorted((key[i], i) for i in range(n) if left[i] == 0)
        busy = {q: [] for q in "vapgs"}
        at = [0.0] * n
        while ready:
            i = ready.pop(0)[1]
            if back:
                t = max([lag[i] - lat] + [at[j] + ns[j] + lag[i] for j in pre[i]])
            else:
                t = max([0.0] + [at[j] + ns[j] + lag[j] for j in pre[i]])
            b = busy[ops[i]["q"]]
            lo, hi = 0, len(b)
            while lo < hi:
                mid = (lo + hi) // 2
                if b[mid][1] <= t:
                    lo = mid + 1
                else:
                    hi = mid
            while lo < len(b) and b[lo][0] < t + ns[i]:
                t = max(t, b[lo][1])
                lo += 1
            b.insert(lo, (t, t + ns[i]))
            at[i] = t
            grew = False
            for u in post[i]:
                left[u] -= 1
                if left[u] == 0:
                    ready.append((key[u], u))
                    grew = True
            if grew:
                ready.sort()
        return at, max(at[i] + ns[i] + (0 if back else lag[i] - lat) for i in range(n))

    way = [0.0] * n
    for i in range(n - 1, -1, -1):
        way[i] = ns[i] + max([lag[i] + way[u] for u in users[i]] + [lag[i]])
    first = [-1e9 + i if ops[i]["lead"] > 1e5 else 0.0 for i in range(n)]
    best, base, r = None, [-w - o["lead"] for w, o in zip(way, ops)], PAR["seed"]
    now = 1e18
    for turn in range(PAR["turns"]):
        key = list(base)
        if turn:
            r = (r * 1103515245 + 12345) % 2147483648
            mid, amp = best[0] * (r >> 8) / 8388608, PAR["shake"] * (1 + r % 4)
            for i in range(n):
                if abs(base[i] - mid) < PAR["span"]:
                    r = (r * 1103515245 + 12345) % 2147483648
                    key[i] += amp * ((r >> 8) / 8388608 - 0.5)
        for rep in range(0 if turn % 8 else 1):
            at, end = place([k + f for k, f in zip(key, first)], False)
            if best is None or end < best[0]:
                best = (end, at)
            bt, _ = place([-(at[i] + ns[i]) for i in range(n)], True)
            key = [-(bt[i] + ns[i]) for i in range(n)]
        at, end = place([k + f for k, f in zip(key, first)], False)
        if end <= best[0]:
            best = (end, at)
        if end <= min(now, best[0] + 1e9 * (turn > 0)) + PAR["give"] * (1.0 - turn / PAR["turns"]):
            base, now = at, end
        if best[0] < now - PAR["give"] * 4:
            now, base = best
    seq = sorted(range(n), key=lambda i: (best[1][i], i))
    qs = ["vapgs".index(o["q"]) for o in ops]
    bset = [set(b) for b in before]
    head = [i for i in range(n) if ops[i]["lead"] > 1e5]
    seq = head + [i for i in seq if i not in head]
    for i in head:
        bset[i].update(j for j in head if j < i and qs[j] == qs[i])

    waits = [[j for j in before[i] if not qs[i] == qs[j] == 2] for i in range(n)]
    ends = [i for i in range(n) if not users[i]]
    marks = [i for i in range(n) if ops[i]["kind"] and ops[i]["kind"][1] in PAR["marks"]]
    far = [o["kind"][6] if o["kind"] and o["kind"][0] == "rem" else 0 for o in ops]
    cases = [([o["ns"] * (call if f else 1) + (ga - GA) * o["ge"] + (sc - SC) * o["se"] for o, f in zip(ops, far)],
              [la + (start if f else o["kind"][2] if o["kind"] else 0) for o, f in zip(ops, far)], [rate * f for f in far])
             for ga, sc, la, call, start, rate in CASES]

    def run(sq, a, old):
        last0, k = [-1] * 5, a - 1
        while k >= 0 and -1 in last0:
            if last0[qs[sq[k]]] < 0:
                last0[qs[sq[k]]] = sq[k]
            k -= 1
        total, arcs, new, rest = 0.0, [], [], sq[a:]
        sent = [x for x in sq[:a] if far[x]]
        for (tm, lg, fly), (was, why, left) in zip(cases, old):
            done, why, left, last = list(was), list(why), list(left), list(last0)
            free = [left[x] if x >= 0 else 0.0 for x in last]
            line = done[sent[-1]] if sent else 0.0
            for i in rest:
                q = qs[i]
                t, w = free[q], -2 - last[q]
                for j in waits[i]:
                    if done[j] > t:
                        t, w = done[j], j
                why[i] = w
                left[i] = free[q] = t = t + tm[i]
                last[q] = i
                if fly[i]:
                    done[i] = line = max(line, t + lg[i]) + fly[i]
                else:
                    done[i] = t + lg[i]
            i = max(ends, key=lambda x: done[x])
            total += done[i] + PAR["early"] * sum(done[x] for x in marks)
            if done[i] > was[i] + PAR["drop"] > PAR["drop"]:
                return 1e18, None, None
            seen = set()
            for i in [i] + marks:
                while i >= 0 and i not in seen:
                    seen.add(i)
                    w = why[i]
                    if w <= -2:
                        w = -2 - w
                        if ops[w]["lead"] < 1e5:
                            arcs.append((w, i))
                    i = w
            new.append((done, why, left))
        return total / len(cases), arcs, new

    blank = [([0.0] * n, [0] * n, [0.0] * n) for c in cases]
    way = [0] * n

    def engine(i, k):
        way[i], d = k, ops[i]["ways"][k][2] - ops[i]["ways"][way[i]][2]
        qs[i] = "vapgs".index(ops[i]["ways"][k][0])
        for c in cases:
            c[0][i] += d

    now, arcs, times = run(seq, 0, blank)
    top = (now, seq, list(way))
    for turn in range(PAR["swaps"]):
        if turn % PAR["sort"] == 0:
            left, tm = times[turn // PAR["sort"] % len(cases)][2], cases[turn // PAR["sort"] % len(cases)][0]
            place_of = {x: k for k, x in enumerate(seq)}
            seq = sorted(seq, key=lambda x: (left[x] - tm[x], place_of[x]))
        r = (r * 1103515245 + 12345) % 2147483648
        j, i = arcs[(r >> 8) % len(arcs)]
        a, b = seq.index(j), seq.index(i)
        r = (r * 1103515245 + 12345) % 2147483648
        if (r >> 16) % PAR["flip"] == 0:
            x, a = (j, a) if (r >> 9) % 2 else (i, b)
            if len(ops[x]["ways"]) < 2:
                continue
            was = way[x]
            engine(x, (was + 1 + (r >> 10) % (len(ops[x]["ways"]) - 1)) % len(ops[x]["ways"]))
            end, ar, tms = run(seq, a, times)
            r = (r * 1103515245 + 12345) % 2147483648
            if end <= now + PAR["heat"] * (1.0 - turn / PAR["swaps"]) * (r >> 8) / 8388608:
                now, arcs, times = end, ar, tms
                if end < top[0]:
                    top = (end, seq, list(way))
            else:
                engine(x, was)
            continue
        if (r >> 9) % 2:
            a = max(0, a - (r >> 12) % PAR["reach"] * ((r >> 10) % 2))
            need, up, rest = set(bset[i]), [i], []
            for x in reversed(seq[a:b]):
                if x in need:
                    up.append(x)
                    need.update(bset[x])
                else:
                    rest.append(x)
            if j in need:
                continue
            new = seq[:a] + up[::-1] + rest[::-1] + seq[b + 1:]
        else:
            b = min(n - 1, b + (r >> 12) % PAR["reach"] * ((r >> 10) % 2))
            gone, down, rest = {j}, [j], []
            for x in seq[a + 1:b + 1]:
                if bset[x] & gone:
                    gone.add(x)
                    down.append(x)
                else:
                    rest.append(x)
            if i in gone:
                continue
            new = seq[:a] + rest + down + seq[b + 1:]
        end, ar, tms = run(new, a, times)
        r = (r * 1103515245 + 12345) % 2147483648
        if end <= now + PAR["heat"] * (1.0 - turn / PAR["swaps"]) * (r >> 8) / 8388608:
            now, arcs, seq, times = end, ar, new, tms
            if end < top[0]:
                top = (end, new, list(way))
    for i in range(n):
        engine(i, top[2][i])
    times = run(top[1], 0, blank)[2]
    for i in range(n):
        ops[i]["at"] = times[0][2][i] - cases[0][0][i]
    KEPT["ends"], KEPT["way"] = [int(max(x[0])) for x in times], top[2]
    return top[1]


def rank_program(g, core, T, topo):
    if T.rank_of(core) is None:
        return
    ops = build(g, T, topo, core)
    depend(ops)
    if "seq" not in KEPT:
        KEPT["seq"] = order(ops)
    seq = KEPT["seq"]
    for o, k in zip(ops, KEPT["way"]):
        o["q"], o["fn"], o["ns"] = o["ways"][k]
    queue = {"v": g.vector, "a": g.scalar, "p": g.tensor, "g": g, "s": g.sync}
    total, count, mark = {"sent": 0}, {q: 0 for q in "vapg"}, {}
    for o in ops:
        k = o["kind"]
        if k and k[0] == "rem":
            total[k[1]] = total.get(k[1], 0) + k[3]
            total[k[5]] = total.get(k[5], 0) + k[4]
        elif k:
            total[k[1]] = 16
    waited = {q: {} for q in queue}
    for i in seq:
        o = ops[i]
        need = {}
        for j in o["dep"]:
            s, v = mark[j]
            if not (s == "ep" and o["q"] == "p"):
                need[s] = max(need.get(s, 0), v)
            k = ops[j]["kind"]
            if k and k[0] == "rem" and k[5] != "sent":
                need[k[5]] = total[k[5]]
        for s, v in sorted(need.items()):
            if waited[o["q"]].get(s, 0) < v:
                queue[o["q"]].wait_ge(T.sem[s], v)
                waited[o["q"]][s] = v
        ins = o["fn"]()
        k = o["kind"]
        if k is None:
            count[o["q"]] += 1
            ins.then_inc(T.sem["e" + o["q"]], 1)
            mark[i] = ("e" + o["q"], count[o["q"]])
        else:
            if k[0] == "dma":
                ins.then_inc(T.sem[k[1]], 16)
            mark[i] = (k[1], total[k[1]])
    for q in count:
        total["e" + q] = count[q]
    for s, v in sorted(total.items()):
        g.wait_ge(T.sem[s], v)
